import numpy as np
import ml_dtypes


def mxq(x, axis, fmt="e4m3"):
    dtype, down = {"e4m3": (ml_dtypes.float8_e4m3fn, 7), "e5m2": (ml_dtypes.float8_e5m2, 14)}[fmt]
    v = np.moveaxis(np.asarray(x, np.float32).astype(ml_dtypes.bfloat16).astype(np.float64), axis, -1)
    blocks = v.reshape(v.shape[:-1] + (-1, 32))
    amax = np.abs(blocks).max(-1, keepdims=True)
    byte = np.maximum(np.where(amax > 0, np.frexp(amax)[1] - 1 + 127, 0) - down, 1)
    scale = np.exp2(byte - 127.0)
    codes = (blocks / scale).astype(np.float32).astype(dtype).astype(np.float64)
    return np.moveaxis((codes * scale).reshape(v.shape), -1, axis)


WIDE = False


def mx_kscale(k):
    if not WIDE:
        return np.ones(k)
    levels = np.array([10, -10, 5, -5, 0])
    if k % 512:
        return np.exp2(np.random.permutation(np.resize(levels, k // 32))).repeat(32)
    a = np.empty((k // 512, 16))
    for p in range(k // 512):
        a[p, :8] = np.random.permutation(np.resize(levels, 8))
        for g in range(8):
            far = levels[np.abs(levels - a[p, g]) >= 10]
            a[p, g + 8] = far[np.random.randint(len(far))]
    return np.exp2(a.ravel()).repeat(32)


def f64(x):
    return np.asarray(x).astype(np.float64)


def striped(idx):
    return np.tile(np.asarray(idx).reshape(-1, 16).T, (8, 1)).astype(np.uint16)


def unstriped(offs):
    return offs[:16].T.reshape(-1).astype(np.int64)


E2M1 = np.array([0.0, 0.5, 1.0, 1.5, 2.0, 3.0, 4.0, 6.0, -0.0, -0.5, -1.0, -1.5, -2.0, -3.0, -4.0, -6.0])


def pack_weight(w, fmt):
    k, n = w.shape
    w = f64(np.asarray(w, np.float32).astype(ml_dtypes.bfloat16)).reshape(k // 32, 32, n)
    amax = np.abs(w).max(1)
    if fmt == "e4m3":
        byte = np.frexp(amax)[1] - 1 + 127 - 7
    else:
        mant, ex = np.frexp(amax / 6.0)
        byte = np.where(mant > 0.5, ex, ex - 1) + 127
    byte = np.clip(np.where(amax > 0, byte, 1), 1, 254)
    scaled = (w * np.exp2(127.0 - byte)[:, None, :]).reshape(k, n).astype(np.float32)
    by_word = np.ascontiguousarray(scaled.reshape(k // 512, 128, 4, n).transpose(0, 1, 3, 2))
    if fmt == "e4m3":
        words = by_word.astype(ml_dtypes.float8_e4m3fn).view(np.uint8)
    else:
        c = by_word.astype(ml_dtypes.float4_e2m1fn).view(np.uint8) & 0xF
        words = (c[..., 0::2] | (c[..., 1::2] << 4)).reshape(k // 512, 128, 2 * n)
    return np.ascontiguousarray(words), np.ascontiguousarray(byte.astype(np.uint8).reshape(k // 512, 16, n))


def unpack_weight(words, scales, fmt):
    g, _, n = scales.shape
    words = np.ascontiguousarray(words).reshape(g, 128, n, -1)
    if fmt == "e4m3":
        vals = words.view(ml_dtypes.float8_e4m3fn).astype(np.float64)
    else:
        nib = np.empty((g, 128, n, 4), np.uint8)
        nib[..., 0::2] = words & 0xF
        nib[..., 1::2] = words >> 4
        vals = E2M1[nib]
    vals = vals * np.repeat(np.exp2(scales.astype(np.float64) - 127.0), 8, axis=1)[..., None]
    return vals.transpose(0, 1, 3, 2).reshape(g * 512, n)


D, T, J, I, E = 512, 2048, 512, 512, 512


def setup_inputs():
    n = np.random.standard_normal
    idx = np.random.permutation(T)[:I]
    idx2 = np.random.permutation(T)[:J]
    fd = mx_kscale(D)
    fj = mx_kscale(J)
    tj = np.ones(T)
    tj[idx2] = fj
    ekeyp = pack_weight(n((D, T)) * 0.5 / np.sqrt(D) * fd[:, None], "e4m3")
    keysp = pack_weight(n((D, T)) / fd[:, None], "e2m1")
    return {
        "ekey_words": ekeyp[0],
        "ekey_scales": ekeyp[1],
        "keys_words": keysp[0],
        "keys_scales": keysp[1],
        "fac": (np.random.uniform(0.5, 2.0, (J, 1)) * fj[:, None]).astype(np.float32),
        "evals": (n((E, T)) * 4.0 / tj).astype(np.float32),
        "vals": (n((E, T)) * 0.3).astype(np.float32),
        "offs": striped(idx),
        "offs2": striped(idx2),
    }


def reference(ekey_words, ekey_scales, keys_words, keys_scales, fac, evals, vals, offs, offs2):
    idx = unstriped(offs)
    idx2 = unstriped(offs2)
    ekeyu = unpack_weight(ekey_words, ekey_scales, "e4m3")
    keysu = unpack_weight(keys_words, keys_scales, "e2m1")
    ekeyidx2g = ekeyu[:, idx2]
    keysidxg = keysu[:, idx]
    a = ekeyidx2g.T @ keysidxg
    p = np.exp(a - np.max(a, axis=1, keepdims=True))
    w = p * f64(fac) / np.sum(p, axis=1, keepdims=True)
    vt = f64(evals)[:, idx2].T
    vtq = mxq(vt, 0, "e4m3")
    wq = mxq(w, 0, "e4m3")
    o = vtq.T @ wq
    y = f64(vals)[:, idx] + o
    return y

@@ -1,0 +1,171 @@
+from contextlib import ExitStack
+
+import concourse.mybir as mybir
+from concourse.masks import make_identity
+
+D, T, J, I, E = 512, 2048, 512, 512, 512
+FLOPS = 2 * D * J * I + 2 * J * E * I
+
+F32 = mybir.dt.float32
+BF16 = mybir.dt.bfloat16
+I32 = mybir.dt.int32
+U32 = mybir.dt.uint32
+U16 = mybir.dt.uint16
+U8 = mybir.dt.uint8
+FP8X4 = mybir.dt.float8_e4m3fn_x4
+FP4X4 = mybir.dt.float4_e2m1fn_x4
+ALU = mybir.AluOpType
+ACT = mybir.ActivationFunctionType
+AXIS = mybir.AxisListType
+
+P = 128
+PACK = 4
+
+
+def tile_attend_softmerge_kernel(tc, ekey_words, ekey_scales, keys_words, keys_scales, fac, evals, vals, offs, offs2, out):
+    nc = tc.nc
+    blocks = E // P
+    finish_order = [1, 2, 3, 0]
+
+    with ExitStack() as ctx:
+        keep = ctx.enter_context(tc.tile_pool(name="keep", bufs=1))
+        psum = ctx.enter_context(tc.psum_pool(name="psum", bufs=1))
+
+        def sb(shape, dtype, name, tag=None):
+            return keep.tile(shape, dtype, name=name, tag=tag or name, align_bytes=64)
+
+        kept_list = sb([P, I // 16], U16, "kept_list")
+        evicted_list = sb([P, J // 16], U16, "evicted_list")
+        keys_pool = sb([P, T], U16, "keys_pool")
+        ekey_pool = sb([P, T], U32, "ekey_pool")
+        keys_scale_pool = sb([P, T], U8, "keys_scale_pool")
+        ekey_scale_pool = sb([P, T], U8, "ekey_scale_pool")
+        fac_sb = sb([P, PACK], F32, "fac_sb")
+        evals_pool = [sb([P, T], F32, "evals_pool%d" % b) for b in range(blocks)]
+        vals_pool = [sb([P, T], F32, "vals_pool%d" % b) for b in range(blocks)]
+
+        nc.gpsimd.memset(keys_scale_pool[:].bitcast(I32), 0)
+        nc.vector.memset(ekey_scale_pool[:].bitcast(I32), 0)
+
+        def load_scales(pool, scales):
+            for q in range(4):
+                nc.sync.dma_start(pool[32 * q : 32 * q + 4, :].bitcast(I32), scales[0, 4 * q : 4 * q + 4, :].bitcast(I32))
+
+        nc.sync.dma_start(keys_pool[:].bitcast(I32), keys_words[0].bitcast(I32))
+        nc.sync.dma_start(kept_list[:], offs)
+        nc.sync.dma_start(evicted_list[:], offs2)
+        load_scales(keys_scale_pool, keys_scales)
+        nc.sync.dma_start(ekey_pool[:].bitcast(I32), ekey_words[0].rearrange("p n t -> p (n t)").bitcast(I32))
+        load_scales(ekey_scale_pool, ekey_scales)
+        nc.sync.dma_start(evals_pool[0][:], evals[0:P, :])
+        nc.sync.dma_start(fac_sb[:], fac.rearrange("(p t) o -> p (t o)", t=PACK))
+        for b in range(1, blocks):
+            nc.sync.dma_start(evals_pool[b][:], evals[b * P : (b + 1) * P, :])
+        for b in finish_order:
+            nc.sync.dma_start(vals_pool[b][:], vals[b * P : (b + 1) * P, :])
+
+        ident = sb([P, P], F32, "ident")
+        make_identity(nc, ident[:])
+
+        keys_g = sb([P, I], U16, "keys_g")
+        keys_scale_g = sb([P, I], U8, "keys_scale_g")
+        ekey_g = sb([P, J], U32, "ekey_g")
+        ekey_scale_g = sb([P, J], U8, "ekey_scale_g")
+        ekey_scale_d = sb([P, J], U8, "ekey_scale_d")
+        nc.vector.tensor_copy(keys_g[:], keys_pool[:].indirect(kept_list[:]))
+        nc.vector.tensor_copy(keys_scale_g[:], keys_scale_pool[:].indirect(kept_list[:]))
+        nc.vector.tensor_copy(ekey_scale_g[:], ekey_scale_pool[:].indirect(evicted_list[:]))
+        nc.vector.tensor_copy(ekey_g[:].rearrange("p (r s) -> p s r", r=PACK), ekey_pool[:].indirect(evicted_list[:]))
+        nc.vector.tensor_copy(
+            ekey_scale_d[:].rearrange("p (r s) -> p s r", r=PACK), ekey_scale_g[:].rearrange("p (s r) -> p s r", r=PACK)
+        )
+
+        evals_cast = sb([P, T], BF16, "evals_cast")
+        nc.scalar.activation(evals_cast[:], evals_pool[0][:], ACT.Copy)
+
+        banks = [psum.tile([P, I], F32, name="score%d" % r) for r in range(PACK)]
+        for r in range(PACK):
+            cols = slice(r * P, (r + 1) * P)
+            nc.tensor.matmul_mx(
+                out=banks[r][:], lhsT=ekey_g[:, cols].bitcast(FP8X4), lhsT_scale=ekey_scale_d[:, cols],
+                rhs=keys_g[:].bitcast(FP4X4), rhs_scale=keys_scale_g[:], start=True, stop=True,
+            )
+
+        vt_codes = [sb([P, P], U32, "vt_codes%d" % b) for b in range(blocks)]
+        vt_scales = [sb([P, P], U8, "vt_scales%d" % b) for b in range(blocks)]
+        vt_rows = [sb([P, P, PACK], BF16, "vt_rows%d" % b) for b in range(blocks)]
+
+        def turn_evals(b, gathered):
+            words = gathered[:].bitcast(F32)
+            turned = psum.tile([P, 2, P], F32, name="turned%d" % b)
+            for u in range(2):
+                nc.tensor.transpose(turned[:, u, :], words[:, u : J // 2 : 2], ident[:])
+            nc.scalar.copy(vt_rows[b][:].bitcast(F32), turned[:].rearrange("p u e -> p e u"))
+
+        def gather_evals(b):
+            gathered = sb([P, J], BF16, "evals_g%d" % b)
+            nc.vector.tensor_copy(gathered[:], evals_pool[b][:].indirect(evicted_list[:]))
+            turn_evals(b, gathered)
+
+        def quantize_vt(b):
+            nc.vector.quantize_mx(
+                out=vt_codes[b][:].bitcast(FP8X4), scales=vt_scales[b][:],
+                in_=vt_rows[b][:].rearrange("p e t -> p (e t)"),
+            )
+
+        neg_max = [sb([P, 1], F32, "neg_max%d" % r) for r in range(PACK)]
+        row_sum = [sb([P, 2], F32, "row_sum%d" % h) for h in range(2)]
+        inv_sum = [sb([P, 2], F32, "inv_sum%d" % h) for h in range(2)]
+        row_factor = [sb([P, 2], F32, "row_factor%d" % h) for h in range(2)]
+        p_rows = [sb([P, I], F32, "p_rows%d" % r, tag="evals_pool0" if r == 0 else None) for r in range(PACK)]
+        w_rows = sb([P, PACK, I], BF16, "w_rows")
+        w_woven = sb([P, I, PACK], BF16, "w_woven")
+        w_codes = sb([P, I], U32, "w_codes")
+        w_scales = sb([P, I], U8, "w_scales")
+
+        def factors(h):
+            nc.vector.reciprocal(inv_sum[h][:], row_sum[h][:])
+            nc.vector.tensor_tensor(row_factor[h][:], inv_sum[h][:], fac_sb[:, 2 * h : 2 * h + 2], ALU.mult)
+
+        for r in range(PACK):
+            nc.vector.tensor_reduce(neg_max[r][:], banks[r][:], AXIS.X, ALU.max, negate=True)
+            nc.scalar.activation(
+                p_rows[r][:], banks[r][:], ACT.Exp, bias=neg_max[r][:], accum_out=row_sum[r // 2][:, r % 2 : r % 2 + 1]
+            )
+        factors(0)
+        factors(1)
+        for r in range(PACK):
+            nc.scalar.activation(w_rows[:, r, :], p_rows[r][:], ACT.Copy, scale=row_factor[r // 2][:, r % 2 : r % 2 + 1])
+        nc.scalar.copy(
+            w_woven[:].rearrange("p (c i) t -> p c t i", i=4), w_rows[:].rearrange("p t (c i) -> p c t i", i=4)
+        )
+        nc.vector.quantize_mx(
+            out=w_codes[:].bitcast(FP8X4), scales=w_scales[:], in_=w_woven[:].rearrange("p i t -> p (i t)")
+        )
+        for b in range(1, blocks):
+            gather_evals(b)
+            quantize_vt(b)
+        gathered0 = sb([P, J], BF16, "evals_g0", tag="w_rows")
+        nc.scalar.activation(gathered0[:], evals_cast[:].indirect(evicted_list[:]), ACT.Copy)
+        turn_evals(0, gathered0)
+        quantize_vt(0)
+
+        for n, b in enumerate(finish_order):
+            merged = psum.tile([P, I], F32, name="merged%d" % b, tag="score%d" % n)
+            nc.tensor.matmul_mx(
+                out=merged[:], lhsT=vt_codes[b][:].bitcast(FP8X4), lhsT_scale=vt_scales[b][:],
+                rhs=w_codes[:].bitcast(FP8X4), rhs_scale=w_scales[:], start=True, stop=True,
+            )
+            vals_g = sb([P, I], F32, "vals_g%d" % b)
+            pieces = 2 if b == finish_order[-1] else 1
+            width = I // pieces
+            for h in range(pieces):
+                nc.vector.tensor_copy(
+                    vals_g[:, h * width : (h + 1) * width],
+                    vals_pool[b][:].indirect(kept_list[:, h * width // 16 : (h + 1) * width // 16]),
+                )
+            for h in range(pieces):
+                cols = slice(h * width, (h + 1) * width)
+                result = sb([P, width], F32, "result%d_%d" % (b, h))
+                nc.vector.tensor_tensor(result[:], merged[:, cols], vals_g[:, cols], ALU.add)
+                nc.sync.dma_start(out[b * P : (b + 1) * P, cols], result[:])

@@ -25,7 +25,7 @@ PACK = 4
 def tile_attend_softmerge_kernel(tc, ekey_words, ekey_scales, keys_words, keys_scales, fac, evals, vals, offs, offs2, out):
     nc = tc.nc
     blocks = E // P
-    finish_order = [1, 2, 3, 0]
+    finish_order = [0, 1, 2, 3]
 
     with ExitStack() as ctx:
         keep = ctx.enter_context(tc.tile_pool(name="keep", bufs=1))
@@ -80,9 +80,6 @@ def tile_attend_softmerge_kernel(tc, ekey_words, ekey_scales, keys_words, keys_s
             ekey_scale_d[:].rearrange("p (r s) -> p s r", r=PACK), ekey_scale_g[:].rearrange("p (s r) -> p s r", r=PACK)
         )
 
-        evals_cast = sb([P, T], BF16, "evals_cast")
-        nc.scalar.activation(evals_cast[:], evals_pool[0][:], ACT.Copy)
-
         banks = [psum.tile([P, I], F32, name="score%d" % r) for r in range(PACK)]
         for r in range(PACK):
             cols = slice(r * P, (r + 1) * P)
@@ -91,81 +88,112 @@ def tile_attend_softmerge_kernel(tc, ekey_words, ekey_scales, keys_words, keys_s
                 rhs=keys_g[:].bitcast(FP4X4), rhs_scale=keys_scale_g[:], start=True, stop=True,
             )
 
-        vt_codes = [sb([P, P], U32, "vt_codes%d" % b) for b in range(blocks)]
-        vt_scales = [sb([P, P], U8, "vt_scales%d" % b) for b in range(blocks)]
-        vt_rows = [sb([P, P, PACK], BF16, "vt_rows%d" % b) for b in range(blocks)]
+        def gather_evals(b, tag=None):
+            gathered = sb([P, J], BF16, "evals_g%d" % b, tag)
+            nc.vector.tensor_copy(gathered[:], evals_pool[b][:].indirect(evicted_list[:]))
+            return gathered
 
-        def turn_evals(b, gathered):
+        def turn_evals(b, gathered, rows):
             words = gathered[:].bitcast(F32)
             turned = psum.tile([P, 2, P], F32, name="turned%d" % b)
             for u in range(2):
                 nc.tensor.transpose(turned[:, u, :], words[:, u : J // 2 : 2], ident[:])
-            nc.scalar.copy(vt_rows[b][:].bitcast(F32), turned[:].rearrange("p u e -> p e u"))
+            nc.scalar.copy(rows.bitcast(F32).rearrange("p (e u) -> p e u", u=2), turned[:].rearrange("p u e -> p e u"))
 
-        def gather_evals(b):
-            gathered = sb([P, J], BF16, "evals_g%d" % b)
-            nc.vector.tensor_copy(gathered[:], evals_pool[b][:].indirect(evicted_list[:]))
-            turn_evals(b, gathered)
+        def quantize(codes, scales, rows):
+            nc.vector.quantize_mx(out=codes.bitcast(FP8X4), scales=scales, in_=rows)
 
-        def quantize_vt(b):
-            nc.vector.quantize_mx(
-                out=vt_codes[b][:].bitcast(FP8X4), scales=vt_scales[b][:],
-                in_=vt_rows[b][:].rearrange("p e t -> p (e t)"),
-            )
-
-        neg_max = [sb([P, 1], F32, "neg_max%d" % r) for r in range(PACK)]
-        row_sum = [sb([P, 2], F32, "row_sum%d" % h) for h in range(2)]
-        inv_sum = [sb([P, 2], F32, "inv_sum%d" % h) for h in range(2)]
-        row_factor = [sb([P, 2], F32, "row_factor%d" % h) for h in range(2)]
-        p_rows = [sb([P, I], F32, "p_rows%d" % r, tag="evals_pool0" if r == 0 else None) for r in range(PACK)]
-        w_rows = sb([P, PACK, I], BF16, "w_rows")
-        w_woven = sb([P, I, PACK], BF16, "w_woven")
-        w_codes = sb([P, I], U32, "w_codes")
-        w_scales = sb([P, I], U8, "w_scales")
-
-        def factors(h):
-            nc.vector.reciprocal(inv_sum[h][:], row_sum[h][:])
-            nc.vector.tensor_tensor(row_factor[h][:], inv_sum[h][:], fac_sb[:, 2 * h : 2 * h + 2], ALU.mult)
-
-        for r in range(PACK):
-            nc.vector.tensor_reduce(neg_max[r][:], banks[r][:], AXIS.X, ALU.max, negate=True)
-            nc.scalar.activation(
-                p_rows[r][:], banks[r][:], ACT.Exp, bias=neg_max[r][:], accum_out=row_sum[r // 2][:, r % 2 : r % 2 + 1]
-            )
-        factors(0)
-        factors(1)
-        for r in range(PACK):
-            nc.scalar.activation(w_rows[:, r, :], p_rows[r][:], ACT.Copy, scale=row_factor[r // 2][:, r % 2 : r % 2 + 1])
-        nc.scalar.copy(
-            w_woven[:].rearrange("p (c i) t -> p c t i", i=4), w_rows[:].rearrange("p t (c i) -> p c t i", i=4)
-        )
-        nc.vector.quantize_mx(
-            out=w_codes[:].bitcast(FP8X4), scales=w_scales[:], in_=w_woven[:].rearrange("p i t -> p (i t)")
-        )
-        for b in range(1, blocks):
-            gather_evals(b)
-            quantize_vt(b)
-        gathered0 = sb([P, J], BF16, "evals_g0", tag="w_rows")
-        nc.scalar.activation(gathered0[:], evals_cast[:].indirect(evicted_list[:]), ACT.Copy)
-        turn_evals(0, gathered0)
-        quantize_vt(0)
-
-        for n, b in enumerate(finish_order):
-            merged = psum.tile([P, I], F32, name="merged%d" % b, tag="score%d" % n)
-            nc.tensor.matmul_mx(
-                out=merged[:], lhsT=vt_codes[b][:].bitcast(FP8X4), lhsT_scale=vt_scales[b][:],
-                rhs=w_codes[:].bitcast(FP8X4), rhs_scale=w_scales[:], start=True, stop=True,
-            )
-            vals_g = sb([P, I], F32, "vals_g%d" % b)
-            pieces = 2 if b == finish_order[-1] else 1
+        def gather_vals(b, pieces, tag):
+            gathered = sb([P, I], F32, "vals_g%d" % b, tag)
             width = I // pieces
             for h in range(pieces):
                 nc.vector.tensor_copy(
-                    vals_g[:, h * width : (h + 1) * width],
+                    gathered[:, h * width : (h + 1) * width],
                     vals_pool[b][:].indirect(kept_list[:, h * width // 16 : (h + 1) * width // 16]),
                 )
+            return gathered
+
+        def merge(b, codes, scales):
+            merged = psum.tile([P, I], F32, name="merged%d" % b, tag="score%d" % b)
+            nc.tensor.matmul_mx(
+                out=merged[:], lhsT=codes.bitcast(FP8X4), lhsT_scale=scales,
+                rhs=w_codes.bitcast(FP8X4), rhs_scale=w_scales[:], start=True, stop=True,
+            )
+            return merged
+
+        def finish(b, merged, gathered, pieces, tag=None):
+            width = I // pieces
             for h in range(pieces):
                 cols = slice(h * width, (h + 1) * width)
-                result = sb([P, width], F32, "result%d_%d" % (b, h))
-                nc.vector.tensor_tensor(result[:], merged[:, cols], vals_g[:, cols], ALU.add)
+                result = sb([P, width], F32, "result%d_%d" % (b, h), tag)
+                nc.vector.tensor_tensor(result[:], merged[:, cols], gathered[:, cols], ALU.add)
                 nc.sync.dma_start(out[b * P : (b + 1) * P, cols], result[:])
+
+        evals_g0 = gather_evals(0)
+        neg_max = sb([P, PACK], F32, "neg_max", tag="evals_pool0")
+        row_sum = [sb([P, 2], F32, "row_sum%d" % h) for h in range(2)]
+        inv_sum = [sb([P, 2], F32, "inv_sum%d" % h) for h in range(2)]
+        row_factor = [sb([P, 2], F32, "row_factor%d" % h) for h in range(2)]
+        p_rows = [sb([P, I], F32, "p_rows%d" % r) for r in range(PACK)]
+        w_rows = sb([P, PACK, I], BF16, "w_rows")
+        w_woven = sb([P, I, PACK], BF16, "w_woven")
+        w_scales = sb([P, I], U8, "w_scales")
+
+        for r in range(PACK):
+            nc.vector.tensor_reduce(neg_max[:, r : r + 1], banks[r][:], AXIS.X, ALU.max, negate=True)
+            nc.scalar.activation(
+                p_rows[r][:], banks[r][:], ACT.Exp, bias=neg_max[:, r : r + 1], accum_out=row_sum[r // 2][:, r % 2 : r % 2 + 1]
+            )
+        for h in range(2):
+            nc.vector.reciprocal(inv_sum[h][:], row_sum[h][:])
+            nc.vector.tensor_tensor(row_factor[h][:], inv_sum[h][:], fac_sb[:, 2 * h : 2 * h + 2], ALU.mult)
+        for r in range(PACK):
+            nc.scalar.activation(w_rows[:, r, :], p_rows[r][:], ACT.Copy, scale=row_factor[r // 2][:, r % 2 : r % 2 + 1])
+        evals_g1 = gather_evals(1, "inv_sum0")
+        evals_g2 = gather_evals(2, "inv_sum1")
+        woven_view = w_woven[:].rearrange("p (c i) t -> p c t i", i=4)
+        rows_view = w_rows[:].rearrange("p t (c i) -> p c t i", i=4)
+        half = I // 8
+        nc.scalar.copy(woven_view[:, :half], rows_view[:, :half])
+        nc.vector.tensor_copy(woven_view[:, half:], rows_view[:, half:])
+
+        vt_rows0 = sb([P, P * PACK], BF16, "vt_rows0", tag="evals_pool0")
+        vt_codes0 = sb([P, P], U32, "vt_codes0")
+        vt_scales0 = sb([P, P], U8, "vt_scales0")
+        turn_evals(0, evals_g0, vt_rows0[:])
+        quantize(vt_codes0[:], vt_scales0[:], vt_rows0[:])
+
+        vt_rows12 = sb([P, 2 * P * PACK], BF16, "vt_rows12", tag="p_rows3")
+        turn_evals(1, evals_g1, vt_rows12[:, : P * PACK])
+        turn_evals(2, evals_g2, vt_rows12[:, P * PACK :])
+
+        vals_g0 = gather_vals(0, 1, "row_factor1")
+        codes = sb([P, I + 2 * P], U32, "codes", tag="vals_pool0")
+        w_codes = codes[:, :I]
+        vt_codes12 = codes[:, I:]
+        vt_scales12 = sb([P, 2 * P], U8, "vt_scales12")
+        quantize(w_codes, w_scales[:], w_woven[:].rearrange("p i t -> p (i t)"))
+        quantize(vt_codes12, vt_scales12[:], vt_rows12[:])
+
+        last = blocks - 1
+        evals_cast = sb([P, T], BF16, "evals_cast", tag="w_rows")
+        nc.scalar.activation(evals_cast[:], evals_pool[last][:], ACT.Copy)
+        evals_g3 = sb([P, J], BF16, "evals_g3")
+        nc.scalar.activation(evals_g3[:], evals_cast[:].indirect(evicted_list[:]), ACT.Copy)
+        vt_rows3 = sb([P, P * PACK], BF16, "vt_rows3")
+        turn_evals(last, evals_g3, vt_rows3[:])
+
+        merged0 = merge(0, vt_codes0[:], vt_scales0[:])
+        merged1 = merge(1, vt_codes12[:, :P], vt_scales12[:, :P])
+        merged2 = merge(2, vt_codes12[:, P:], vt_scales12[:, P:])
+        vals_g1 = gather_vals(1, 1, "w_woven")
+        finish(0, merged0, vals_g0, 1, "vals_pool1")
+        finish(1, merged1, vals_g1, 1)
+        vals_g2 = gather_vals(2, 1, "w_woven")
+        finish(2, merged2, vals_g2, 1)
+        vt_codes3 = sb([P, P], U32, "vt_codes3", tag="vals_pool2")
+        vt_scales3 = sb([P, P], U8, "vt_scales3")
+        quantize(vt_codes3[:], vt_scales3[:], vt_rows3[:])
+        merged3 = merge(last, vt_codes3[:], vt_scales3[:])
+        vals_g3 = gather_vals(last, 2, "w_woven")
+        finish(last, merged3, vals_g3, 2)

@@ -93,9 +93,9 @@ def tile_attend_softmerge_kernel(tc, ekey_words, ekey_scales, keys_words, keys_s
             nc.vector.tensor_copy(gathered[:], evals_pool[b][:].indirect(evicted_list[:]))
             return gathered
 
-        def turn_evals(b, gathered, rows):
+        def turn_evals(b, gathered, rows, bank=None):
             words = gathered[:].bitcast(F32)
-            turned = psum.tile([P, 2, P], F32, name="turned%d" % b)
+            turned = psum.tile([P, 2, P], F32, name="turned%d" % b, tag=bank or "turned%d" % b)
             for u in range(2):
                 nc.tensor.transpose(turned[:, u, :], words[:, u : J // 2 : 2], ident[:])
             nc.scalar.copy(rows.bitcast(F32).rearrange("p (e u) -> p e u", u=2), turned[:].rearrange("p u e -> p e u"))
@@ -103,40 +103,34 @@ def tile_attend_softmerge_kernel(tc, ekey_words, ekey_scales, keys_words, keys_s
         def quantize(codes, scales, rows):
             nc.vector.quantize_mx(out=codes.bitcast(FP8X4), scales=scales, in_=rows)
 
-        def gather_vals(b, pieces, tag):
-            gathered = sb([P, I], F32, "vals_g%d" % b, tag)
-            width = I // pieces
-            for h in range(pieces):
-                nc.vector.tensor_copy(
-                    gathered[:, h * width : (h + 1) * width],
-                    vals_pool[b][:].indirect(kept_list[:, h * width // 16 : (h + 1) * width // 16]),
-                )
-            return gathered
-
         def merge(b, codes, scales):
             merged = psum.tile([P, I], F32, name="merged%d" % b, tag="score%d" % b)
             nc.tensor.matmul_mx(
                 out=merged[:], lhsT=codes.bitcast(FP8X4), lhsT_scale=scales,
-                rhs=w_codes.bitcast(FP8X4), rhs_scale=w_scales[:], start=True, stop=True,
+                rhs=w_codes[:].bitcast(FP8X4), rhs_scale=w_scales[:], start=True, stop=True,
             )
-            return merged
+            merged_sb = sb([P, I], F32, "merged_sb%d" % b)
+            nc.scalar.copy(merged_sb[:], merged[:])
+            return merged_sb
 
-        def finish(b, merged, gathered, pieces, tag=None):
+        def finish(b, merged_sb, pieces, tag=None):
             width = I // pieces
             for h in range(pieces):
                 cols = slice(h * width, (h + 1) * width)
                 result = sb([P, width], F32, "result%d_%d" % (b, h), tag)
-                nc.vector.tensor_tensor(result[:], merged[:, cols], gathered[:, cols], ALU.add)
+                window = vals_pool[b][:].indirect(kept_list[:, h * width // 16 : (h + 1) * width // 16])
+                nc.vector.tensor_tensor(result[:], window, merged_sb[:, cols], ALU.add)
                 nc.sync.dma_start(out[b * P : (b + 1) * P, cols], result[:])
 
         evals_g0 = gather_evals(0)
         neg_max = sb([P, PACK], F32, "neg_max", tag="evals_pool0")
         row_sum = [sb([P, 2], F32, "row_sum%d" % h) for h in range(2)]
         inv_sum = [sb([P, 2], F32, "inv_sum%d" % h) for h in range(2)]
-        row_factor = [sb([P, 2], F32, "row_factor%d" % h) for h in range(2)]
+        row_factor = sb([P, 2], F32, "row_factor")
         p_rows = [sb([P, I], F32, "p_rows%d" % r) for r in range(PACK)]
-        w_rows = sb([P, PACK, I], BF16, "w_rows")
+        w_pairs = sb([P, 2, I, 2], BF16, "w_pairs")
         w_woven = sb([P, I, PACK], BF16, "w_woven")
+        w_codes = sb([P, I], U32, "w_codes")
         w_scales = sb([P, I], U8, "w_scales")
 
         for r in range(PACK):
@@ -144,56 +138,46 @@ def tile_attend_softmerge_kernel(tc, ekey_words, ekey_scales, keys_words, keys_s
             nc.scalar.activation(
                 p_rows[r][:], banks[r][:], ACT.Exp, bias=neg_max[:, r : r + 1], accum_out=row_sum[r // 2][:, r % 2 : r % 2 + 1]
             )
-        for h in range(2):
-            nc.vector.reciprocal(inv_sum[h][:], row_sum[h][:])
-            nc.vector.tensor_tensor(row_factor[h][:], inv_sum[h][:], fac_sb[:, 2 * h : 2 * h + 2], ALU.mult)
-        for r in range(PACK):
-            nc.scalar.activation(w_rows[:, r, :], p_rows[r][:], ACT.Copy, scale=row_factor[r // 2][:, r % 2 : r % 2 + 1])
+        nc.vector.reciprocal(inv_sum[0][:], row_sum[0][:])
+        nc.vector.tensor_tensor(row_factor[:], inv_sum[0][:], fac_sb[:, 0:2], ALU.mult)
+        nc.vector.reciprocal(inv_sum[1][:], row_sum[1][:])
+        for e in range(2):
+            nc.scalar.activation(w_pairs[:, 0, :, e], p_rows[e][:], ACT.Copy, scale=row_factor[:, e : e + 1])
+        for e in range(2):
+            nc.vector.tensor_scalar(
+                w_pairs[:, 1, :, e], p_rows[2 + e][:], inv_sum[1][:, e : e + 1], fac_sb[:, 2 + e : 3 + e], ALU.mult, ALU.mult
+            )
         evals_g1 = gather_evals(1, "inv_sum0")
-        evals_g2 = gather_evals(2, "inv_sum1")
-        woven_view = w_woven[:].rearrange("p (c i) t -> p c t i", i=4)
-        rows_view = w_rows[:].rearrange("p t (c i) -> p c t i", i=4)
-        half = I // 8
-        nc.scalar.copy(woven_view[:, :half], rows_view[:, :half])
-        nc.vector.tensor_copy(woven_view[:, half:], rows_view[:, half:])
-
+        evals_g2 = gather_evals(2, "p_rows3")
+        nc.scalar.copy(
+            w_woven[:].bitcast(F32), w_pairs[:].bitcast(F32).rearrange("p u i o -> p i (u o)")
+        )
         vt_rows0 = sb([P, P * PACK], BF16, "vt_rows0", tag="evals_pool0")
         vt_codes0 = sb([P, P], U32, "vt_codes0")
         vt_scales0 = sb([P, P], U8, "vt_scales0")
         turn_evals(0, evals_g0, vt_rows0[:])
         quantize(vt_codes0[:], vt_scales0[:], vt_rows0[:])
+        quantize(w_codes[:], w_scales[:], w_woven[:].rearrange("p i t -> p (i t)"))
 
-        vt_rows12 = sb([P, 2 * P * PACK], BF16, "vt_rows12", tag="p_rows3")
+        vt_rows12 = sb([P, 2 * P * PACK], BF16, "vt_rows12", tag="w_pairs")
         turn_evals(1, evals_g1, vt_rows12[:, : P * PACK])
         turn_evals(2, evals_g2, vt_rows12[:, P * PACK :])
-
-        vals_g0 = gather_vals(0, 1, "row_factor1")
-        codes = sb([P, I + 2 * P], U32, "codes", tag="vals_pool0")
-        w_codes = codes[:, :I]
-        vt_codes12 = codes[:, I:]
-        vt_scales12 = sb([P, 2 * P], U8, "vt_scales12")
-        quantize(w_codes, w_scales[:], w_woven[:].rearrange("p i t -> p (i t)"))
-        quantize(vt_codes12, vt_scales12[:], vt_rows12[:])
-
-        last = blocks - 1
-        evals_cast = sb([P, T], BF16, "evals_cast", tag="w_rows")
-        nc.scalar.activation(evals_cast[:], evals_pool[last][:], ACT.Copy)
-        evals_g3 = sb([P, J], BF16, "evals_g3")
-        nc.scalar.activation(evals_g3[:], evals_cast[:].indirect(evicted_list[:]), ACT.Copy)
-        vt_rows3 = sb([P, P * PACK], BF16, "vt_rows3")
-        turn_evals(last, evals_g3, vt_rows3[:])
-
         merged0 = merge(0, vt_codes0[:], vt_scales0[:])
+
+        evals_g3 = gather_evals(3, "w_woven")
+        vt_codes12 = sb([P, 2 * P], U32, "vt_codes12", tag="evals_pool3")
+        vt_scales12 = sb([P, 2 * P], U8, "vt_scales12")
+        quantize(vt_codes12[:], vt_scales12[:], vt_rows12[:])
+        vt_rows3 = sb([P, P * PACK], BF16, "vt_rows3")
+        turn_evals(3, evals_g3, vt_rows3[:])
         merged1 = merge(1, vt_codes12[:, :P], vt_scales12[:, :P])
         merged2 = merge(2, vt_codes12[:, P:], vt_scales12[:, P:])
-        vals_g1 = gather_vals(1, 1, "w_woven")
-        finish(0, merged0, vals_g0, 1, "vals_pool1")
-        finish(1, merged1, vals_g1, 1)
-        vals_g2 = gather_vals(2, 1, "w_woven")
-        finish(2, merged2, vals_g2, 1)
-        vt_codes3 = sb([P, P], U32, "vt_codes3", tag="vals_pool2")
+
+        finish(0, merged0, 1, "w_pairs")
+        vt_codes3 = sb([P, P], U32, "vt_codes3", tag="vals_pool0")
         vt_scales3 = sb([P, P], U8, "vt_scales3")
         quantize(vt_codes3[:], vt_scales3[:], vt_rows3[:])
-        merged3 = merge(last, vt_codes3[:], vt_scales3[:])
-        vals_g3 = gather_vals(last, 2, "w_woven")
-        finish(last, merged3, vals_g3, 2)
+        merged3 = merge(3, vt_codes3[:], vt_scales3[:])
+        finish(1, merged1, 1, "vt_rows3")
+        finish(2, merged2, 1)
+        finish(3, merged3, 2)

@@ -48,8 +48,8 @@ def tile_attend_softmerge_kernel(tc, ekey_words, ekey_scales, keys_words, keys_s
         nc.vector.memset(ekey_scale_pool[:].bitcast(I32), 0)
 
         def load_scales(pool, scales):
-            for q in range(4):
-                nc.sync.dma_start(pool[32 * q : 32 * q + 4, :].bitcast(I32), scales[0, 4 * q : 4 * q + 4, :].bitcast(I32))
+            for r in range(4):
+                nc.sync.dma_start(pool[r:P:32, :].bitcast(I32), scales[0, r:16:4, :].bitcast(I32))
 
         nc.sync.dma_start(keys_pool[:].bitcast(I32), keys_words[0].bitcast(I32))
         nc.sync.dma_start(kept_list[:], offs)
@@ -57,12 +57,15 @@ def tile_attend_softmerge_kernel(tc, ekey_words, ekey_scales, keys_words, keys_s
         load_scales(keys_scale_pool, keys_scales)
         nc.sync.dma_start(ekey_pool[:].bitcast(I32), ekey_words[0].rearrange("p n t -> p (n t)").bitcast(I32))
         load_scales(ekey_scale_pool, ekey_scales)
-        nc.sync.dma_start(evals_pool[0][:], evals[0:P, :])
+        nc.sync.dma_start(evals_pool[0][:], evals[0 * P : 1 * P, :])
         nc.sync.dma_start(fac_sb[:], fac.rearrange("(p t) o -> p (t o)", t=PACK))
-        for b in range(1, blocks):
-            nc.sync.dma_start(evals_pool[b][:], evals[b * P : (b + 1) * P, :])
-        for b in finish_order:
-            nc.sync.dma_start(vals_pool[b][:], vals[b * P : (b + 1) * P, :])
+        nc.sync.dma_start(evals_pool[1][:], evals[1 * P : 2 * P, :])
+        nc.sync.dma_start(evals_pool[2][:], evals[2 * P : 3 * P, :])
+        nc.sync.dma_start(evals_pool[3][:], evals[3 * P : 4 * P, :])
+        nc.sync.dma_start(vals_pool[0][:], vals[0 * P : 1 * P, :])
+        nc.sync.dma_start(vals_pool[1][:], vals[1 * P : 2 * P, :])
+        nc.sync.dma_start(vals_pool[2][:], vals[2 * P : 3 * P, :])
+        nc.sync.dma_start(vals_pool[3][:], vals[3 * P : 4 * P, :])
 
         ident = sb([P, P], F32, "ident")
         make_identity(nc, ident[:])
@@ -74,10 +77,10 @@ def tile_attend_softmerge_kernel(tc, ekey_words, ekey_scales, keys_words, keys_s
         ekey_scale_d = sb([P, J], U8, "ekey_scale_d")
         nc.vector.tensor_copy(keys_g[:], keys_pool[:].indirect(kept_list[:]))
         nc.vector.tensor_copy(keys_scale_g[:], keys_scale_pool[:].indirect(kept_list[:]))
-        nc.vector.tensor_copy(ekey_scale_g[:], ekey_scale_pool[:].indirect(evicted_list[:]))
         nc.vector.tensor_copy(ekey_g[:].rearrange("p (r s) -> p s r", r=PACK), ekey_pool[:].indirect(evicted_list[:]))
+        nc.vector.tensor_copy(ekey_scale_g[:], ekey_scale_pool[:].indirect(evicted_list[:]))
         nc.vector.tensor_copy(
-            ekey_scale_d[:].rearrange("p (r s) -> p s r", r=PACK), ekey_scale_g[:].rearrange("p (s r) -> p s r", r=PACK)
+            ekey_scale_d[:].rearrange("p (r s) -> p r s", r=PACK), ekey_scale_g[:].rearrange("p (s r) -> p r s", r=PACK)
         )
 
         banks = [psum.tile([P, I], F32, name="score%d" % r) for r in range(PACK)]

@@ -20,18 +20,21 @@ AXIS = mybir.AxisListType
 
 P = 128
 PACK = 4
+KIB = 1024
 
 
 def tile_attend_softmerge_kernel(tc, ekey_words, ekey_scales, keys_words, keys_scales, fac, evals, vals, offs, offs2, out):
     nc = tc.nc
     blocks = E // P
-    finish_order = [0, 1, 2, 3]
 
     with ExitStack() as ctx:
         keep = ctx.enter_context(tc.tile_pool(name="keep", bufs=1))
+        placed = ctx.enter_context(tc.tile_pool(name="placed", bufs=1))
         psum = ctx.enter_context(tc.psum_pool(name="psum", bufs=1))
 
-        def sb(shape, dtype, name, tag=None):
+        def sb(shape, dtype, name, tag=None, at=None):
+            if at is not None:
+                return placed.tile(shape, dtype, name=name, align_bytes=64, offset=at)
             return keep.tile(shape, dtype, name=name, tag=tag or name, align_bytes=64)
 
         kept_list = sb([P, I // 16], U16, "kept_list")
@@ -40,12 +43,12 @@ def tile_attend_softmerge_kernel(tc, ekey_words, ekey_scales, keys_words, keys_s
         ekey_pool = sb([P, T], U32, "ekey_pool")
         keys_scale_pool = sb([P, T], U8, "keys_scale_pool")
         ekey_scale_pool = sb([P, T], U8, "ekey_scale_pool")
-        fac_sb = sb([P, PACK], F32, "fac_sb")
-        evals_pool = [sb([P, T], F32, "evals_pool%d" % b) for b in range(blocks)]
-        vals_pool = [sb([P, T], F32, "vals_pool%d" % b) for b in range(blocks)]
+        fac_sb = [sb([P, 2], F32, "fac_sb%d" % h) for h in range(2)]
+        evals_pool = [sb([P, T], F32, "evals_pool%d" % b, at={0: 0, 3: 16 * KIB}.get(b)) for b in range(blocks)]
+        vals_pool = [sb([P, T], F32, "vals_pool%d" % b, at=8 * KIB if b == 0 else None) for b in range(blocks)]
 
-        nc.gpsimd.memset(keys_scale_pool[:].bitcast(I32), 0)
-        nc.vector.memset(ekey_scale_pool[:].bitcast(I32), 0)
+        nc.gpsimd.memset(ekey_scale_pool[:].bitcast(I32), 0)
+        nc.vector.memset(keys_scale_pool[:].bitcast(I32), 0)
 
         def load_scales(pool, scales):
             for r in range(4):
@@ -54,34 +57,33 @@ def tile_attend_softmerge_kernel(tc, ekey_words, ekey_scales, keys_words, keys_s
         nc.sync.dma_start(keys_pool[:].bitcast(I32), keys_words[0].bitcast(I32))
         nc.sync.dma_start(kept_list[:], offs)
         nc.sync.dma_start(evicted_list[:], offs2)
-        load_scales(keys_scale_pool, keys_scales)
-        nc.sync.dma_start(ekey_pool[:].bitcast(I32), ekey_words[0].rearrange("p n t -> p (n t)").bitcast(I32))
         load_scales(ekey_scale_pool, ekey_scales)
-        nc.sync.dma_start(evals_pool[0][:], evals[0 * P : 1 * P, :])
-        nc.sync.dma_start(fac_sb[:], fac.rearrange("(p t) o -> p (t o)", t=PACK))
-        nc.sync.dma_start(evals_pool[1][:], evals[1 * P : 2 * P, :])
-        nc.sync.dma_start(evals_pool[2][:], evals[2 * P : 3 * P, :])
-        nc.sync.dma_start(evals_pool[3][:], evals[3 * P : 4 * P, :])
-        nc.sync.dma_start(vals_pool[0][:], vals[0 * P : 1 * P, :])
-        nc.sync.dma_start(vals_pool[1][:], vals[1 * P : 2 * P, :])
-        nc.sync.dma_start(vals_pool[2][:], vals[2 * P : 3 * P, :])
-        nc.sync.dma_start(vals_pool[3][:], vals[3 * P : 4 * P, :])
+        nc.sync.dma_start(ekey_pool[:].bitcast(I32), ekey_words[0].rearrange("p n t -> p (n t)").bitcast(I32))
+        load_scales(keys_scale_pool, keys_scales)
+        for b in range(blocks):
+            nc.sync.dma_start(evals_pool[b][:], evals[b * P : (b + 1) * P, :])
+            if b % 2 == 0:
+                nc.sync.dma_start(fac_sb[b // 2][:], fac.rearrange("(p t) o -> p (t o)", t=PACK)[:, b : b + 2])
+        for b in range(blocks):
+            nc.sync.dma_start(vals_pool[b][:], vals[b * P : (b + 1) * P, :])
 
         ident = sb([P, P], F32, "ident")
         make_identity(nc, ident[:])
+        minus_one = sb([P, 2], F32, "minus_one")
+        nc.gpsimd.memset(minus_one[:], -1.0)
 
         keys_g = sb([P, I], U16, "keys_g")
         keys_scale_g = sb([P, I], U8, "keys_scale_g")
         ekey_g = sb([P, J], U32, "ekey_g")
         ekey_scale_g = sb([P, J], U8, "ekey_scale_g")
-        ekey_scale_d = sb([P, J], U8, "ekey_scale_d")
         nc.vector.tensor_copy(keys_g[:], keys_pool[:].indirect(kept_list[:]))
-        nc.vector.tensor_copy(keys_scale_g[:], keys_scale_pool[:].indirect(kept_list[:]))
-        nc.vector.tensor_copy(ekey_g[:].rearrange("p (r s) -> p s r", r=PACK), ekey_pool[:].indirect(evicted_list[:]))
         nc.vector.tensor_copy(ekey_scale_g[:], ekey_scale_pool[:].indirect(evicted_list[:]))
+        ekey_scale_d = sb([P, J], U8, "ekey_scale_d")
         nc.vector.tensor_copy(
             ekey_scale_d[:].rearrange("p (r s) -> p r s", r=PACK), ekey_scale_g[:].rearrange("p (s r) -> p r s", r=PACK)
         )
+        nc.vector.tensor_copy(ekey_g[:].rearrange("p (r s) -> p s r", r=PACK), ekey_pool[:].indirect(evicted_list[:]))
+        nc.vector.tensor_copy(keys_scale_g[:], keys_scale_pool[:].indirect(kept_list[:]))
 
         banks = [psum.tile([P, I], F32, name="score%d" % r) for r in range(PACK)]
         for r in range(PACK):
@@ -91,96 +93,90 @@ def tile_attend_softmerge_kernel(tc, ekey_words, ekey_scales, keys_words, keys_s
                 rhs=keys_g[:].bitcast(FP4X4), rhs_scale=keys_scale_g[:], start=True, stop=True,
             )
 
-        def gather_evals(b, tag=None):
-            gathered = sb([P, J], BF16, "evals_g%d" % b, tag)
+        def gather_evals(b, tag=None, at=None):
+            gathered = sb([P, J], BF16, "evals_g%d" % b, tag, at)
             nc.vector.tensor_copy(gathered[:], evals_pool[b][:].indirect(evicted_list[:]))
             return gathered
 
-        def turn_evals(b, gathered, rows, bank=None):
-            words = gathered[:].bitcast(F32)
-            turned = psum.tile([P, 2, P], F32, name="turned%d" % b, tag=bank or "turned%d" % b)
-            for u in range(2):
-                nc.tensor.transpose(turned[:, u, :], words[:, u : J // 2 : 2], ident[:])
-            nc.scalar.copy(rows.bitcast(F32).rearrange("p (e u) -> p e u", u=2), turned[:].rearrange("p u e -> p e u"))
+        def turn(h, gathered, rows):
+            turned = psum.tile([P, len(gathered), 2, P], F32, name="turned%d" % h)
+            for c in range(len(gathered)):
+                words = gathered[c][:].bitcast(F32)
+                for u in range(2):
+                    nc.tensor.transpose(turned[:, c, u, :], words[:, u : J // 2 : 2], ident[:])
+            nc.scalar.copy(rows[:].bitcast(F32).rearrange("p (c e u) -> p c e u", e=P, u=2), turned[:].rearrange("p c u e -> p c e u"))
 
         def quantize(codes, scales, rows):
             nc.vector.quantize_mx(out=codes.bitcast(FP8X4), scales=scales, in_=rows)
 
-        def merge(b, codes, scales):
-            merged = psum.tile([P, I], F32, name="merged%d" % b, tag="score%d" % b)
+        def finish(b, codes, scales, cols, bank):
+            width = cols.stop - cols.start
+            merged = psum.tile([P, width], F32, name="merged%d_%d" % (b, cols.start), tag=bank)
             nc.tensor.matmul_mx(
                 out=merged[:], lhsT=codes.bitcast(FP8X4), lhsT_scale=scales,
-                rhs=w_codes[:].bitcast(FP8X4), rhs_scale=w_scales[:], start=True, stop=True,
+                rhs=w_codes[:, cols].bitcast(FP8X4), rhs_scale=w_scales[:, cols], start=True, stop=True,
             )
-            merged_sb = sb([P, I], F32, "merged_sb%d" % b)
+            merged_sb = sb([P, width], F32, "merged_sb%d_%d" % (b, cols.start))
             nc.scalar.copy(merged_sb[:], merged[:])
-            return merged_sb
-
-        def finish(b, merged_sb, pieces, tag=None):
-            width = I // pieces
+            pieces = 2 if b == blocks - 1 else 1
+            part = width // pieces
             for h in range(pieces):
-                cols = slice(h * width, (h + 1) * width)
-                result = sb([P, width], F32, "result%d_%d" % (b, h), tag)
-                window = vals_pool[b][:].indirect(kept_list[:, h * width // 16 : (h + 1) * width // 16])
-                nc.vector.tensor_tensor(result[:], window, merged_sb[:, cols], ALU.add)
-                nc.sync.dma_start(out[b * P : (b + 1) * P, cols], result[:])
+                first = cols.start + h * part
+                result = sb([P, part], F32, "result%d_%d" % (b, first))
+                window = vals_pool[b][:].indirect(kept_list[:, first // 16 : (first + part) // 16])
+                nc.vector.tensor_tensor(result[:], window, merged_sb[:, h * part : (h + 1) * part], ALU.add)
+                nc.sync.dma_start(out[b * P : (b + 1) * P, first : first + part], result[:])
 
         evals_g0 = gather_evals(0)
-        neg_max = sb([P, PACK], F32, "neg_max", tag="evals_pool0")
+        neg_max = [sb([P, 1], F32, "neg_max%d" % r, at=r * KIB) for r in range(PACK)]
         row_sum = [sb([P, 2], F32, "row_sum%d" % h) for h in range(2)]
-        inv_sum = [sb([P, 2], F32, "inv_sum%d" % h) for h in range(2)]
+        inv_sum = [sb([P, 2], F32, "inv_sum%d" % h, "inv_sum") for h in range(2)]
         row_factor = sb([P, 2], F32, "row_factor")
         p_rows = [sb([P, I], F32, "p_rows%d" % r) for r in range(PACK)]
         w_pairs = sb([P, 2, I, 2], BF16, "w_pairs")
-        w_woven = sb([P, I, PACK], BF16, "w_woven")
-        w_codes = sb([P, I], U32, "w_codes")
+        w_woven = [sb([P, I // 2, PACK], BF16, "w_woven%d" % h) for h in range(2)]
         w_scales = sb([P, I], U8, "w_scales")
+        halves = [slice(0, I // 2), slice(I // 2, I)]
 
         for r in range(PACK):
-            nc.vector.tensor_reduce(neg_max[:, r : r + 1], banks[r][:], AXIS.X, ALU.max, negate=True)
+            nc.vector.tensor_reduce(neg_max[r][:], banks[r][:], AXIS.X, ALU.max, negate=True)
             nc.scalar.activation(
-                p_rows[r][:], banks[r][:], ACT.Exp, bias=neg_max[:, r : r + 1], accum_out=row_sum[r // 2][:, r % 2 : r % 2 + 1]
+                p_rows[r][:], banks[r][:], ACT.Exp, bias=neg_max[r][:], accum_out=row_sum[r // 2][:, r % 2 : r % 2 + 1]
             )
-        nc.vector.reciprocal(inv_sum[0][:], row_sum[0][:])
-        nc.vector.tensor_tensor(row_factor[:], inv_sum[0][:], fac_sb[:, 0:2], ALU.mult)
-        nc.vector.reciprocal(inv_sum[1][:], row_sum[1][:])
+        evals_g1 = gather_evals(1, at=0)
+        evals_g2 = gather_evals(2, at=KIB)
+        nc.gpsimd.tensor_tensor(inv_sum[0][:], row_sum[0][:], minus_one[:], ALU.pow)
+        nc.gpsimd.tensor_tensor(row_factor[:], inv_sum[0][:], fac_sb[0][:], ALU.mult)
+        nc.gpsimd.tensor_tensor(inv_sum[1][:], row_sum[1][:], minus_one[:], ALU.pow)
         for e in range(2):
             nc.scalar.activation(w_pairs[:, 0, :, e], p_rows[e][:], ACT.Copy, scale=row_factor[:, e : e + 1])
         for e in range(2):
             nc.vector.tensor_scalar(
-                w_pairs[:, 1, :, e], p_rows[2 + e][:], inv_sum[1][:, e : e + 1], fac_sb[:, 2 + e : 3 + e], ALU.mult, ALU.mult
+                w_pairs[:, 1, :, e], p_rows[2 + e][:], inv_sum[1][:, e : e + 1], fac_sb[1][:, e : e + 1], ALU.mult, ALU.mult
             )
-        evals_g1 = gather_evals(1, "inv_sum0")
-        evals_g2 = gather_evals(2, "p_rows3")
-        nc.scalar.copy(
-            w_woven[:].bitcast(F32), w_pairs[:].bitcast(F32).rearrange("p u i o -> p i (u o)")
-        )
-        vt_rows0 = sb([P, P * PACK], BF16, "vt_rows0", tag="evals_pool0")
-        vt_codes0 = sb([P, P], U32, "vt_codes0")
+        vt_rows0 = sb([P, P * PACK], BF16, "vt_rows0", at=3 * KIB)
+        turn(0, [evals_g0], vt_rows0)
+        vt_codes0 = sb([P, P], U32, "vt_codes0", tag="p_rows2")
         vt_scales0 = sb([P, P], U8, "vt_scales0")
-        turn_evals(0, evals_g0, vt_rows0[:])
         quantize(vt_codes0[:], vt_scales0[:], vt_rows0[:])
-        quantize(w_codes[:], w_scales[:], w_woven[:].rearrange("p i t -> p (i t)"))
+        evals_g3 = gather_evals(3, at=3 * KIB)
+        vt_rows1 = sb([P, P * PACK], BF16, "vt_rows1", tag="p_rows0")
+        turn(1, [evals_g1], vt_rows1)
+        vt_codes1 = sb([P, P], U32, "vt_codes1", at=16 * KIB)
+        w_codes = sb([P, I], U32, "w_codes", at=17 * KIB)
+        vt_scales1 = sb([P, P], U8, "vt_scales1")
+        quantize(vt_codes1[:], vt_scales1[:], vt_rows1[:])
+        for h in range(2):
+            nc.scalar.copy(w_woven[h][:].bitcast(F32), w_pairs[:, :, halves[h], :].bitcast(F32).rearrange("p u i o -> p i (u o)"))
+            quantize(w_codes[:, halves[h]], w_scales[:, halves[h]], w_woven[h][:].rearrange("p i t -> p (i t)"))
 
-        vt_rows12 = sb([P, 2 * P * PACK], BF16, "vt_rows12", tag="w_pairs")
-        turn_evals(1, evals_g1, vt_rows12[:, : P * PACK])
-        turn_evals(2, evals_g2, vt_rows12[:, P * PACK :])
-        merged0 = merge(0, vt_codes0[:], vt_scales0[:])
-
-        evals_g3 = gather_evals(3, "w_woven")
-        vt_codes12 = sb([P, 2 * P], U32, "vt_codes12", tag="evals_pool3")
-        vt_scales12 = sb([P, 2 * P], U8, "vt_scales12")
-        quantize(vt_codes12[:], vt_scales12[:], vt_rows12[:])
-        vt_rows3 = sb([P, P * PACK], BF16, "vt_rows3")
-        turn_evals(3, evals_g3, vt_rows3[:])
-        merged1 = merge(1, vt_codes12[:, :P], vt_scales12[:, :P])
-        merged2 = merge(2, vt_codes12[:, P:], vt_scales12[:, P:])
-
-        finish(0, merged0, 1, "w_pairs")
-        vt_codes3 = sb([P, P], U32, "vt_codes3", tag="vals_pool0")
-        vt_scales3 = sb([P, P], U8, "vt_scales3")
-        quantize(vt_codes3[:], vt_scales3[:], vt_rows3[:])
-        merged3 = merge(3, vt_codes3[:], vt_scales3[:])
-        finish(1, merged1, 1, "vt_rows3")
-        finish(2, merged2, 1)
-        finish(3, merged3, 2)
+        vt_rows23 = sb([P, 2 * P * PACK], BF16, "vt_rows23", tag="w_pairs")
+        turn(2, [evals_g2, evals_g3], vt_rows23)
+        vt_codes23 = sb([P, 2 * P], U32, "vt_codes23", tag="w_woven0")
+        vt_scales23 = sb([P, 2 * P], U8, "vt_scales23")
+        quantize(vt_codes23[:], vt_scales23[:], vt_rows23[:])
+        finish(0, vt_codes0[:], vt_scales0[:], halves[0], "score0")
+        finish(0, vt_codes0[:], vt_scales0[:], halves[1], "spare")
+        finish(1, vt_codes1[:], vt_scales1[:], slice(0, I), "score1")
+        finish(2, vt_codes23[:, :P], vt_scales23[:, :P], slice(0, I), "score2")
+        finish(3, vt_codes23[:, P:], vt_scales23[:, P:], slice(0, I), "score3")

@@ -104,7 +104,7 @@ def tile_attend_softmerge_kernel(tc, ekey_words, ekey_scales, keys_words, keys_s
                 words = gathered[c][:].bitcast(F32)
                 for u in range(2):
                     nc.tensor.transpose(turned[:, c, u, :], words[:, u : J // 2 : 2], ident[:])
-            nc.scalar.copy(rows[:].bitcast(F32).rearrange("p (c e u) -> p c e u", e=P, u=2), turned[:].rearrange("p c u e -> p c e u"))
+            nc.scalar.copy(rows.bitcast(F32).rearrange("p (c e u) -> p c e u", e=P, u=2), turned[:].rearrange("p c u e -> p c e u"))
 
         def quantize(codes, scales, rows):
             nc.vector.quantize_mx(out=codes.bitcast(FP8X4), scales=scales, in_=rows)
@@ -155,28 +155,29 @@ def tile_attend_softmerge_kernel(tc, ekey_words, ekey_scales, keys_words, keys_s
                 w_pairs[:, 1, :, e], p_rows[2 + e][:], inv_sum[1][:, e : e + 1], fac_sb[1][:, e : e + 1], ALU.mult, ALU.mult
             )
         vt_rows0 = sb([P, P * PACK], BF16, "vt_rows0", at=3 * KIB)
-        turn(0, [evals_g0], vt_rows0)
+        turn(0, [evals_g0], vt_rows0[:])
         vt_codes0 = sb([P, P], U32, "vt_codes0", tag="p_rows2")
         vt_scales0 = sb([P, P], U8, "vt_scales0")
         quantize(vt_codes0[:], vt_scales0[:], vt_rows0[:])
         evals_g3 = gather_evals(3, at=3 * KIB)
         vt_rows1 = sb([P, P * PACK], BF16, "vt_rows1", tag="p_rows0")
-        turn(1, [evals_g1], vt_rows1)
+        turn(1, [evals_g1], vt_rows1[:])
         vt_codes1 = sb([P, P], U32, "vt_codes1", at=16 * KIB)
         w_codes = sb([P, I], U32, "w_codes", at=17 * KIB)
         vt_scales1 = sb([P, P], U8, "vt_scales1")
-        quantize(vt_codes1[:], vt_scales1[:], vt_rows1[:])
         for h in range(2):
             nc.scalar.copy(w_woven[h][:].bitcast(F32), w_pairs[:, :, halves[h], :].bitcast(F32).rearrange("p u i o -> p i (u o)"))
             quantize(w_codes[:, halves[h]], w_scales[:, halves[h]], w_woven[h][:].rearrange("p i t -> p (i t)"))
+        quantize(vt_codes1[:], vt_scales1[:], vt_rows1[:])
 
         vt_rows23 = sb([P, 2 * P * PACK], BF16, "vt_rows23", tag="w_pairs")
-        turn(2, [evals_g2, evals_g3], vt_rows23)
+        turn(2, [evals_g2], vt_rows23[:, : P * PACK])
+        turn(3, [evals_g3], vt_rows23[:, P * PACK :])
         vt_codes23 = sb([P, 2 * P], U32, "vt_codes23", tag="w_woven0")
         vt_scales23 = sb([P, 2 * P], U8, "vt_scales23")
         quantize(vt_codes23[:], vt_scales23[:], vt_rows23[:])
         finish(0, vt_codes0[:], vt_scales0[:], halves[0], "score0")
-        finish(0, vt_codes0[:], vt_scales0[:], halves[1], "spare")
+        finish(0, vt_codes0[:], vt_scales0[:], halves[1], "turned0")
         finish(1, vt_codes1[:], vt_scales1[:], slice(0, I), "score1")
         finish(2, vt_codes23[:, :P], vt_scales23[:, :P], slice(0, I), "score2")
         finish(3, vt_codes23[:, P:], vt_scales23[:, P:], slice(0, I), "score3")

@@ -21,6 +21,7 @@ AXIS = mybir.AxisListType
 P = 128
 PACK = 4
 KIB = 1024
+ROW0 = P - 16
 
 
 def tile_attend_softmerge_kernel(tc, ekey_words, ekey_scales, keys_words, keys_scales, fac, evals, vals, offs, offs2, out):
@@ -39,58 +40,68 @@ def tile_attend_softmerge_kernel(tc, ekey_words, ekey_scales, keys_words, keys_s
 
         kept_list = sb([P, I // 16], U16, "kept_list")
         evicted_list = sb([P, J // 16], U16, "evicted_list")
-        keys_pool = sb([P, T], U16, "keys_pool")
-        ekey_pool = sb([P, T], U32, "ekey_pool")
-        keys_scale_pool = sb([P, T], U8, "keys_scale_pool")
+        ev0_at, kscg_at, ekey_at, ksc_at, keys_at = 8 * KIB, 32 * KIB, 52 * KIB, 68 * KIB, 72 * KIB
+
+        def below(at):
+            return at + 128 - 8 * KIB
+
+        def above(at, size):
+            return at + size - 128
+
+        keys_pool = sb([P, T], U16, "keys_pool", at=keys_at)
+        ekey_pool = sb([P, T], U32, "ekey_pool", at=ekey_at)
+        keys_scale_pool = sb([P, T], U8, "keys_scale_pool", at=ksc_at)
         ekey_scale_pool = sb([P, T], U8, "ekey_scale_pool")
-        fac_sb = [sb([P, 2], F32, "fac_sb%d" % h) for h in range(2)]
-        evals_pool = [sb([P, T], F32, "evals_pool%d" % b, at={0: 0, 3: 16 * KIB}.get(b)) for b in range(blocks)]
-        vals_pool = [sb([P, T], F32, "vals_pool%d" % b, at=8 * KIB if b == 0 else None) for b in range(blocks)]
+        fac_sb = sb([P, PACK], F32, "fac_sb")
+        evals_at = [ev0_at, below(kscg_at), above(kscg_at, I), below(ekey_at)]
+        vals_at = [above(ekey_at, 8 * KIB), below(ev0_at), above(ev0_at, 8 * KIB), evals_at[1]]
+        evals_pool = [sb([P, T], F32, "evals_pool%d" % b, at=evals_at[b]) for b in range(blocks)]
+        vals_pool = [sb([P, T], F32, "vals_pool%d" % b, at=vals_at[b]) for b in range(blocks)]
+        stats_at = ev0_at + KIB
+        codes_at = evals_at[3] + KIB // 2
 
-        nc.gpsimd.memset(ekey_scale_pool[:].bitcast(I32), 0)
-        nc.vector.memset(keys_scale_pool[:].bitcast(I32), 0)
+        nc.gpsimd.memset(ekey_scale_pool[:ROW0, :].bitcast(I32), 0)
+        nc.vector.memset(keys_scale_pool[:ROW0, :].bitcast(I32), 0)
 
-        def load_scales(pool, scales):
-            for r in range(4):
-                nc.sync.dma_start(pool[r:P:32, :].bitcast(I32), scales[0, r:16:4, :].bitcast(I32))
-
+        nc.sync.dma_start(evicted_list[:], offs2)
+        nc.scalar.dma_start(ekey_scale_pool[ROW0:, :].bitcast(I32), ekey_scales[0].bitcast(I32))
         nc.sync.dma_start(keys_pool[:].bitcast(I32), keys_words[0].bitcast(I32))
         nc.sync.dma_start(kept_list[:], offs)
-        nc.sync.dma_start(evicted_list[:], offs2)
-        load_scales(ekey_scale_pool, ekey_scales)
+        nc.scalar.dma_start(keys_scale_pool[ROW0:, :].bitcast(I32), keys_scales[0].bitcast(I32))
+        nc.scalar.dma_start(fac_sb[:], fac.rearrange("(p t) o -> p (t o)", t=PACK))
         nc.sync.dma_start(ekey_pool[:].bitcast(I32), ekey_words[0].rearrange("p n t -> p (n t)").bitcast(I32))
-        load_scales(keys_scale_pool, keys_scales)
-        for b in range(blocks):
-            nc.sync.dma_start(evals_pool[b][:], evals[b * P : (b + 1) * P, :])
-            if b % 2 == 0:
-                nc.sync.dma_start(fac_sb[b // 2][:], fac.rearrange("(p t) o -> p (t o)", t=PACK)[:, b : b + 2])
-        for b in range(blocks):
-            nc.sync.dma_start(vals_pool[b][:], vals[b * P : (b + 1) * P, :])
+        nc.sync.dma_start(evals_pool[0][:], evals[0:P, :])
 
         ident = sb([P, P], F32, "ident")
         make_identity(nc, ident[:])
         minus_one = sb([P, 2], F32, "minus_one")
         nc.gpsimd.memset(minus_one[:], -1.0)
 
-        keys_g = sb([P, I], U16, "keys_g")
-        keys_scale_g = sb([P, I], U8, "keys_scale_g")
-        ekey_g = sb([P, J], U32, "ekey_g")
-        ekey_scale_g = sb([P, J], U8, "ekey_scale_g")
-        nc.vector.tensor_copy(keys_g[:], keys_pool[:].indirect(kept_list[:]))
+        keys_g = sb([P, I], U16, "keys_g", at=77 * KIB + 128)
+        keys_scale_g = sb([P, I], U8, "keys_scale_g", at=kscg_at)
+        ekey_g = sb([P, J], U32, "ekey_g", at=78 * KIB + 256)
+        ekey_scale_g = sb([P, J], U8, "ekey_scale_g", at=78 * KIB)
+        planes = sb([P, J + I], U8, "planes", at=ksc_at)
         nc.vector.tensor_copy(ekey_scale_g[:], ekey_scale_pool[:].indirect(evicted_list[:]))
-        ekey_scale_d = sb([P, J], U8, "ekey_scale_d")
-        nc.vector.tensor_copy(
-            ekey_scale_d[:].rearrange("p (r s) -> p r s", r=PACK), ekey_scale_g[:].rearrange("p (s r) -> p r s", r=PACK)
-        )
-        nc.vector.tensor_copy(ekey_g[:].rearrange("p (r s) -> p s r", r=PACK), ekey_pool[:].indirect(evicted_list[:]))
         nc.vector.tensor_copy(keys_scale_g[:], keys_scale_pool[:].indirect(kept_list[:]))
+        nc.vector.tensor_copy(
+            planes[:, :J].rearrange("p (r s) -> p r s", r=PACK), ekey_scale_g[:].rearrange("p (s r) -> p r s", r=PACK)
+        )
+        nc.vector.tensor_copy(planes[:, J:].bitcast(I32), keys_scale_g[:].bitcast(I32))
+        for r in range(4):
+            nc.sync.dma_start(planes[r:P:32, :].bitcast(I32), planes[ROW0 + r : P : 4, :].bitcast(I32))
+        nc.vector.tensor_copy(keys_g[:], keys_pool[:].indirect(kept_list[:]))
+        nc.vector.tensor_copy(ekey_g[:].rearrange("p (r s) -> p s r", r=PACK), ekey_pool[:].indirect(evicted_list[:]))
+        for b in range(1, blocks):
+            nc.sync.dma_start(evals_pool[b][:], evals[b * P : (b + 1) * P, :])
+        nc.sync.dma_start(vals_pool[0][:], vals[0:P, :])
 
         banks = [psum.tile([P, I], F32, name="score%d" % r) for r in range(PACK)]
         for r in range(PACK):
             cols = slice(r * P, (r + 1) * P)
             nc.tensor.matmul_mx(
-                out=banks[r][:], lhsT=ekey_g[:, cols].bitcast(FP8X4), lhsT_scale=ekey_scale_d[:, cols],
-                rhs=keys_g[:].bitcast(FP4X4), rhs_scale=keys_scale_g[:], start=True, stop=True,
+                out=banks[r][:], lhsT=ekey_g[:, cols].bitcast(FP8X4), lhsT_scale=planes[:, cols],
+                rhs=keys_g[:].bitcast(FP4X4), rhs_scale=planes[:, J:], start=True, stop=True,
             )
 
         def gather_evals(b, tag=None, at=None):
@@ -99,7 +110,7 @@ def tile_attend_softmerge_kernel(tc, ekey_words, ekey_scales, keys_words, keys_s
             return gathered
 
         def turn(h, gathered, rows):
-            turned = psum.tile([P, len(gathered), 2, P], F32, name="turned%d" % h)
+            turned = psum.tile([P, len(gathered), 2, P], F32, name="turned%d" % h, tag="score0" if h == 0 else "turned%d" % h)
             for c in range(len(gathered)):
                 words = gathered[c][:].bitcast(F32)
                 for u in range(2):
@@ -127,8 +138,10 @@ def tile_attend_softmerge_kernel(tc, ekey_words, ekey_scales, keys_words, keys_s
                 nc.vector.tensor_tensor(result[:], window, merged_sb[:, h * part : (h + 1) * part], ALU.add)
                 nc.sync.dma_start(out[b * P : (b + 1) * P, first : first + part], result[:])
 
-        evals_g0 = gather_evals(0)
-        neg_max = [sb([P, 1], F32, "neg_max%d" % r, at=r * KIB) for r in range(PACK)]
+        evals_g0 = gather_evals(0, at=keys_at + KIB)
+        for b in (1, 2):
+            nc.sync.dma_start(vals_pool[b][:], vals[b * P : (b + 1) * P, :])
+        neg_max = [sb([P, 1], F32, "neg_max%d" % r, at=stats_at + r * KIB) for r in range(PACK)]
         row_sum = [sb([P, 2], F32, "row_sum%d" % h) for h in range(2)]
         inv_sum = [sb([P, 2], F32, "inv_sum%d" % h, "inv_sum") for h in range(2)]
         row_factor = sb([P, 2], F32, "row_factor")
@@ -143,27 +156,28 @@ def tile_attend_softmerge_kernel(tc, ekey_words, ekey_scales, keys_words, keys_s
             nc.scalar.activation(
                 p_rows[r][:], banks[r][:], ACT.Exp, bias=neg_max[r][:], accum_out=row_sum[r // 2][:, r % 2 : r % 2 + 1]
             )
-        evals_g1 = gather_evals(1, at=0)
-        evals_g2 = gather_evals(2, at=KIB)
+        evals_g1 = gather_evals(1, at=stats_at)
+        nc.sync.dma_start(vals_pool[3][:], vals[3 * P :, :])
+        evals_g2 = gather_evals(2, at=stats_at + KIB)
         nc.gpsimd.tensor_tensor(inv_sum[0][:], row_sum[0][:], minus_one[:], ALU.pow)
-        nc.gpsimd.tensor_tensor(row_factor[:], inv_sum[0][:], fac_sb[0][:], ALU.mult)
+        nc.gpsimd.tensor_tensor(row_factor[:], inv_sum[0][:], fac_sb[:, 0:2], ALU.mult)
         nc.gpsimd.tensor_tensor(inv_sum[1][:], row_sum[1][:], minus_one[:], ALU.pow)
         for e in range(2):
             nc.scalar.activation(w_pairs[:, 0, :, e], p_rows[e][:], ACT.Copy, scale=row_factor[:, e : e + 1])
         for e in range(2):
             nc.vector.tensor_scalar(
-                w_pairs[:, 1, :, e], p_rows[2 + e][:], inv_sum[1][:, e : e + 1], fac_sb[1][:, e : e + 1], ALU.mult, ALU.mult
+                w_pairs[:, 1, :, e], p_rows[2 + e][:], inv_sum[1][:, e : e + 1], fac_sb[:, 2 + e : 3 + e], ALU.mult, ALU.mult
             )
-        vt_rows0 = sb([P, P * PACK], BF16, "vt_rows0", at=3 * KIB)
+        vt_rows0 = sb([P, P * PACK], BF16, "vt_rows0", at=stats_at + 3 * KIB)
         turn(0, [evals_g0], vt_rows0[:])
         vt_codes0 = sb([P, P], U32, "vt_codes0", tag="p_rows2")
         vt_scales0 = sb([P, P], U8, "vt_scales0")
         quantize(vt_codes0[:], vt_scales0[:], vt_rows0[:])
-        evals_g3 = gather_evals(3, at=3 * KIB)
+        evals_g3 = gather_evals(3, at=stats_at + 3 * KIB)
         vt_rows1 = sb([P, P * PACK], BF16, "vt_rows1", tag="p_rows0")
         turn(1, [evals_g1], vt_rows1[:])
-        vt_codes1 = sb([P, P], U32, "vt_codes1", at=16 * KIB)
-        w_codes = sb([P, I], U32, "w_codes", at=17 * KIB)
+        vt_codes1 = sb([P, P], U32, "vt_codes1", at=codes_at)
+        w_codes = sb([P, I], U32, "w_codes", at=codes_at + KIB)
         vt_scales1 = sb([P, P], U8, "vt_scales1")
         for h in range(2):
             nc.scalar.copy(w_woven[h][:].bitcast(F32), w_pairs[:, :, halves[h], :].bitcast(F32).rearrange("p u i o -> p i (u o)"))
@@ -176,8 +190,8 @@ def tile_attend_softmerge_kernel(tc, ekey_words, ekey_scales, keys_words, keys_s
         vt_codes23 = sb([P, 2 * P], U32, "vt_codes23", tag="w_woven0")
         vt_scales23 = sb([P, 2 * P], U8, "vt_scales23")
         quantize(vt_codes23[:], vt_scales23[:], vt_rows23[:])
-        finish(0, vt_codes0[:], vt_scales0[:], halves[0], "score0")
-        finish(0, vt_codes0[:], vt_scales0[:], halves[1], "turned0")
+        finish(0, vt_codes0[:], vt_scales0[:], halves[0], "merged0")
+        finish(0, vt_codes0[:], vt_scales0[:], halves[1], "score0")
         finish(1, vt_codes1[:], vt_scales1[:], slice(0, I), "score1")
         finish(2, vt_codes23[:, :P], vt_scales23[:, :P], slice(0, I), "score2")
         finish(3, vt_codes23[:, P:], vt_scales23[:, P:], slice(0, I), "score3")

@@ -52,7 +52,7 @@ def tile_attend_softmerge_kernel(tc, ekey_words, ekey_scales, keys_words, keys_s
         ekey_pool = sb([P, T], U32, "ekey_pool", at=ekey_at)
         keys_scale_pool = sb([P, T], U8, "keys_scale_pool", at=ksc_at)
         ekey_scale_pool = sb([P, T], U8, "ekey_scale_pool")
-        fac_sb = sb([P, PACK], F32, "fac_sb")
+        fac_sb = sb([P, PACK], F32, "fac_sb", at=keys_at + 3 * KIB)
         evals_at = [ev0_at, below(kscg_at), above(kscg_at, I), below(ekey_at)]
         vals_at = [above(ekey_at, 8 * KIB), below(ev0_at), above(ev0_at, 8 * KIB), evals_at[1]]
         evals_pool = [sb([P, T], F32, "evals_pool%d" % b, at=evals_at[b]) for b in range(blocks)]
@@ -63,12 +63,14 @@ def tile_attend_softmerge_kernel(tc, ekey_words, ekey_scales, keys_words, keys_s
         nc.gpsimd.memset(ekey_scale_pool[:ROW0, :].bitcast(I32), 0)
         nc.vector.memset(keys_scale_pool[:ROW0, :].bitcast(I32), 0)
 
+        fac_row = sb([P, J], F32, "fac_row")
+        nc.vector.memset(fac_row[: P - 1, :], 0.0)
         nc.sync.dma_start(evicted_list[:], offs2)
         nc.scalar.dma_start(ekey_scale_pool[ROW0:, :].bitcast(I32), ekey_scales[0].bitcast(I32))
-        nc.sync.dma_start(keys_pool[:].bitcast(I32), keys_words[0].bitcast(I32))
         nc.sync.dma_start(kept_list[:], offs)
         nc.scalar.dma_start(keys_scale_pool[ROW0:, :].bitcast(I32), keys_scales[0].bitcast(I32))
-        nc.scalar.dma_start(fac_sb[:], fac.rearrange("(p t) o -> p (t o)", t=PACK))
+        nc.sync.dma_start(keys_pool[:].bitcast(I32), keys_words[0].bitcast(I32))
+        nc.scalar.dma_start(fac_row[P - 1 :, :], fac.rearrange("j o -> o j"))
         nc.sync.dma_start(ekey_pool[:].bitcast(I32), ekey_words[0].rearrange("p n t -> p (n t)").bitcast(I32))
         nc.sync.dma_start(evals_pool[0][:], evals[0:P, :])
 
@@ -76,6 +78,10 @@ def tile_attend_softmerge_kernel(tc, ekey_words, ekey_scales, keys_words, keys_s
         make_identity(nc, ident[:])
         minus_one = sb([P, 2], F32, "minus_one")
         nc.gpsimd.memset(minus_one[:], -1.0)
+
+        fac_turned = psum.tile([P, PACK, P], F32, name="fac_turned", tag="merged0")
+        for t in range(PACK):
+            nc.tensor.transpose(fac_turned[:, t, :], fac_row[:, t:J:PACK], ident[:])
 
         keys_g = sb([P, I], U16, "keys_g", at=77 * KIB + 128)
         keys_scale_g = sb([P, I], U8, "keys_scale_g", at=kscg_at)
@@ -92,6 +98,7 @@ def tile_attend_softmerge_kernel(tc, ekey_words, ekey_scales, keys_words, keys_s
             nc.sync.dma_start(planes[r:P:32, :].bitcast(I32), planes[ROW0 + r : P : 4, :].bitcast(I32))
         nc.vector.tensor_copy(keys_g[:], keys_pool[:].indirect(kept_list[:]))
         nc.vector.tensor_copy(ekey_g[:].rearrange("p (r s) -> p s r", r=PACK), ekey_pool[:].indirect(evicted_list[:]))
+        nc.vector.tensor_copy(fac_sb[:], fac_turned[:, :, P - 1])
         for b in range(1, blocks):
             nc.sync.dma_start(evals_pool[b][:], evals[b * P : (b + 1) * P, :])
         nc.sync.dma_start(vals_pool[0][:], vals[0:P, :])
@@ -129,13 +136,12 @@ def tile_attend_softmerge_kernel(tc, ekey_words, ekey_scales, keys_words, keys_s
             )
             merged_sb = sb([P, width], F32, "merged_sb%d_%d" % (b, cols.start))
             nc.scalar.copy(merged_sb[:], merged[:])
-            pieces = 2 if b == blocks - 1 else 1
-            part = width // pieces
-            for h in range(pieces):
-                first = cols.start + h * part
+            cuts = [0, 256, 384, 512] if b == blocks - 1 else [0, width]
+            for lo, hi in zip(cuts, cuts[1:]):
+                first, part = cols.start + lo, hi - lo
                 result = sb([P, part], F32, "result%d_%d" % (b, first))
                 window = vals_pool[b][:].indirect(kept_list[:, first // 16 : (first + part) // 16])
-                nc.vector.tensor_tensor(result[:], window, merged_sb[:, h * part : (h + 1) * part], ALU.add)
+                nc.vector.tensor_tensor(result[:], window, merged_sb[:, lo:hi], ALU.add)
                 nc.sync.dma_start(out[b * P : (b + 1) * P, first : first + part], result[:])
 
         evals_g0 = gather_evals(0, at=keys_at + KIB)

@@ -21,12 +21,18 @@ AXIS = mybir.AxisListType
 P = 128
 PACK = 4
 KIB = 1024
-ROW0 = P - 16
+SCALE_ROWS = 16
+ROW0 = P - SCALE_ROWS
+OVERLAP = 128
+TABLE_BYTES = T * 4
+TAIL_CUTS = [0, 256, 384, 512]
 
 
 def tile_attend_softmerge_kernel(tc, ekey_words, ekey_scales, keys_words, keys_scales, fac, evals, vals, offs, offs2, out):
     nc = tc.nc
-    blocks = E // P
+    evals_rows = evals.rearrange("(p t) n -> p t n", t=PACK)
+    vals_rows = vals.rearrange("(p t) n -> p t n", t=PACK)
+    out_rows = out.rearrange("(p t) n -> p t n", t=PACK)
 
     with ExitStack() as ctx:
         keep = ctx.enter_context(tc.tile_pool(name="keep", bufs=1))
@@ -38,166 +44,184 @@ def tile_attend_softmerge_kernel(tc, ekey_words, ekey_scales, keys_words, keys_s
                 return placed.tile(shape, dtype, name=name, align_bytes=64, offset=at)
             return keep.tile(shape, dtype, name=name, tag=tag or name, align_bytes=64)
 
-        kept_list = sb([P, I // 16], U16, "kept_list")
-        evicted_list = sb([P, J // 16], U16, "evicted_list")
-        ev0_at, kscg_at, ekey_at, ksc_at, keys_at = 8 * KIB, 32 * KIB, 52 * KIB, 68 * KIB, 72 * KIB
-
         def below(at):
-            return at + 128 - 8 * KIB
+            return at + OVERLAP - TABLE_BYTES
 
         def above(at, size):
-            return at + size - 128
+            return at + size - OVERLAP
 
-        keys_pool = sb([P, T], U16, "keys_pool", at=keys_at)
-        ekey_pool = sb([P, T], U32, "ekey_pool", at=ekey_at)
-        keys_scale_pool = sb([P, T], U8, "keys_scale_pool", at=ksc_at)
-        ekey_scale_pool = sb([P, T], U8, "ekey_scale_pool")
-        fac_sb = sb([P, PACK], F32, "fac_sb", at=keys_at + 3 * KIB)
-        evals_at = [ev0_at, below(kscg_at), above(kscg_at, I), below(ekey_at)]
-        vals_at = [above(ekey_at, 8 * KIB), below(ev0_at), above(ev0_at, 8 * KIB), evals_at[1]]
-        evals_pool = [sb([P, T], F32, "evals_pool%d" % b, at=evals_at[b]) for b in range(blocks)]
-        vals_pool = [sb([P, T], F32, "vals_pool%d" % b, at=vals_at[b]) for b in range(blocks)]
-        stats_at = ev0_at + KIB
-        codes_at = evals_at[3] + KIB // 2
+        evals0_at, keys_scale_g_at, keys_at, ekey_at, keys_scale_at, ekey_scale_g_at = (k * KIB for k in (8, 32, 50, 56, 72, 78))
+        evals_at = [evals0_at, below(keys_scale_g_at), above(keys_scale_g_at, I), below(keys_at)]
+        vals_at = [above(ekey_at, TABLE_BYTES), below(evals0_at), above(evals0_at, TABLE_BYTES), evals_at[1]]
+        stats_at = ekey_at + KIB
 
-        nc.gpsimd.memset(ekey_scale_pool[:ROW0, :].bitcast(I32), 0)
-        nc.vector.memset(keys_scale_pool[:ROW0, :].bitcast(I32), 0)
-
+        kept_list = sb([P, I // 16], U16, "kept_list")
+        evicted_list = sb([P, J // 16], U16, "evicted_list")
+        keys_table = sb([P, T], U16, "keys_table", at=keys_at)
+        ekey_table = sb([P, T], U32, "ekey_table", at=ekey_at)
+        keys_scale_table = sb([P, T], U8, "keys_scale_table", at=keys_scale_at)
+        ekey_scale_table = sb([P, T], U8, "ekey_scale_table")
+        evals_table = [sb([P, T], F32, "evals_table%d" % b, at=evals_at[b]) for b in range(PACK)]
+        vals_table = [sb([P, T], F32, "vals_table%d" % b, at=vals_at[b]) for b in range(PACK)]
         fac_row = sb([P, J], F32, "fac_row")
+
+        def load_evals(b):
+            nc.sync.dma_start(evals_table[b][:], evals_rows[:, b, :])
+
+        def load_vals(b):
+            nc.sync.dma_start(vals_table[b][:], vals_rows[:, b, :])
+
+        nc.gpsimd.memset(ekey_scale_table[:ROW0, :].bitcast(I32), 0)
+        nc.vector.memset(keys_scale_table[:ROW0, :].bitcast(I32), 0)
         nc.vector.memset(fac_row[: P - 1, :], 0.0)
         nc.sync.dma_start(evicted_list[:], offs2)
-        nc.scalar.dma_start(ekey_scale_pool[ROW0:, :].bitcast(I32), ekey_scales[0].bitcast(I32))
+        nc.scalar.dma_start(ekey_scale_table[ROW0:, :].bitcast(I32), ekey_scales[0].bitcast(I32))
         nc.sync.dma_start(kept_list[:], offs)
-        nc.scalar.dma_start(keys_scale_pool[ROW0:, :].bitcast(I32), keys_scales[0].bitcast(I32))
-        nc.sync.dma_start(keys_pool[:].bitcast(I32), keys_words[0].bitcast(I32))
+        nc.scalar.dma_start(keys_scale_table[ROW0:, :].bitcast(I32), keys_scales[0].bitcast(I32))
+        nc.sync.dma_start(keys_table[:].bitcast(I32), keys_words[0].bitcast(I32))
         nc.scalar.dma_start(fac_row[P - 1 :, :], fac.rearrange("j o -> o j"))
-        nc.sync.dma_start(ekey_pool[:].bitcast(I32), ekey_words[0].rearrange("p n t -> p (n t)").bitcast(I32))
-        nc.sync.dma_start(evals_pool[0][:], evals[0:P, :])
+        nc.sync.dma_start(ekey_table[:].bitcast(I32), ekey_words[0].rearrange("p n t -> p (n t)").bitcast(I32))
+        load_evals(0)
 
         ident = sb([P, P], F32, "ident")
         make_identity(nc, ident[:])
-        minus_one = sb([P, 2], F32, "minus_one")
-        nc.gpsimd.memset(minus_one[:], -1.0)
-
-        fac_turned = psum.tile([P, PACK, P], F32, name="fac_turned", tag="merged0")
+        fac_turned = psum.tile([P, PACK, P], F32, name="fac_turned", tag="spare")
         for t in range(PACK):
             nc.tensor.transpose(fac_turned[:, t, :], fac_row[:, t:J:PACK], ident[:])
 
-        keys_g = sb([P, I], U16, "keys_g", at=77 * KIB + 128)
-        keys_scale_g = sb([P, I], U8, "keys_scale_g", at=kscg_at)
-        ekey_g = sb([P, J], U32, "ekey_g", at=78 * KIB + 256)
-        ekey_scale_g = sb([P, J], U8, "ekey_scale_g", at=78 * KIB)
-        planes = sb([P, J + I], U8, "planes", at=ksc_at)
-        nc.vector.tensor_copy(ekey_scale_g[:], ekey_scale_pool[:].indirect(evicted_list[:]))
-        nc.vector.tensor_copy(keys_scale_g[:], keys_scale_pool[:].indirect(kept_list[:]))
+        ekey_scale_g = sb([P, J], U8, "ekey_scale_g", at=ekey_scale_g_at)
+        keys_scale_g = sb([P, I], U8, "keys_scale_g", at=keys_scale_g_at)
+        planes = sb([P, J + I], U8, "planes", at=keys_scale_at)
+        nc.vector.tensor_copy(ekey_scale_g[:], ekey_scale_table[:].indirect(evicted_list[:]))
+        nc.vector.tensor_copy(keys_scale_g[:], keys_scale_table[:].indirect(kept_list[:]))
         nc.vector.tensor_copy(
             planes[:, :J].rearrange("p (r s) -> p r s", r=PACK), ekey_scale_g[:].rearrange("p (s r) -> p r s", r=PACK)
         )
         nc.vector.tensor_copy(planes[:, J:].bitcast(I32), keys_scale_g[:].bitcast(I32))
         for r in range(4):
             nc.sync.dma_start(planes[r:P:32, :].bitcast(I32), planes[ROW0 + r : P : 4, :].bitcast(I32))
-        nc.vector.tensor_copy(keys_g[:], keys_pool[:].indirect(kept_list[:]))
-        nc.vector.tensor_copy(ekey_g[:].rearrange("p (r s) -> p s r", r=PACK), ekey_pool[:].indirect(evicted_list[:]))
+        keys_g = sb([P, I], U16, "keys_g", at=ekey_scale_g_at + OVERLAP - 2 * I)
+        ekey_g = sb([P, J], U32, "ekey_g", at=ekey_scale_g_at + 2 * OVERLAP)
+        nc.vector.tensor_copy(keys_g[:], keys_table[:].indirect(kept_list[:]))
+        nc.vector.tensor_copy(ekey_g[:].rearrange("p (r s) -> p s r", r=PACK), ekey_table[:].indirect(evicted_list[:]))
+        fac_sb = sb([P, PACK], F32, "fac_sb", at=keys_at + 3 * KIB)
         nc.vector.tensor_copy(fac_sb[:], fac_turned[:, :, P - 1])
-        for b in range(1, blocks):
-            nc.sync.dma_start(evals_pool[b][:], evals[b * P : (b + 1) * P, :])
-        nc.sync.dma_start(vals_pool[0][:], vals[0:P, :])
+        for b in range(1, PACK):
+            load_evals(b)
+        load_vals(0)
 
-        banks = [psum.tile([P, I], F32, name="score%d" % r) for r in range(PACK)]
+        scores = [psum.tile([P, I], F32, name="score%d" % r) for r in range(PACK)]
         for r in range(PACK):
             cols = slice(r * P, (r + 1) * P)
             nc.tensor.matmul_mx(
-                out=banks[r][:], lhsT=ekey_g[:, cols].bitcast(FP8X4), lhsT_scale=planes[:, cols],
+                out=scores[r][:], lhsT=ekey_g[:, cols].bitcast(FP8X4), lhsT_scale=planes[:, cols],
                 rhs=keys_g[:].bitcast(FP4X4), rhs_scale=planes[:, J:], start=True, stop=True,
             )
 
         def gather_evals(b, tag=None, at=None):
             gathered = sb([P, J], BF16, "evals_g%d" % b, tag, at)
-            nc.vector.tensor_copy(gathered[:], evals_pool[b][:].indirect(evicted_list[:]))
+            nc.vector.tensor_copy(gathered[:], evals_table[b][:].indirect(evicted_list[:]))
             return gathered
 
-        def turn(h, gathered, rows):
-            turned = psum.tile([P, len(gathered), 2, P], F32, name="turned%d" % h, tag="score0" if h == 0 else "turned%d" % h)
-            for c in range(len(gathered)):
-                words = gathered[c][:].bitcast(F32)
-                for u in range(2):
-                    nc.tensor.transpose(turned[:, c, u, :], words[:, u : J // 2 : 2], ident[:])
-            nc.scalar.copy(rows.bitcast(F32).rearrange("p (c e u) -> p c e u", e=P, u=2), turned[:].rearrange("p c u e -> p c e u"))
+        def turn(b, gathered, bank, tag=None, at=None):
+            turned = psum.tile([P, 2, P], F32, name="turned%d" % b, tag=bank)
+            words = gathered[:].bitcast(F32)
+            for u in range(2):
+                nc.tensor.transpose(turned[:, u, :], words[:, u : J // 2 : 2], ident[:])
+            rows = sb([P, P * PACK], BF16, "vt_rows%d" % b, tag, at)
+            nc.scalar.copy(rows[:].bitcast(F32).rearrange("p (e u) -> p e u", u=2), turned[:].rearrange("p u e -> p e u"))
+            return rows
 
-        def quantize(codes, scales, rows):
-            nc.vector.quantize_mx(out=codes.bitcast(FP8X4), scales=scales, in_=rows)
+        def quantize_vt(b, rows, tag=None, at=None):
+            codes = sb([P, P], U32, "vt_codes%d" % b, tag, at)
+            scales = sb([P, P], U8, "vt_scales%d" % b)
+            nc.vector.quantize_mx(out=codes[:].bitcast(FP8X4), scales=scales[:], in_=rows[:])
+            return codes, scales
 
-        def finish(b, codes, scales, cols, bank):
+        def merge(b, vt, cols, bank):
             width = cols.stop - cols.start
             merged = psum.tile([P, width], F32, name="merged%d_%d" % (b, cols.start), tag=bank)
             nc.tensor.matmul_mx(
-                out=merged[:], lhsT=codes.bitcast(FP8X4), lhsT_scale=scales,
+                out=merged[:], lhsT=vt[0][:].bitcast(FP8X4), lhsT_scale=vt[1][:],
                 rhs=w_codes[:, cols].bitcast(FP8X4), rhs_scale=w_scales[:, cols], start=True, stop=True,
             )
             merged_sb = sb([P, width], F32, "merged_sb%d_%d" % (b, cols.start))
             nc.scalar.copy(merged_sb[:], merged[:])
-            cuts = [0, 256, 384, 512] if b == blocks - 1 else [0, width]
-            for lo, hi in zip(cuts, cuts[1:]):
-                first, part = cols.start + lo, hi - lo
-                result = sb([P, part], F32, "result%d_%d" % (b, first))
-                window = vals_pool[b][:].indirect(kept_list[:, first // 16 : (first + part) // 16])
-                nc.vector.tensor_tensor(result[:], window, merged_sb[:, lo:hi], ALU.add)
-                nc.sync.dma_start(out[b * P : (b + 1) * P, first : first + part], result[:])
+            return merged_sb
+
+        def add_vals(b, result, merged_part, cols):
+            window = vals_table[b][:].indirect(kept_list[:, cols.start // 16 : cols.stop // 16])
+            nc.vector.tensor_tensor(result, window, merged_part, ALU.add)
 
         evals_g0 = gather_evals(0, at=keys_at + KIB)
-        for b in (1, 2):
-            nc.sync.dma_start(vals_pool[b][:], vals[b * P : (b + 1) * P, :])
+        load_vals(1)
+        load_vals(2)
+
         neg_max = [sb([P, 1], F32, "neg_max%d" % r, at=stats_at + r * KIB) for r in range(PACK)]
-        row_sum = [sb([P, 2], F32, "row_sum%d" % h) for h in range(2)]
-        inv_sum = [sb([P, 2], F32, "inv_sum%d" % h, "inv_sum") for h in range(2)]
+        row_sum = [sb([P, 2], F32, "row_sum0"), sb([P, 2], F32, "row_sum1", at=stats_at + 5 * KIB)]
+        inv_sum = [sb([P, 2], F32, "inv_sum%d" % h) for h in range(2)]
         row_factor = sb([P, 2], F32, "row_factor")
         p_rows = [sb([P, I], F32, "p_rows%d" % r) for r in range(PACK)]
         w_pairs = sb([P, 2, I, 2], BF16, "w_pairs")
         w_woven = [sb([P, I // 2, PACK], BF16, "w_woven%d" % h) for h in range(2)]
+        w_codes = sb([P, I], U32, "w_codes")
         w_scales = sb([P, I], U8, "w_scales")
         halves = [slice(0, I // 2), slice(I // 2, I)]
+        whole = slice(0, I)
 
         for r in range(PACK):
-            nc.vector.tensor_reduce(neg_max[r][:], banks[r][:], AXIS.X, ALU.max, negate=True)
+            nc.vector.tensor_reduce(neg_max[r][:], scores[r][:], AXIS.X, ALU.max, negate=True)
             nc.scalar.activation(
-                p_rows[r][:], banks[r][:], ACT.Exp, bias=neg_max[r][:], accum_out=row_sum[r // 2][:, r % 2 : r % 2 + 1]
+                p_rows[r][:], scores[r][:], ACT.Exp, bias=neg_max[r][:], accum_out=row_sum[r // 2][:, r % 2 : r % 2 + 1]
             )
-        evals_g1 = gather_evals(1, at=stats_at)
-        nc.sync.dma_start(vals_pool[3][:], vals[3 * P :, :])
-        evals_g2 = gather_evals(2, at=stats_at + KIB)
-        nc.gpsimd.tensor_tensor(inv_sum[0][:], row_sum[0][:], minus_one[:], ALU.pow)
-        nc.gpsimd.tensor_tensor(row_factor[:], inv_sum[0][:], fac_sb[:, 0:2], ALU.mult)
-        nc.gpsimd.tensor_tensor(inv_sum[1][:], row_sum[1][:], minus_one[:], ALU.pow)
-        for e in range(2):
+        nc.vector.reciprocal(inv_sum[0][:], row_sum[0][:])
+        evals_g1 = gather_evals(1, at=stats_at + KIB)
+        load_vals(3)
+        nc.vector.reciprocal(inv_sum[1][:], row_sum[1][:])
+        nc.vector.tensor_tensor(row_factor[:], inv_sum[0][:], fac_sb[:, 0:2], ALU.mult)
+
+        def product_scalar(e):
             nc.scalar.activation(w_pairs[:, 0, :, e], p_rows[e][:], ACT.Copy, scale=row_factor[:, e : e + 1])
-        for e in range(2):
+
+        def product_vector(e):
             nc.vector.tensor_scalar(
                 w_pairs[:, 1, :, e], p_rows[2 + e][:], inv_sum[1][:, e : e + 1], fac_sb[:, 2 + e : 3 + e], ALU.mult, ALU.mult
             )
-        vt_rows0 = sb([P, P * PACK], BF16, "vt_rows0", at=stats_at + 3 * KIB)
-        turn(0, [evals_g0], vt_rows0[:])
-        vt_codes0 = sb([P, P], U32, "vt_codes0", tag="p_rows2")
-        vt_scales0 = sb([P, P], U8, "vt_scales0")
-        quantize(vt_codes0[:], vt_scales0[:], vt_rows0[:])
-        evals_g3 = gather_evals(3, at=stats_at + 3 * KIB)
-        vt_rows1 = sb([P, P * PACK], BF16, "vt_rows1", tag="p_rows0")
-        turn(1, [evals_g1], vt_rows1[:])
-        vt_codes1 = sb([P, P], U32, "vt_codes1", at=codes_at)
-        w_codes = sb([P, I], U32, "w_codes", at=codes_at + KIB)
-        vt_scales1 = sb([P, P], U8, "vt_scales1")
-        for h in range(2):
-            nc.scalar.copy(w_woven[h][:].bitcast(F32), w_pairs[:, :, halves[h], :].bitcast(F32).rearrange("p u i o -> p i (u o)"))
-            quantize(w_codes[:, halves[h]], w_scales[:, halves[h]], w_woven[h][:].rearrange("p i t -> p (i t)"))
-        quantize(vt_codes1[:], vt_scales1[:], vt_rows1[:])
 
-        vt_rows23 = sb([P, 2 * P * PACK], BF16, "vt_rows23", tag="w_pairs")
-        turn(2, [evals_g2], vt_rows23[:, : P * PACK])
-        turn(3, [evals_g3], vt_rows23[:, P * PACK :])
-        vt_codes23 = sb([P, 2 * P], U32, "vt_codes23", tag="w_woven0")
-        vt_scales23 = sb([P, 2 * P], U8, "vt_scales23")
-        quantize(vt_codes23[:], vt_scales23[:], vt_rows23[:])
-        finish(0, vt_codes0[:], vt_scales0[:], halves[0], "merged0")
-        finish(0, vt_codes0[:], vt_scales0[:], halves[1], "score0")
-        finish(1, vt_codes1[:], vt_scales1[:], slice(0, I), "score1")
-        finish(2, vt_codes23[:, :P], vt_scales23[:, :P], slice(0, I), "score2")
-        finish(3, vt_codes23[:, P:], vt_scales23[:, P:], slice(0, I), "score3")
+        vt_rows0 = turn(0, evals_g0, "score0", at=stats_at + 2 * KIB)
+        product_scalar(0)
+        product_vector(0)
+        vt0 = quantize_vt(0, vt_rows0, at=stats_at + 5 * KIB)
+        vt_rows1 = turn(1, evals_g1, "turned1", tag="p_rows0")
+        product_scalar(1)
+        product_vector(1)
+        evals_g2 = gather_evals(2, at=stats_at + 2 * KIB)
+
+        def weave(h):
+            nc.scalar.copy(w_woven[h][:].bitcast(F32), w_pairs[:, :, halves[h], :].bitcast(F32).rearrange("p u i o -> p i (u o)"))
+            nc.vector.quantize_mx(
+                out=w_codes[:, halves[h]].bitcast(FP8X4), scales=w_scales[:, halves[h]], in_=w_woven[h][:].rearrange("p i t -> p (i t)")
+            )
+
+        weave(0)
+        vt1 = quantize_vt(1, vt_rows1, tag="p_rows3")
+        weave(1)
+        evals_g3 = gather_evals(3, tag="w_woven0")
+        vt_rows2 = turn(2, evals_g2, "turned2", tag="w_pairs")
+        vt2 = quantize_vt(2, vt_rows2, tag="w_woven1")
+
+        result01 = sb([P, 2, I], F32, "result01", at=evals_at[3] + KIB)
+        for h, bank in enumerate(("spare", "score0")):
+            add_vals(0, result01[:, 0, halves[h]], merge(0, vt0, halves[h], bank)[:], halves[h])
+        merged1 = merge(1, vt1, whole, "score1")
+        vt3 = quantize_vt(3, turn(3, evals_g3, "score0"), tag="merged_sb0_0")
+        add_vals(1, result01[:, 1, :], merged1[:], whole)
+        nc.sync.dma_start(out_rows[:, 0:2, :], result01[:])
+        result2 = sb([P, I], F32, "result2")
+        add_vals(2, result2[:], merge(2, vt2, whole, "score2")[:], whole)
+        nc.sync.dma_start(out_rows[:, 2, :], result2[:])
+        merged3 = merge(3, vt3, whole, "score3")
+        for lo, hi in zip(TAIL_CUTS, TAIL_CUTS[1:]):
+            piece = sb([P, hi - lo], F32, "result3_%d" % lo)
+            add_vals(3, piece[:], merged3[:, lo:hi], slice(lo, hi))
+            nc.sync.dma_start(out_rows[:, 3, lo:hi], piece[:])

@@ -30,9 +30,9 @@ TAIL_CUTS = [0, 256, 384, 512]
 
 def tile_attend_softmerge_kernel(tc, ekey_words, ekey_scales, keys_words, keys_scales, fac, evals, vals, offs, offs2, out):
     nc = tc.nc
-    evals_rows = evals.rearrange("(p t) n -> p t n", t=PACK)
-    vals_rows = vals.rearrange("(p t) n -> p t n", t=PACK)
-    out_rows = out.rearrange("(p t) n -> p t n", t=PACK)
+    evals_rows = evals.rearrange("(t p) n -> p t n", t=PACK)
+    vals_rows = vals.rearrange("(t p) n -> p t n", t=PACK)
+    out_rows = out.rearrange("(t p) n -> p t n", t=PACK)
 
     with ExitStack() as ctx:
         keep = ctx.enter_context(tc.tile_pool(name="keep", bufs=1))
@@ -138,14 +138,14 @@ def tile_attend_softmerge_kernel(tc, ekey_words, ekey_scales, keys_words, keys_s
             nc.vector.quantize_mx(out=codes[:].bitcast(FP8X4), scales=scales[:], in_=rows[:])
             return codes, scales
 
-        def merge(b, vt, cols, bank):
+        def merge(b, vt, cols, bank, tag=None):
             width = cols.stop - cols.start
             merged = psum.tile([P, width], F32, name="merged%d_%d" % (b, cols.start), tag=bank)
             nc.tensor.matmul_mx(
                 out=merged[:], lhsT=vt[0][:].bitcast(FP8X4), lhsT_scale=vt[1][:],
                 rhs=w_codes[:, cols].bitcast(FP8X4), rhs_scale=w_scales[:, cols], start=True, stop=True,
             )
-            merged_sb = sb([P, width], F32, "merged_sb%d_%d" % (b, cols.start))
+            merged_sb = sb([P, width], F32, "merged_sb%d_%d" % (b, cols.start), tag)
             nc.scalar.copy(merged_sb[:], merged[:])
             return merged_sb
 
@@ -213,12 +213,12 @@ def tile_attend_softmerge_kernel(tc, ekey_words, ekey_scales, keys_words, keys_s
         result01 = sb([P, 2, I], F32, "result01", at=evals_at[3] + KIB)
         for h, bank in enumerate(("spare", "score0")):
             add_vals(0, result01[:, 0, halves[h]], merge(0, vt0, halves[h], bank)[:], halves[h])
+        vt3 = quantize_vt(3, turn(3, evals_g3, "turned3", at=stats_at + 5 * KIB), tag="merged_sb0_0")
         merged1 = merge(1, vt1, whole, "score1")
-        vt3 = quantize_vt(3, turn(3, evals_g3, "score0"), tag="merged_sb0_0")
         add_vals(1, result01[:, 1, :], merged1[:], whole)
         nc.sync.dma_start(out_rows[:, 0:2, :], result01[:])
         result2 = sb([P, I], F32, "result2")
-        add_vals(2, result2[:], merge(2, vt2, whole, "score2")[:], whole)
+        add_vals(2, result2[:], merge(2, vt2, whole, "score2", tag="w_woven0")[:], whole)
         nc.sync.dma_start(out_rows[:, 2, :], result2[:])
         merged3 = merge(3, vt3, whole, "score3")
         for lo, hi in zip(TAIL_CUTS, TAIL_CUTS[1:]):

@@ -50,8 +50,8 @@ def tile_attend_softmerge_kernel(tc, ekey_words, ekey_scales, keys_words, keys_s
         def above(at, size):
             return at + size - OVERLAP
 
-        evals0_at, keys_scale_g_at, keys_at, ekey_at, keys_scale_at, ekey_scale_g_at = (k * KIB for k in (8, 32, 50, 56, 72, 78))
-        evals_at = [evals0_at, below(keys_scale_g_at), above(keys_scale_g_at, I), below(keys_at)]
+        evals0_at, keys_scale_g_at, keys_at, ekey_at, keys_scale_at, ekey_scale_g_at = (k * KIB for k in (8, 32, 42, 56, 72, 78))
+        evals_at = [evals0_at, below(keys_scale_g_at), below(keys_at), below(ekey_at)]
         vals_at = [above(ekey_at, TABLE_BYTES), below(evals0_at), above(evals0_at, TABLE_BYTES), evals_at[1]]
         stats_at = ekey_at + KIB
 
@@ -66,7 +66,8 @@ def tile_attend_softmerge_kernel(tc, ekey_words, ekey_scales, keys_words, keys_s
         fac_row = sb([P, J], F32, "fac_row")
 
         def load_evals(b):
-            nc.sync.dma_start(evals_table[b][:], evals_rows[:, b, :])
+            queue = nc.scalar if b == 2 else nc.sync
+            queue.dma_start(evals_table[b][:], evals_rows[:, b, :])
 
         def load_vals(b):
             nc.sync.dma_start(vals_table[b][:], vals_rows[:, b, :])
@@ -74,13 +75,13 @@ def tile_attend_softmerge_kernel(tc, ekey_words, ekey_scales, keys_words, keys_s
         nc.gpsimd.memset(ekey_scale_table[:ROW0, :].bitcast(I32), 0)
         nc.vector.memset(keys_scale_table[:ROW0, :].bitcast(I32), 0)
         nc.vector.memset(fac_row[: P - 1, :], 0.0)
-        nc.sync.dma_start(evicted_list[:], offs2)
-        nc.scalar.dma_start(ekey_scale_table[ROW0:, :].bitcast(I32), ekey_scales[0].bitcast(I32))
         nc.sync.dma_start(kept_list[:], offs)
+        nc.scalar.dma_start(ekey_scale_table[ROW0:, :].bitcast(I32), ekey_scales[0].bitcast(I32))
+        nc.sync.dma_start(evicted_list[:], offs2)
         nc.scalar.dma_start(keys_scale_table[ROW0:, :].bitcast(I32), keys_scales[0].bitcast(I32))
         nc.sync.dma_start(keys_table[:].bitcast(I32), keys_words[0].bitcast(I32))
-        nc.scalar.dma_start(fac_row[P - 1 :, :], fac.rearrange("j o -> o j"))
-        nc.sync.dma_start(ekey_table[:].bitcast(I32), ekey_words[0].rearrange("p n t -> p (n t)").bitcast(I32))
+        nc.scalar.dma_start(ekey_table[:].bitcast(I32), ekey_words[0].rearrange("p n t -> p (n t)").bitcast(I32))
+        nc.sync.dma_start(fac_row[P - 1 :, :], fac.rearrange("j o -> o j"))
         load_evals(0)
 
         ident = sb([P, P], F32, "ident")
@@ -91,7 +92,7 @@ def tile_attend_softmerge_kernel(tc, ekey_words, ekey_scales, keys_words, keys_s
 
         ekey_scale_g = sb([P, J], U8, "ekey_scale_g", at=ekey_scale_g_at)
         keys_scale_g = sb([P, I], U8, "keys_scale_g", at=keys_scale_g_at)
-        planes = sb([P, J + I], U8, "planes", at=keys_scale_at)
+        planes = sb([P, J + I], U8, "planes")
         nc.vector.tensor_copy(ekey_scale_g[:], ekey_scale_table[:].indirect(evicted_list[:]))
         nc.vector.tensor_copy(keys_scale_g[:], keys_scale_table[:].indirect(kept_list[:]))
         nc.vector.tensor_copy(

@@ -66,8 +66,7 @@ def tile_attend_softmerge_kernel(tc, ekey_words, ekey_scales, keys_words, keys_s
         fac_row = sb([P, J], F32, "fac_row")
 
         def load_evals(b):
-            queue = nc.scalar if b == 2 else nc.sync
-            queue.dma_start(evals_table[b][:], evals_rows[:, b, :])
+            nc.sync.dma_start(evals_table[b][:], evals_rows[:, b, :])
 
         def load_vals(b):
             nc.sync.dma_start(vals_table[b][:], vals_rows[:, b, :])

@@ -30,9 +30,9 @@ TAIL_CUTS = [0, 256, 384, 512]
 
 def tile_attend_softmerge_kernel(tc, ekey_words, ekey_scales, keys_words, keys_scales, fac, evals, vals, offs, offs2, out):
     nc = tc.nc
-    evals_rows = evals.rearrange("(t p) n -> p t n", t=PACK)
-    vals_rows = vals.rearrange("(t p) n -> p t n", t=PACK)
-    out_rows = out.rearrange("(t p) n -> p t n", t=PACK)
+    evals_rows = evals.rearrange("(h p u) n -> h p u n", h=2, u=2)
+    vals_rows = vals.rearrange("(h p u) n -> h p u n", h=2, u=2)
+    out_rows = out.rearrange("(h p u) n -> h p u n", h=2, u=2)
 
     with ExitStack() as ctx:
         keep = ctx.enter_context(tc.tile_pool(name="keep", bufs=1))
@@ -50,10 +50,12 @@ def tile_attend_softmerge_kernel(tc, ekey_words, ekey_scales, keys_words, keys_s
         def above(at, size):
             return at + size - OVERLAP
 
-        evals0_at, keys_scale_g_at, keys_at, ekey_at, keys_scale_at, ekey_scale_g_at = (k * KIB for k in (8, 32, 42, 56, 72, 78))
-        evals_at = [evals0_at, below(keys_scale_g_at), below(keys_at), below(ekey_at)]
-        vals_at = [above(ekey_at, TABLE_BYTES), below(evals0_at), above(evals0_at, TABLE_BYTES), evals_at[1]]
+        evals0_at, keys_scale_g_at, keys_at, ekey_at, keys_scale_at, ekey_scale_g_at = (k * KIB for k in (8, 32, 50, 64, 80, 86))
+        evals_at = [evals0_at, below(keys_scale_g_at)]
+        evals23_at = below(keys_at) - TABLE_BYTES
+        vals_at = [below(ekey_at), above(ekey_at, TABLE_BYTES), below(evals0_at), above(evals0_at, TABLE_BYTES)]
         stats_at = ekey_at + KIB
+        pairs_at = 96 * KIB
 
         kept_list = sb([P, I // 16], U16, "kept_list")
         evicted_list = sb([P, J // 16], U16, "evicted_list")
@@ -61,15 +63,16 @@ def tile_attend_softmerge_kernel(tc, ekey_words, ekey_scales, keys_words, keys_s
         ekey_table = sb([P, T], U32, "ekey_table", at=ekey_at)
         keys_scale_table = sb([P, T], U8, "keys_scale_table", at=keys_scale_at)
         ekey_scale_table = sb([P, T], U8, "ekey_scale_table")
-        evals_table = [sb([P, T], F32, "evals_table%d" % b, at=evals_at[b]) for b in range(PACK)]
+        evals_table = [sb([P, T], F32, "evals_table%d" % b, at=evals_at[b]) for b in range(2)]
+        evals23 = sb([P, 2, T], F32, "evals23", at=evals23_at)
         vals_table = [sb([P, T], F32, "vals_table%d" % b, at=vals_at[b]) for b in range(PACK)]
         fac_row = sb([P, J], F32, "fac_row")
 
         def load_evals(b):
-            nc.sync.dma_start(evals_table[b][:], evals_rows[:, b, :])
+            nc.sync.dma_start(evals_table[b][:], evals_rows[b // 2, :, b % 2, :])
 
         def load_vals(b):
-            nc.sync.dma_start(vals_table[b][:], vals_rows[:, b, :])
+            nc.sync.dma_start(vals_table[b][:], vals_rows[b // 2, :, b % 2, :])
 
         nc.gpsimd.memset(ekey_scale_table[:ROW0, :].bitcast(I32), 0)
         nc.vector.memset(keys_scale_table[:ROW0, :].bitcast(I32), 0)
@@ -106,9 +109,10 @@ def tile_attend_softmerge_kernel(tc, ekey_words, ekey_scales, keys_words, keys_s
         nc.vector.tensor_copy(ekey_g[:].rearrange("p (r s) -> p s r", r=PACK), ekey_table[:].indirect(evicted_list[:]))
         fac_sb = sb([P, PACK], F32, "fac_sb", at=keys_at + 3 * KIB)
         nc.vector.tensor_copy(fac_sb[:], fac_turned[:, :, P - 1])
-        for b in range(1, PACK):
-            load_evals(b)
+        load_evals(1)
+        nc.sync.dma_start(evals23[:], evals_rows[1])
         load_vals(0)
+        load_vals(1)
 
         scores = [psum.tile([P, I], F32, name="score%d" % r) for r in range(PACK)]
         for r in range(PACK):
@@ -128,6 +132,22 @@ def tile_attend_softmerge_kernel(tc, ekey_words, ekey_scales, keys_words, keys_s
             words = gathered[:].bitcast(F32)
             for u in range(2):
                 nc.tensor.transpose(turned[:, u, :], words[:, u : J // 2 : 2], ident[:])
+            rows = sb([P, P * PACK], BF16, "vt_rows%d" % b, tag, at)
+            nc.scalar.copy(rows[:].bitcast(F32).rearrange("p (e u) -> p e u", u=2), turned[:].rearrange("p u e -> p e u"))
+            return rows
+
+        def gather_dealt(b, tag=None, at=None):
+            gathered = sb([P, J], BF16, "evals_g%d" % b, tag, at)
+            nc.vector.tensor_copy(
+                gathered[:].rearrange("p (u s e) -> p s u e", u=2, e=2), evals23[:, b - 2, :].indirect(evicted_list[:])
+            )
+            return gathered
+
+        def turn_dealt(b, gathered, tag=None, at=None):
+            turned = psum.tile([P, 2, P], F32, name="turned%d" % b)
+            words = gathered[:].bitcast(F32)
+            for u in range(2):
+                nc.tensor.transpose(turned[:, u, :], words[:, u * P : (u + 1) * P], ident[:])
             rows = sb([P, P * PACK], BF16, "vt_rows%d" % b, tag, at)
             nc.scalar.copy(rows[:].bitcast(F32).rearrange("p (e u) -> p e u", u=2), turned[:].rearrange("p u e -> p e u"))
             return rows
@@ -154,17 +174,17 @@ def tile_attend_softmerge_kernel(tc, ekey_words, ekey_scales, keys_words, keys_s
             nc.vector.tensor_tensor(result, window, merged_part, ALU.add)
 
         evals_g0 = gather_evals(0, at=keys_at + KIB)
-        load_vals(1)
         load_vals(2)
+        load_vals(3)
 
         neg_max = [sb([P, 1], F32, "neg_max%d" % r, at=stats_at + r * KIB) for r in range(PACK)]
-        row_sum = [sb([P, 2], F32, "row_sum0"), sb([P, 2], F32, "row_sum1", at=stats_at + 5 * KIB)]
+        row_sum = [sb([P, 2], F32, "row_sum0", at=stats_at + 4 * KIB), sb([P, 2], F32, "row_sum1", at=stats_at + 5 * KIB)]
         inv_sum = [sb([P, 2], F32, "inv_sum%d" % h) for h in range(2)]
         row_factor = sb([P, 2], F32, "row_factor")
         p_rows = [sb([P, I], F32, "p_rows%d" % r) for r in range(PACK)]
-        w_pairs = sb([P, 2, I, 2], BF16, "w_pairs")
+        w_pairs = sb([P, 2, I, 2], BF16, "w_pairs", at=pairs_at)
         w_woven = [sb([P, I // 2, PACK], BF16, "w_woven%d" % h) for h in range(2)]
-        w_codes = sb([P, I], U32, "w_codes")
+        w_codes = sb([P, I], U32, "w_codes", at=evals23_at + KIB)
         w_scales = sb([P, I], U8, "w_scales")
         halves = [slice(0, I // 2), slice(I // 2, I)]
         whole = slice(0, I)
@@ -175,10 +195,9 @@ def tile_attend_softmerge_kernel(tc, ekey_words, ekey_scales, keys_words, keys_s
                 p_rows[r][:], scores[r][:], ACT.Exp, bias=neg_max[r][:], accum_out=row_sum[r // 2][:, r % 2 : r % 2 + 1]
             )
         nc.vector.reciprocal(inv_sum[0][:], row_sum[0][:])
-        evals_g1 = gather_evals(1, at=stats_at + KIB)
-        load_vals(3)
-        nc.vector.reciprocal(inv_sum[1][:], row_sum[1][:])
         nc.vector.tensor_tensor(row_factor[:], inv_sum[0][:], fac_sb[:, 0:2], ALU.mult)
+        evals_g1 = gather_evals(1, at=stats_at + 4 * KIB)
+        nc.vector.reciprocal(inv_sum[1][:], row_sum[1][:])
 
         def product_scalar(e):
             nc.scalar.activation(w_pairs[:, 0, :, e], p_rows[e][:], ACT.Copy, scale=row_factor[:, e : e + 1])
@@ -192,10 +211,12 @@ def tile_attend_softmerge_kernel(tc, ekey_words, ekey_scales, keys_words, keys_s
         product_scalar(0)
         product_vector(0)
         vt0 = quantize_vt(0, vt_rows0, at=stats_at + 5 * KIB)
-        vt_rows1 = turn(1, evals_g1, "turned1", tag="p_rows0")
         product_scalar(1)
         product_vector(1)
-        evals_g2 = gather_evals(2, at=stats_at + 2 * KIB)
+        vt_rows1 = turn(1, evals_g1, "turned1", tag="p_rows1")
+
+        evals_g2 = gather_dealt(2, at=stats_at + 2 * KIB)
+        evals_g3 = gather_dealt(3, tag="p_rows3")
 
         def weave(h):
             nc.scalar.copy(w_woven[h][:].bitcast(F32), w_pairs[:, :, halves[h], :].bitcast(F32).rearrange("p u i o -> p i (u o)"))
@@ -203,25 +224,24 @@ def tile_attend_softmerge_kernel(tc, ekey_words, ekey_scales, keys_words, keys_s
                 out=w_codes[:, halves[h]].bitcast(FP8X4), scales=w_scales[:, halves[h]], in_=w_woven[h][:].rearrange("p i t -> p (i t)")
             )
 
+        vt1 = quantize_vt(1, vt_rows1, at=evals23_at + 4 * KIB)
         weave(0)
-        vt1 = quantize_vt(1, vt_rows1, tag="p_rows3")
         weave(1)
-        evals_g3 = gather_evals(3, tag="w_woven0")
-        vt_rows2 = turn(2, evals_g2, "turned2", tag="w_pairs")
-        vt2 = quantize_vt(2, vt_rows2, tag="w_woven1")
+        vt2 = quantize_vt(2, turn_dealt(2, evals_g2, at=pairs_at), tag="w_woven0")
+        vt3 = quantize_vt(3, turn_dealt(3, evals_g3, at=pairs_at + KIB), tag="w_woven1")
 
-        result01 = sb([P, 2, I], F32, "result01", at=evals_at[3] + KIB)
+        result01 = sb([P, 2, I], F32, "result01")
         for h, bank in enumerate(("spare", "score0")):
             add_vals(0, result01[:, 0, halves[h]], merge(0, vt0, halves[h], bank)[:], halves[h])
-        vt3 = quantize_vt(3, turn(3, evals_g3, "turned3", at=stats_at + 5 * KIB), tag="merged_sb0_0")
         merged1 = merge(1, vt1, whole, "score1")
         add_vals(1, result01[:, 1, :], merged1[:], whole)
-        nc.sync.dma_start(out_rows[:, 0:2, :], result01[:])
+        nc.sync.dma_start(out_rows[0], result01[:])
+        merged2 = merge(2, vt2, whole, "score2")
         result2 = sb([P, I], F32, "result2")
-        add_vals(2, result2[:], merge(2, vt2, whole, "score2", tag="w_woven0")[:], whole)
-        nc.sync.dma_start(out_rows[:, 2, :], result2[:])
+        add_vals(2, result2[:], merged2[:], whole)
+        nc.sync.dma_start(out_rows[1, :, 0, :], result2[:])
         merged3 = merge(3, vt3, whole, "score3")
         for lo, hi in zip(TAIL_CUTS, TAIL_CUTS[1:]):
             piece = sb([P, hi - lo], F32, "result3_%d" % lo)
             add_vals(3, piece[:], merged3[:, lo:hi], slice(lo, hi))
-            nc.sync.dma_start(out_rows[:, 3, lo:hi], piece[:])
+            nc.sync.dma_start(out_rows[1, :, 1, lo:hi], piece[:])

@@ -215,7 +215,8 @@ def tile_attend_softmerge_kernel(tc, ekey_words, ekey_scales, keys_words, keys_s
         product_vector(1)
         vt_rows1 = turn(1, evals_g1, "turned1", tag="p_rows1")
 
-        evals_g2 = gather_dealt(2, at=stats_at + 2 * KIB)
+        evals_g2 = sb([P, J], BF16, "evals_g2", at=stats_at + 2 * KIB)
+        nc.vector.tensor_copy(evals_g2[:], evals23[:].rearrange("p u t -> p (u t)").indirect(evicted_list[:]))
         evals_g3 = gather_dealt(3, tag="p_rows3")
 
         def weave(h):
@@ -227,7 +228,7 @@ def tile_attend_softmerge_kernel(tc, ekey_words, ekey_scales, keys_words, keys_s
         vt1 = quantize_vt(1, vt_rows1, at=evals23_at + 4 * KIB)
         weave(0)
         weave(1)
-        vt2 = quantize_vt(2, turn_dealt(2, evals_g2, at=pairs_at), tag="w_woven0")
+        vt2 = quantize_vt(2, turn(2, evals_g2, "turned2", at=pairs_at), tag="w_woven0")
         vt3 = quantize_vt(3, turn_dealt(3, evals_g3, at=pairs_at + KIB), tag="w_woven1")
 
         result01 = sb([P, 2, I], F32, "result01")

@@ -158,15 +158,15 @@ def tile_attend_softmerge_kernel(tc, ekey_words, ekey_scales, keys_words, keys_s
             nc.vector.quantize_mx(out=codes[:].bitcast(FP8X4), scales=scales[:], in_=rows[:])
             return codes, scales
 
-        def merge(b, vt, cols, bank, tag=None):
-            width = cols.stop - cols.start
-            merged = psum.tile([P, width], F32, name="merged%d_%d" % (b, cols.start), tag=bank)
-            nc.tensor.matmul_mx(
-                out=merged[:], lhsT=vt[0][:].bitcast(FP8X4), lhsT_scale=vt[1][:],
-                rhs=w_codes[:, cols].bitcast(FP8X4), rhs_scale=w_scales[:, cols], start=True, stop=True,
-            )
-            merged_sb = sb([P, width], F32, "merged_sb%d_%d" % (b, cols.start), tag)
-            nc.scalar.copy(merged_sb[:], merged[:])
+        def merge(b, vt, which, bank):
+            merged = psum.tile([P, len(which), I // 2], F32, name="merged%d_%d" % (b, which[0]), tag=bank)
+            for place, h in enumerate(which):
+                nc.tensor.matmul_mx(
+                    out=merged[:, place, :], lhsT=vt[0][:].bitcast(FP8X4), lhsT_scale=vt[1][:],
+                    rhs=w_codes[h][:].bitcast(FP8X4), rhs_scale=w_scales[h][:], start=True, stop=True,
+                )
+            merged_sb = sb([P, len(which) * I // 2], F32, "merged_sb%d_%d" % (b, which[0]))
+            nc.scalar.copy(merged_sb[:], merged[:].rearrange("p h i -> p (h i)"))
             return merged_sb
 
         def add_vals(b, result, merged_part, cols):
@@ -184,8 +184,8 @@ def tile_attend_softmerge_kernel(tc, ekey_words, ekey_scales, keys_words, keys_s
         p_rows = [sb([P, I], F32, "p_rows%d" % r) for r in range(PACK)]
         w_pairs = sb([P, 2, I, 2], BF16, "w_pairs", at=pairs_at)
         w_woven = [sb([P, I // 2, PACK], BF16, "w_woven%d" % h) for h in range(2)]
-        w_codes = sb([P, I], U32, "w_codes", at=evals23_at + KIB)
-        w_scales = sb([P, I], U8, "w_scales")
+        w_codes = [sb([P, I // 2], U32, "w_codes0"), sb([P, I // 2], U32, "w_codes1")]
+        w_scales = [sb([P, I // 2], U8, "w_scales%d" % h) for h in range(2)]
         halves = [slice(0, I // 2), slice(I // 2, I)]
         whole = slice(0, I)
 
@@ -199,49 +199,54 @@ def tile_attend_softmerge_kernel(tc, ekey_words, ekey_scales, keys_words, keys_s
         evals_g1 = gather_evals(1, at=stats_at + 4 * KIB)
         nc.vector.reciprocal(inv_sum[1][:], row_sum[1][:])
 
-        def product_scalar(e):
-            nc.scalar.activation(w_pairs[:, 0, :, e], p_rows[e][:], ACT.Copy, scale=row_factor[:, e : e + 1])
+        def product_scalar(e, h):
+            nc.scalar.activation(w_pairs[:, 0, halves[h], e], p_rows[e][:, halves[h]], ACT.Copy, scale=row_factor[:, e : e + 1])
 
-        def product_vector(e):
+        def product_vector(e, h):
             nc.vector.tensor_scalar(
-                w_pairs[:, 1, :, e], p_rows[2 + e][:], inv_sum[1][:, e : e + 1], fac_sb[:, 2 + e : 3 + e], ALU.mult, ALU.mult
+                w_pairs[:, 1, halves[h], e], p_rows[2 + e][:, halves[h]],
+                inv_sum[1][:, e : e + 1], fac_sb[:, 2 + e : 3 + e], ALU.mult, ALU.mult,
             )
-
-        vt_rows0 = turn(0, evals_g0, "score0", at=stats_at + 2 * KIB)
-        product_scalar(0)
-        product_vector(0)
-        vt0 = quantize_vt(0, vt_rows0, at=stats_at + 5 * KIB)
-        product_scalar(1)
-        product_vector(1)
-        vt_rows1 = turn(1, evals_g1, "turned1", tag="p_rows1")
-
-        evals_g2 = sb([P, J], BF16, "evals_g2", at=stats_at + 2 * KIB)
-        nc.vector.tensor_copy(evals_g2[:], evals23[:].rearrange("p u t -> p (u t)").indirect(evicted_list[:]))
-        evals_g3 = gather_dealt(3, tag="p_rows3")
 
         def weave(h):
             nc.scalar.copy(w_woven[h][:].bitcast(F32), w_pairs[:, :, halves[h], :].bitcast(F32).rearrange("p u i o -> p i (u o)"))
+
+        def quantize_w(h):
             nc.vector.quantize_mx(
-                out=w_codes[:, halves[h]].bitcast(FP8X4), scales=w_scales[:, halves[h]], in_=w_woven[h][:].rearrange("p i t -> p (i t)")
+                out=w_codes[h][:].bitcast(FP8X4), scales=w_scales[h][:], in_=w_woven[h][:].rearrange("p i t -> p (i t)")
             )
 
-        vt1 = quantize_vt(1, vt_rows1, at=evals23_at + 4 * KIB)
+        for e in range(2):
+            for h in range(2):
+                product_scalar(e, h)
+                product_vector(e, h)
         weave(0)
+        quantize_w(0)
+        vt0 = quantize_vt(0, turn(0, evals_g0, "score0", tag="p_rows1"))
         weave(1)
-        vt2 = quantize_vt(2, turn(2, evals_g2, "turned2", at=pairs_at), tag="w_woven0")
-        vt3 = quantize_vt(3, turn_dealt(3, evals_g3, at=pairs_at + KIB), tag="w_woven1")
+        vt_rows1 = turn(1, evals_g1, "turned1", at=pairs_at + 2 * KIB)
+
+        evals_g2 = sb([P, J], BF16, "evals_g2")
+        nc.vector.tensor_copy(evals_g2[:], evals23[:].rearrange("p u t -> p (u t)").indirect(evicted_list[:]))
+        quantize_w(1)
+        vt1 = quantize_vt(1, vt_rows1)
+        vt2 = quantize_vt(2, turn(2, evals_g2, "turned2", at=pairs_at))
+        evals_g3 = gather_dealt(3, at=pairs_at + 2 * KIB)
+        merged0 = [merge(0, vt0, [h], bank) for h, bank in enumerate(("spare", "score0"))]
+        merged1 = merge(1, vt1, [0, 1], "score1")
+        vt_rows3 = turn_dealt(3, evals_g3, at=pairs_at + KIB)
 
         result01 = sb([P, 2, I], F32, "result01")
-        for h, bank in enumerate(("spare", "score0")):
-            add_vals(0, result01[:, 0, halves[h]], merge(0, vt0, halves[h], bank)[:], halves[h])
-        merged1 = merge(1, vt1, whole, "score1")
+        for h in range(2):
+            add_vals(0, result01[:, 0, halves[h]], merged0[h][:], halves[h])
+        vt3 = quantize_vt(3, vt_rows3, tag="merged_sb0_0")
         add_vals(1, result01[:, 1, :], merged1[:], whole)
         nc.sync.dma_start(out_rows[0], result01[:])
-        merged2 = merge(2, vt2, whole, "score2")
+        merged2 = merge(2, vt2, [0, 1], "turned3")
         result2 = sb([P, I], F32, "result2")
         add_vals(2, result2[:], merged2[:], whole)
         nc.sync.dma_start(out_rows[1, :, 0, :], result2[:])
-        merged3 = merge(3, vt3, whole, "score3")
+        merged3 = merge(3, vt3, [0, 1], "score3")
         for lo, hi in zip(TAIL_CUTS, TAIL_CUTS[1:]):
             piece = sb([P, hi - lo], F32, "result3_%d" % lo)
             add_vals(3, piece[:], merged3[:, lo:hi], slice(lo, hi))

@@ -30,9 +30,11 @@ TAIL_CUTS = [0, 256, 384, 512]
 
 def tile_attend_softmerge_kernel(tc, ekey_words, ekey_scales, keys_words, keys_scales, fac, evals, vals, offs, offs2, out):
     nc = tc.nc
-    evals_rows = evals.rearrange("(h p u) n -> h p u n", h=2, u=2)
-    vals_rows = vals.rearrange("(h p u) n -> h p u n", h=2, u=2)
-    out_rows = out.rearrange("(h p u) n -> h p u n", h=2, u=2)
+
+    def by_tile(rows):
+        return [rows[: E // 2].rearrange("(p u) n -> p u n", u=2), rows[E // 2 :].rearrange("(u p) n -> p u n", u=2)]
+
+    evals_rows, vals_rows, out_rows = by_tile(evals), by_tile(vals), by_tile(out)
 
     with ExitStack() as ctx:
         keep = ctx.enter_context(tc.tile_pool(name="keep", bufs=1))
@@ -69,10 +71,10 @@ def tile_attend_softmerge_kernel(tc, ekey_words, ekey_scales, keys_words, keys_s
         fac_row = sb([P, J], F32, "fac_row")
 
         def load_evals(b):
-            nc.sync.dma_start(evals_table[b][:], evals_rows[b // 2, :, b % 2, :])
+            nc.sync.dma_start(evals_table[b][:], evals_rows[b // 2][:, b % 2, :])
 
         def load_vals(b):
-            nc.sync.dma_start(vals_table[b][:], vals_rows[b // 2, :, b % 2, :])
+            nc.sync.dma_start(vals_table[b][:], vals_rows[b // 2][:, b % 2, :])
 
         nc.gpsimd.memset(ekey_scale_table[:ROW0, :].bitcast(I32), 0)
         nc.vector.memset(keys_scale_table[:ROW0, :].bitcast(I32), 0)
@@ -245,9 +247,9 @@ def tile_attend_softmerge_kernel(tc, ekey_words, ekey_scales, keys_words, keys_s
         merged2 = merge(2, vt2, [0, 1], "turned3")
         result2 = sb([P, I], F32, "result2")
         add_vals(2, result2[:], merged2[:], whole)
-        nc.sync.dma_start(out_rows[1, :, 0, :], result2[:])
+        nc.sync.dma_start(out_rows[1][:, 0, :], result2[:])
         merged3 = merge(3, vt3, [0, 1], "score3")
         for lo, hi in zip(TAIL_CUTS, TAIL_CUTS[1:]):
             piece = sb([P, hi - lo], F32, "result3_%d" % lo)
             add_vals(3, piece[:], merged3[:, lo:hi], slice(lo, hi))
-            nc.sync.dma_start(out_rows[1, :, 1, lo:hi], piece[:])
+            nc.sync.dma_start(out_rows[1][:, 1, lo:hi], piece[:])

@@ -25,56 +25,53 @@ SCALE_ROWS = 16
 ROW0 = P - SCALE_ROWS
 OVERLAP = 128
 TABLE_BYTES = T * 4
-TAIL_CUTS = [0, 256, 384, 512]
+BANK_BYTES = 2 * KIB
+TAIL_CUTS = [0, 256, 416, 512]
 
 
 def tile_attend_softmerge_kernel(tc, ekey_words, ekey_scales, keys_words, keys_scales, fac, evals, vals, offs, offs2, out):
     nc = tc.nc
 
-    def by_tile(rows):
-        return [rows[: E // 2].rearrange("(p u) n -> p u n", u=2), rows[E // 2 :].rearrange("(u p) n -> p u n", u=2)]
-
-    evals_rows, vals_rows, out_rows = by_tile(evals), by_tile(vals), by_tile(out)
+    evals_rows = evals.rearrange("(b p) n -> p b n", p=P)
+    vals_rows = vals.rearrange("(b p) n -> p b n", p=P)
+    out_rows = out.rearrange("(b p) n -> p b n", p=P)
 
     with ExitStack() as ctx:
         keep = ctx.enter_context(tc.tile_pool(name="keep", bufs=1))
         placed = ctx.enter_context(tc.tile_pool(name="placed", bufs=1))
         psum = ctx.enter_context(tc.psum_pool(name="psum", bufs=1))
 
-        def sb(shape, dtype, name, tag=None, at=None):
+        def bank(shape, name, number):
+            return psum.tile(shape, F32, name=name, offset=number * BANK_BYTES)
+
+        def sb(shape, dtype, name, at=None):
             if at is not None:
                 return placed.tile(shape, dtype, name=name, align_bytes=64, offset=at)
-            return keep.tile(shape, dtype, name=name, tag=tag or name, align_bytes=64)
+            return keep.tile(shape, dtype, name=name, align_bytes=64)
 
-        def below(at):
-            return at + OVERLAP - TABLE_BYTES
-
-        def above(at, size):
-            return at + size - OVERLAP
-
-        evals0_at, keys_scale_g_at, keys_at, ekey_at, keys_scale_at, ekey_scale_g_at = (k * KIB for k in (8, 32, 50, 64, 80, 86))
-        evals_at = [evals0_at, below(keys_scale_g_at)]
-        evals23_at = below(keys_at) - TABLE_BYTES
-        vals_at = [below(ekey_at), above(ekey_at, TABLE_BYTES), below(evals0_at), above(evals0_at, TABLE_BYTES)]
-        stats_at = ekey_at + KIB
-        pairs_at = 96 * KIB
+        evals1_at = 0
+        keys_scale_g_at = evals1_at + TABLE_BYTES - OVERLAP
+        evals23_at = keys_scale_g_at + I - OVERLAP
+        vals01_at = 26 * KIB
+        keys_at = vals01_at + 2 * TABLE_BYTES - OVERLAP
+        vals2_at = keys_at + 2 * T - OVERLAP
+        ekey_at, ekey_scale_g_at = 58 * KIB, 76 * KIB
+        vals3_at = ekey_at + TABLE_BYTES - OVERLAP
+        fac_at, woven_at, last_max_at, result_at = 80 * KIB, 84 * KIB, 90 * KIB, 94 * KIB
 
         kept_list = sb([P, I // 16], U16, "kept_list")
         evicted_list = sb([P, J // 16], U16, "evicted_list")
         keys_table = sb([P, T], U16, "keys_table", at=keys_at)
         ekey_table = sb([P, T], U32, "ekey_table", at=ekey_at)
-        keys_scale_table = sb([P, T], U8, "keys_scale_table", at=keys_scale_at)
+        keys_scale_table = sb([P, T], U8, "keys_scale_table")
         ekey_scale_table = sb([P, T], U8, "ekey_scale_table")
-        evals_table = [sb([P, T], F32, "evals_table%d" % b, at=evals_at[b]) for b in range(2)]
+        evals0 = sb([P, T], F32, "evals0")
+        evals1 = sb([P, T], F32, "evals1", at=evals1_at)
         evals23 = sb([P, 2, T], F32, "evals23", at=evals23_at)
-        vals_table = [sb([P, T], F32, "vals_table%d" % b, at=vals_at[b]) for b in range(PACK)]
-        fac_row = sb([P, J], F32, "fac_row")
-
-        def load_evals(b):
-            nc.sync.dma_start(evals_table[b][:], evals_rows[b // 2][:, b % 2, :])
-
-        def load_vals(b):
-            nc.sync.dma_start(vals_table[b][:], vals_rows[b // 2][:, b % 2, :])
+        vals01 = sb([P, 2, T], F32, "vals01", at=vals01_at)
+        vals2 = sb([P, T], F32, "vals2", at=vals2_at)
+        vals3 = sb([P, T], F32, "vals3", at=vals3_at)
+        fac_row = sb([P, J], F32, "fac_row", at=fac_at)
 
         nc.gpsimd.memset(ekey_scale_table[:ROW0, :].bitcast(I32), 0)
         nc.vector.memset(keys_scale_table[:ROW0, :].bitcast(I32), 0)
@@ -86,22 +83,22 @@ def tile_attend_softmerge_kernel(tc, ekey_words, ekey_scales, keys_words, keys_s
         nc.sync.dma_start(keys_table[:].bitcast(I32), keys_words[0].bitcast(I32))
         nc.scalar.dma_start(ekey_table[:].bitcast(I32), ekey_words[0].rearrange("p n t -> p (n t)").bitcast(I32))
         nc.sync.dma_start(fac_row[P - 1 :, :], fac.rearrange("j o -> o j"))
-        load_evals(0)
+        nc.sync.dma_start(evals0[:], evals_rows[:, 0, :])
 
         ident = sb([P, P], F32, "ident")
         make_identity(nc, ident[:])
-        fac_turned = psum.tile([P, PACK, P], F32, name="fac_turned", tag="spare")
-        for t in range(PACK):
-            nc.tensor.transpose(fac_turned[:, t, :], fac_row[:, t:J:PACK], ident[:])
+        fac_turned = bank([P, PACK, P], "fac_turned", 4)
+        for r in range(PACK):
+            nc.tensor.transpose(fac_turned[:, r, :], fac_row[:, r:J:PACK], ident[:])
+        fac_sb = sb([P, PACK], F32, "fac_sb")
+        nc.scalar.copy(fac_sb[:], fac_turned[:, :, P - 1])
 
         ekey_scale_g = sb([P, J], U8, "ekey_scale_g", at=ekey_scale_g_at)
         keys_scale_g = sb([P, I], U8, "keys_scale_g", at=keys_scale_g_at)
         planes = sb([P, J + I], U8, "planes")
-        nc.vector.tensor_copy(ekey_scale_g[:], ekey_scale_table[:].indirect(evicted_list[:]))
+        nc.vector.tensor_copy(ekey_scale_g[:].rearrange("p (r s) -> p s r", r=PACK), ekey_scale_table[:].indirect(evicted_list[:]))
         nc.vector.tensor_copy(keys_scale_g[:], keys_scale_table[:].indirect(kept_list[:]))
-        nc.vector.tensor_copy(
-            planes[:, :J].rearrange("p (r s) -> p r s", r=PACK), ekey_scale_g[:].rearrange("p (s r) -> p r s", r=PACK)
-        )
+        nc.vector.tensor_copy(planes[:, :J].bitcast(I32), ekey_scale_g[:].bitcast(I32))
         nc.vector.tensor_copy(planes[:, J:].bitcast(I32), keys_scale_g[:].bitcast(I32))
         for r in range(4):
             nc.sync.dma_start(planes[r:P:32, :].bitcast(I32), planes[ROW0 + r : P : 4, :].bitcast(I32))
@@ -109,14 +106,27 @@ def tile_attend_softmerge_kernel(tc, ekey_words, ekey_scales, keys_words, keys_s
         ekey_g = sb([P, J], U32, "ekey_g", at=ekey_scale_g_at + 2 * OVERLAP)
         nc.vector.tensor_copy(keys_g[:], keys_table[:].indirect(kept_list[:]))
         nc.vector.tensor_copy(ekey_g[:].rearrange("p (r s) -> p s r", r=PACK), ekey_table[:].indirect(evicted_list[:]))
-        fac_sb = sb([P, PACK], F32, "fac_sb", at=keys_at + 3 * KIB)
-        nc.vector.tensor_copy(fac_sb[:], fac_turned[:, :, P - 1])
-        load_evals(1)
-        nc.sync.dma_start(evals23[:], evals_rows[1])
-        load_vals(0)
-        load_vals(1)
+        nc.sync.dma_start(evals1[:], evals_rows[:, 1, :])
+        nc.sync.dma_start(evals23[:], evals_rows[:, 2:4, :])
+        nc.sync.dma_start(vals01[:], vals_rows[:, 0:2, :])
+        nc.sync.dma_start(vals2[:], vals_rows[:, 2, :])
+        nc.sync.dma_start(vals3[:], vals_rows[:, 3, :])
 
-        scores = [psum.tile([P, I], F32, name="score%d" % r) for r in range(PACK)]
+        def gather_whole(table, name, at=None):
+            gathered = sb([P, J], BF16, name, at=at)
+            nc.scalar.activation(gathered[:], table.indirect(evicted_list[:]), ACT.Copy)
+            words = gathered[:].bitcast(F32)
+            return [words[:, u : J // 2 : 2] for u in range(2)]
+
+        def gather_second(pair, name, at=None):
+            gathered = sb([P, J], BF16, name, at=at)
+            nc.vector.tensor_copy(gathered[:].rearrange("p (u s c) -> p s u c", u=2, c=2), pair[:, 1, :].indirect(evicted_list[:]))
+            words = gathered[:].bitcast(F32)
+            return [words[:, u * P : (u + 1) * P] for u in range(2)]
+
+        words0 = gather_whole(evals0[:], "evals_g0", at=fac_at)
+
+        scores = [bank([P, I], "score%d" % r, r) for r in range(PACK)]
         for r in range(PACK):
             cols = slice(r * P, (r + 1) * P)
             nc.tensor.matmul_mx(
@@ -124,132 +134,102 @@ def tile_attend_softmerge_kernel(tc, ekey_words, ekey_scales, keys_words, keys_s
                 rhs=keys_g[:].bitcast(FP4X4), rhs_scale=planes[:, J:], start=True, stop=True,
             )
 
-        def gather_evals(b, tag=None, at=None):
-            gathered = sb([P, J], BF16, "evals_g%d" % b, tag, at)
-            nc.vector.tensor_copy(gathered[:], evals_table[b][:].indirect(evicted_list[:]))
-            return gathered
-
-        def turn(b, gathered, bank, tag=None, at=None):
-            turned = psum.tile([P, 2, P], F32, name="turned%d" % b, tag=bank)
-            words = gathered[:].bitcast(F32)
-            for u in range(2):
-                nc.tensor.transpose(turned[:, u, :], words[:, u : J // 2 : 2], ident[:])
-            rows = sb([P, P * PACK], BF16, "vt_rows%d" % b, tag, at)
-            nc.scalar.copy(rows[:].bitcast(F32).rearrange("p (e u) -> p e u", u=2), turned[:].rearrange("p u e -> p e u"))
-            return rows
-
-        def gather_dealt(b, tag=None, at=None):
-            gathered = sb([P, J], BF16, "evals_g%d" % b, tag, at)
-            nc.vector.tensor_copy(
-                gathered[:].rearrange("p (u s e) -> p s u e", u=2, e=2), evals23[:, b - 2, :].indirect(evicted_list[:])
-            )
-            return gathered
-
-        def turn_dealt(b, gathered, tag=None, at=None):
-            turned = psum.tile([P, 2, P], F32, name="turned%d" % b)
-            words = gathered[:].bitcast(F32)
-            for u in range(2):
-                nc.tensor.transpose(turned[:, u, :], words[:, u * P : (u + 1) * P], ident[:])
-            rows = sb([P, P * PACK], BF16, "vt_rows%d" % b, tag, at)
-            nc.scalar.copy(rows[:].bitcast(F32).rearrange("p (e u) -> p e u", u=2), turned[:].rearrange("p u e -> p e u"))
-            return rows
-
-        def quantize_vt(b, rows, tag=None, at=None):
-            codes = sb([P, P], U32, "vt_codes%d" % b, tag, at)
-            scales = sb([P, P], U8, "vt_scales%d" % b)
-            nc.vector.quantize_mx(out=codes[:].bitcast(FP8X4), scales=scales[:], in_=rows[:])
-            return codes, scales
-
-        def merge(b, vt, which, bank):
-            merged = psum.tile([P, len(which), I // 2], F32, name="merged%d_%d" % (b, which[0]), tag=bank)
-            for place, h in enumerate(which):
-                nc.tensor.matmul_mx(
-                    out=merged[:, place, :], lhsT=vt[0][:].bitcast(FP8X4), lhsT_scale=vt[1][:],
-                    rhs=w_codes[h][:].bitcast(FP8X4), rhs_scale=w_scales[h][:], start=True, stop=True,
-                )
-            merged_sb = sb([P, len(which) * I // 2], F32, "merged_sb%d_%d" % (b, which[0]))
-            nc.scalar.copy(merged_sb[:], merged[:].rearrange("p h i -> p (h i)"))
-            return merged_sb
-
-        def add_vals(b, result, merged_part, cols):
-            window = vals_table[b][:].indirect(kept_list[:, cols.start // 16 : cols.stop // 16])
-            nc.vector.tensor_tensor(result, window, merged_part, ALU.add)
-
-        evals_g0 = gather_evals(0, at=keys_at + KIB)
-        load_vals(2)
-        load_vals(3)
-
-        neg_max = [sb([P, 1], F32, "neg_max%d" % r, at=stats_at + r * KIB) for r in range(PACK)]
-        row_sum = [sb([P, 2], F32, "row_sum0", at=stats_at + 4 * KIB), sb([P, 2], F32, "row_sum1", at=stats_at + 5 * KIB)]
-        inv_sum = [sb([P, 2], F32, "inv_sum%d" % h) for h in range(2)]
-        row_factor = sb([P, 2], F32, "row_factor")
+        neg_max = [sb([P, 1], F32, "neg_max%d" % r, at=last_max_at - (PACK - 1 - r) * 64) for r in range(PACK)]
+        row_sum = [sb([P, 2], F32, "row_sum%d" % u) for u in range(2)]
+        inv_sum = [sb([P, 2], F32, "inv_sum%d" % u) for u in range(2)]
         p_rows = [sb([P, I], F32, "p_rows%d" % r) for r in range(PACK)]
-        w_pairs = sb([P, 2, I, 2], BF16, "w_pairs", at=pairs_at)
-        w_woven = [sb([P, I // 2, PACK], BF16, "w_woven%d" % h) for h in range(2)]
-        w_codes = [sb([P, I // 2], U32, "w_codes0"), sb([P, I // 2], U32, "w_codes1")]
-        w_scales = [sb([P, I // 2], U8, "w_scales%d" % h) for h in range(2)]
+        w_pairs = sb([P, 2, I, 2], BF16, "w_pairs")
+        w_woven = [sb([P, I // 2, PACK], BF16, "w_woven%d" % h, at=woven_at + h * 2 * KIB) for h in range(2)]
+        w_codes = sb([P, I], U32, "w_codes")
+        w_scales = sb([P, I], U8, "w_scales")
         halves = [slice(0, I // 2), slice(I // 2, I)]
-        whole = slice(0, I)
 
         for r in range(PACK):
             nc.vector.tensor_reduce(neg_max[r][:], scores[r][:], AXIS.X, ALU.max, negate=True)
             nc.scalar.activation(
                 p_rows[r][:], scores[r][:], ACT.Exp, bias=neg_max[r][:], accum_out=row_sum[r // 2][:, r % 2 : r % 2 + 1]
             )
-        nc.vector.reciprocal(inv_sum[0][:], row_sum[0][:])
-        nc.vector.tensor_tensor(row_factor[:], inv_sum[0][:], fac_sb[:, 0:2], ALU.mult)
-        evals_g1 = gather_evals(1, at=stats_at + 4 * KIB)
-        nc.vector.reciprocal(inv_sum[1][:], row_sum[1][:])
+        words1 = gather_whole(evals1[:], "evals_g1", at=last_max_at)
 
-        def product_scalar(e, h):
-            nc.scalar.activation(w_pairs[:, 0, halves[h], e], p_rows[e][:, halves[h]], ACT.Copy, scale=row_factor[:, e : e + 1])
-
-        def product_vector(e, h):
+        def product(r, cols):
+            u, c = divmod(r, 2)
             nc.vector.tensor_scalar(
-                w_pairs[:, 1, halves[h], e], p_rows[2 + e][:, halves[h]],
-                inv_sum[1][:, e : e + 1], fac_sb[:, 2 + e : 3 + e], ALU.mult, ALU.mult,
+                w_pairs[:, u, cols, c], p_rows[r][:, cols], inv_sum[u][:, c : c + 1], fac_sb[:, r : r + 1], ALU.mult, ALU.mult
             )
 
-        def weave(h):
-            nc.scalar.copy(w_woven[h][:].bitcast(F32), w_pairs[:, :, halves[h], :].bitcast(F32).rearrange("p u i o -> p i (u o)"))
-
-        def quantize_w(h):
-            nc.vector.quantize_mx(
-                out=w_codes[h][:].bitcast(FP8X4), scales=w_scales[h][:], in_=w_woven[h][:].rearrange("p i t -> p (i t)")
-            )
-
-        for e in range(2):
-            for h in range(2):
-                product_scalar(e, h)
-                product_vector(e, h)
-        weave(0)
-        quantize_w(0)
-        vt0 = quantize_vt(0, turn(0, evals_g0, "score0", tag="p_rows1"))
-        weave(1)
-        vt_rows1 = turn(1, evals_g1, "turned1", at=pairs_at + 2 * KIB)
-
-        evals_g2 = sb([P, J], BF16, "evals_g2")
-        nc.vector.tensor_copy(evals_g2[:], evals23[:].rearrange("p u t -> p (u t)").indirect(evicted_list[:]))
-        quantize_w(1)
-        vt1 = quantize_vt(1, vt_rows1)
-        vt2 = quantize_vt(2, turn(2, evals_g2, "turned2", at=pairs_at))
-        evals_g3 = gather_dealt(3, at=pairs_at + 2 * KIB)
-        merged0 = [merge(0, vt0, [h], bank) for h, bank in enumerate(("spare", "score0"))]
-        merged1 = merge(1, vt1, [0, 1], "score1")
-        vt_rows3 = turn_dealt(3, evals_g3, at=pairs_at + KIB)
-
-        result01 = sb([P, 2, I], F32, "result01")
+        nc.vector.reciprocal(inv_sum[0][:], row_sum[0][:])
+        product(0, slice(0, I))
+        product(1, slice(0, I))
+        nc.vector.reciprocal(inv_sum[1][:], row_sum[1][:])
         for h in range(2):
-            add_vals(0, result01[:, 0, halves[h]], merged0[h][:], halves[h])
-        vt3 = quantize_vt(3, vt_rows3, tag="merged_sb0_0")
-        add_vals(1, result01[:, 1, :], merged1[:], whole)
-        nc.sync.dma_start(out_rows[0], result01[:])
-        merged2 = merge(2, vt2, [0, 1], "turned3")
+            product(2, halves[h])
+            product(3, halves[h])
+        for h in range(2):
+            nc.vector.tensor_copy(w_woven[h][:].bitcast(F32), w_pairs[:, :, halves[h], :].bitcast(F32).rearrange("p u i o -> p i (u o)"))
+        for h in range(2):
+            nc.vector.quantize_mx(
+                out=w_codes[:, halves[h]].bitcast(FP8X4), scales=w_scales[:, halves[h]], in_=w_woven[h][:].rearrange("p i t -> p (i t)")
+            )
+
+        def turn_pairs(b, words, number, at=None):
+            turned = bank([P, 2, P], "turned%d" % b, number)
+            for u in range(2):
+                nc.tensor.transpose(turned[:, u, :], words[u], ident[:])
+            rows = sb([P, P * PACK], BF16, "vt_rows%d" % b, at=at)
+            nc.scalar.copy(rows[:].bitcast(F32).rearrange("p (e u) -> p e u", u=2), turned[:].rearrange("p u e -> p e u"))
+            return rows
+
+        def quantize_vt(b, rows, at=None):
+            codes = sb([P, P], U32, "vt_codes%d" % b, at=at)
+            scales = sb([P, P], U8, "vt_scales%d" % b)
+            nc.vector.quantize_mx(out=codes[:].bitcast(FP8X4), scales=scales[:], in_=rows[:])
+            return codes, scales
+
+        def merge(b, vt, number):
+            merged = bank([P, I], "merged%d" % b, number)
+            nc.tensor.matmul_mx(
+                out=merged[:], lhsT=vt[0][:].bitcast(FP8X4), lhsT_scale=vt[1][:],
+                rhs=w_codes[:].bitcast(FP8X4), rhs_scale=w_scales[:], start=True, stop=True,
+            )
+            return merged
+
+        merged0 = merge(0, quantize_vt(0, turn_pairs(0, words0, 3)), 0)
+        merged1 = merge(1, quantize_vt(1, turn_pairs(1, words1, 4)), 1)
+        words2 = gather_whole(evals23[:].rearrange("p b t -> p (b t)"), "evals_g2", at=last_max_at)
+        words3 = gather_second(evals23, "evals_g3", at=woven_at + 2 * KIB)
+        vt_rows2 = turn_pairs(2, words2, 5, at=result_at)
+        merged0_sb = sb([P, I], F32, "merged0_sb", at=last_max_at)
+        nc.scalar.copy(merged0_sb[:], merged0[:])
+        vt_rows3 = turn_pairs(3, words3, 5)
+        merged2 = merge(2, quantize_vt(2, vt_rows2), 2)
+
+        def offsets(cols):
+            return kept_list[:, cols.start // 16 : cols.stop // 16]
+
+        def add_gathered(result, table, cols, merged, name, at=None):
+            gathered = sb([P, cols.stop - cols.start], F32, name, at=at)
+            nc.scalar.activation(gathered[:], table.indirect(offsets(cols)), ACT.Copy)
+            nc.vector.tensor_tensor(result, gathered[:], merged[:, cols], ALU.add)
+
+        result01 = sb([P, 2, I], F32, "result01", at=result_at)
+        nc.vector.tensor_tensor(result01[:, 0, :], vals01[:].rearrange("p b t -> p (b t)").indirect(kept_list[:]), merged0_sb[:], ALU.add)
+        merged3 = merge(3, quantize_vt(3, vt_rows3, at=last_max_at), 3)
+        add_gathered(result01[:, 1, :], vals01[:, 1, :], slice(0, I), merged1, "vals_g1", at=woven_at + 2 * KIB)
+        nc.sync.dma_start(out_rows[:, 0:2, :], result01[:])
+
+        pieces = [slice(lo, hi) for lo, hi in zip(TAIL_CUTS, TAIL_CUTS[1:])]
+        merged2_sb = sb([P, I // 2], F32, "merged2_sb", at=vals01_at + KIB)
+        nc.scalar.copy(merged2_sb[:], merged2[:, halves[0]])
         result2 = sb([P, I], F32, "result2")
-        add_vals(2, result2[:], merged2[:], whole)
-        nc.sync.dma_start(out_rows[1][:, 0, :], result2[:])
-        merged3 = merge(3, vt3, [0, 1], "score3")
-        for lo, hi in zip(TAIL_CUTS, TAIL_CUTS[1:]):
-            piece = sb([P, hi - lo], F32, "result3_%d" % lo)
-            add_vals(3, piece[:], merged3[:, lo:hi], slice(lo, hi))
-            nc.sync.dma_start(out_rows[1][:, 1, lo:hi], piece[:])
+        nc.vector.tensor_tensor(result2[:, halves[0]], vals2[:].indirect(offsets(halves[0])), merged2_sb[:], ALU.add)
+        add_gathered(result2[:, halves[1]], vals2[:], halves[1], merged2, "vals_g2", at=fac_at)
+        nc.sync.dma_start(out_rows[:, 2, :], result2[:])
+
+        merged3_sb = sb([P, TAIL_CUTS[1]], F32, "merged3_sb", at=vals2_at + KIB)
+        nc.scalar.copy(merged3_sb[:], merged3[:, pieces[0]])
+        last = [sb([P, cols.stop - cols.start], F32, "last%d" % n, at=fac_at + n * KIB) for n, cols in enumerate(pieces)]
+        nc.vector.tensor_tensor(last[0][:], vals3[:].indirect(offsets(pieces[0])), merged3_sb[:], ALU.add)
+        nc.sync.dma_start(out_rows[:, 3, pieces[0]], last[0][:])
+        for n in (1, 2):
+            add_gathered(last[n][:], vals3[:], pieces[n], merged3, "vals_g3_%d" % n)
+            nc.sync.dma_start(out_rows[:, 3, pieces[n]], last[n][:])

@@ -26,7 +26,7 @@ ROW0 = P - SCALE_ROWS
 OVERLAP = 128
 TABLE_BYTES = T * 4
 BANK_BYTES = 2 * KIB
-TAIL_CUTS = [0, 256, 416, 512]
+TAIL_CUTS = [0, 256, 384, 512]
 
 
 def tile_attend_softmerge_kernel(tc, ekey_words, ekey_scales, keys_words, keys_scales, fac, evals, vals, offs, offs2, out):
@@ -96,9 +96,11 @@ def tile_attend_softmerge_kernel(tc, ekey_words, ekey_scales, keys_words, keys_s
         ekey_scale_g = sb([P, J], U8, "ekey_scale_g", at=ekey_scale_g_at)
         keys_scale_g = sb([P, I], U8, "keys_scale_g", at=keys_scale_g_at)
         planes = sb([P, J + I], U8, "planes")
-        nc.vector.tensor_copy(ekey_scale_g[:].rearrange("p (r s) -> p s r", r=PACK), ekey_scale_table[:].indirect(evicted_list[:]))
+        nc.vector.tensor_copy(ekey_scale_g[:], ekey_scale_table[:].indirect(evicted_list[:]))
         nc.vector.tensor_copy(keys_scale_g[:], keys_scale_table[:].indirect(kept_list[:]))
-        nc.vector.tensor_copy(planes[:, :J].bitcast(I32), ekey_scale_g[:].bitcast(I32))
+        nc.vector.tensor_copy(
+            planes[:, :J].rearrange("p (r s) -> p r s", r=PACK), ekey_scale_g[:].rearrange("p (s r) -> p r s", r=PACK)
+        )
         nc.vector.tensor_copy(planes[:, J:].bitcast(I32), keys_scale_g[:].bitcast(I32))
         for r in range(4):
             nc.sync.dma_start(planes[r:P:32, :].bitcast(I32), planes[ROW0 + r : P : 4, :].bitcast(I32))

@@ -52,12 +52,13 @@ def tile_attend_softmerge_kernel(tc, ekey_words, ekey_scales, keys_words, keys_s
         evals1_at = 0
         keys_scale_g_at = evals1_at + TABLE_BYTES - OVERLAP
         evals23_at = keys_scale_g_at + I - OVERLAP
-        vals01_at = 26 * KIB
-        keys_at = vals01_at + 2 * TABLE_BYTES - OVERLAP
-        vals2_at = keys_at + 2 * T - OVERLAP
-        ekey_at, ekey_scale_g_at = 58 * KIB, 76 * KIB
+        vals0_at = 26 * KIB
+        keys_at = vals0_at + TABLE_BYTES - OVERLAP
+        vals1_at = keys_at + 2 * T - OVERLAP
+        vals2_at = 48 * KIB
+        ekey_at = vals2_at + TABLE_BYTES - OVERLAP
         vals3_at = ekey_at + TABLE_BYTES - OVERLAP
-        fac_at, woven_at, last_max_at, result_at = 80 * KIB, 84 * KIB, 90 * KIB, 94 * KIB
+        ekey_scale_g_at, sums_at, woven_at, pairs_at, fac_at = (k * KIB for k in (76, 80, 84, 88, 92))
 
         kept_list = sb([P, I // 16], U16, "kept_list")
         evicted_list = sb([P, J // 16], U16, "evicted_list")
@@ -68,9 +69,7 @@ def tile_attend_softmerge_kernel(tc, ekey_words, ekey_scales, keys_words, keys_s
         evals0 = sb([P, T], F32, "evals0")
         evals1 = sb([P, T], F32, "evals1", at=evals1_at)
         evals23 = sb([P, 2, T], F32, "evals23", at=evals23_at)
-        vals01 = sb([P, 2, T], F32, "vals01", at=vals01_at)
-        vals2 = sb([P, T], F32, "vals2", at=vals2_at)
-        vals3 = sb([P, T], F32, "vals3", at=vals3_at)
+        vals_table = [sb([P, T], F32, "vals%d" % b, at=at) for b, at in enumerate((vals0_at, vals1_at, vals2_at, vals3_at))]
         fac_row = sb([P, J], F32, "fac_row", at=fac_at)
 
         nc.gpsimd.memset(ekey_scale_table[:ROW0, :].bitcast(I32), 0)
@@ -110,23 +109,22 @@ def tile_attend_softmerge_kernel(tc, ekey_words, ekey_scales, keys_words, keys_s
         nc.vector.tensor_copy(ekey_g[:].rearrange("p (r s) -> p s r", r=PACK), ekey_table[:].indirect(evicted_list[:]))
         nc.sync.dma_start(evals1[:], evals_rows[:, 1, :])
         nc.sync.dma_start(evals23[:], evals_rows[:, 2:4, :])
-        nc.sync.dma_start(vals01[:], vals_rows[:, 0:2, :])
-        nc.sync.dma_start(vals2[:], vals_rows[:, 2, :])
-        nc.sync.dma_start(vals3[:], vals_rows[:, 3, :])
+        for b in range(PACK):
+            nc.sync.dma_start(vals_table[b][:], vals_rows[:, b, :])
 
-        def gather_whole(table, name, at=None):
+        def gather_whole(table, name, at):
             gathered = sb([P, J], BF16, name, at=at)
             nc.scalar.activation(gathered[:], table.indirect(evicted_list[:]), ACT.Copy)
             words = gathered[:].bitcast(F32)
             return [words[:, u : J // 2 : 2] for u in range(2)]
 
-        def gather_second(pair, name, at=None):
-            gathered = sb([P, J], BF16, name, at=at)
-            nc.vector.tensor_copy(gathered[:].rearrange("p (u s c) -> p s u c", u=2, c=2), pair[:, 1, :].indirect(evicted_list[:]))
+        def gather_dealt(b, at):
+            gathered = sb([P, J], BF16, "evals_g%d" % b, at=at)
+            nc.vector.tensor_copy(gathered[:].rearrange("p (u s c) -> p s u c", u=2, c=2), evals23[:, b - 2, :].indirect(evicted_list[:]))
             words = gathered[:].bitcast(F32)
             return [words[:, u * P : (u + 1) * P] for u in range(2)]
 
-        words0 = gather_whole(evals0[:], "evals_g0", at=fac_at)
+        words0 = gather_whole(evals0[:], "evals_g0", fac_at)
 
         scores = [bank([P, I], "score%d" % r, r) for r in range(PACK)]
         for r in range(PACK):
@@ -136,22 +134,23 @@ def tile_attend_softmerge_kernel(tc, ekey_words, ekey_scales, keys_words, keys_s
                 rhs=keys_g[:].bitcast(FP4X4), rhs_scale=planes[:, J:], start=True, stop=True,
             )
 
-        neg_max = [sb([P, 1], F32, "neg_max%d" % r, at=last_max_at - (PACK - 1 - r) * 64) for r in range(PACK)]
+        neg_max = [sb([P, 1], F32, "neg_max%d" % r, at=sums_at if r == PACK - 1 else None) for r in range(PACK)]
         row_sum = [sb([P, 2], F32, "row_sum%d" % u) for u in range(2)]
         inv_sum = [sb([P, 2], F32, "inv_sum%d" % u) for u in range(2)]
         p_rows = [sb([P, I], F32, "p_rows%d" % r) for r in range(PACK)]
-        w_pairs = sb([P, 2, I, 2], BF16, "w_pairs")
+        w_pairs = sb([P, 2, I, 2], BF16, "w_pairs", at=pairs_at)
         w_woven = [sb([P, I // 2, PACK], BF16, "w_woven%d" % h, at=woven_at + h * 2 * KIB) for h in range(2)]
         w_codes = sb([P, I], U32, "w_codes")
         w_scales = sb([P, I], U8, "w_scales")
         halves = [slice(0, I // 2), slice(I // 2, I)]
+        whole = slice(0, I)
 
         for r in range(PACK):
             nc.vector.tensor_reduce(neg_max[r][:], scores[r][:], AXIS.X, ALU.max, negate=True)
             nc.scalar.activation(
                 p_rows[r][:], scores[r][:], ACT.Exp, bias=neg_max[r][:], accum_out=row_sum[r // 2][:, r % 2 : r % 2 + 1]
             )
-        words1 = gather_whole(evals1[:], "evals_g1", at=last_max_at)
+        words1 = gather_whole(evals1[:], "evals_g1", sums_at)
 
         def product(r, cols):
             u, c = divmod(r, 2)
@@ -160,12 +159,11 @@ def tile_attend_softmerge_kernel(tc, ekey_words, ekey_scales, keys_words, keys_s
             )
 
         nc.vector.reciprocal(inv_sum[0][:], row_sum[0][:])
-        product(0, slice(0, I))
-        product(1, slice(0, I))
+        product(0, whole)
+        product(1, whole)
         nc.vector.reciprocal(inv_sum[1][:], row_sum[1][:])
-        for h in range(2):
-            product(2, halves[h])
-            product(3, halves[h])
+        product(2, whole)
+        product(3, whole)
         for h in range(2):
             nc.vector.tensor_copy(w_woven[h][:].bitcast(F32), w_pairs[:, :, halves[h], :].bitcast(F32).rearrange("p u i o -> p i (u o)"))
         for h in range(2):
@@ -195,43 +193,46 @@ def tile_attend_softmerge_kernel(tc, ekey_words, ekey_scales, keys_words, keys_s
             )
             return merged
 
+        def window(b, cols):
+            return vals_table[b][:].indirect(kept_list[:, cols.start // 16 : cols.stop // 16])
+
+        def gather_vals(b, cols, at):
+            gathered = sb([P, cols.stop - cols.start], F32, "vals_g%d_%d" % (b, cols.start), at=at)
+            nc.scalar.activation(gathered[:], window(b, cols), ACT.Copy)
+            return gathered
+
+        def to_sbuf(b, merged, cols, at):
+            merged_sb = sb([P, cols.stop - cols.start], F32, "merged_sb%d" % b, at=at)
+            nc.scalar.copy(merged_sb[:], merged[:, cols])
+            return merged_sb
+
         merged0 = merge(0, quantize_vt(0, turn_pairs(0, words0, 3)), 0)
-        merged1 = merge(1, quantize_vt(1, turn_pairs(1, words1, 4)), 1)
-        words2 = gather_whole(evals23[:].rearrange("p b t -> p (b t)"), "evals_g2", at=last_max_at)
-        words3 = gather_second(evals23, "evals_g3", at=woven_at + 2 * KIB)
-        vt_rows2 = turn_pairs(2, words2, 5, at=result_at)
-        merged0_sb = sb([P, I], F32, "merged0_sb", at=last_max_at)
-        nc.scalar.copy(merged0_sb[:], merged0[:])
-        vt_rows3 = turn_pairs(3, words3, 5)
-        merged2 = merge(2, quantize_vt(2, vt_rows2), 2)
+        merged1 = merge(1, quantize_vt(1, turn_pairs(1, words1, 4, at=woven_at - KIB)), 1)
+        words2 = gather_dealt(2, woven_at + 2 * KIB)
+        words3 = gather_dealt(3, woven_at + 3 * KIB)
+        vals_g0 = gather_vals(0, whole, pairs_at)
+        vt_rows2 = turn_pairs(2, words2, 5, at=vals0_at)
+        merged_sb1 = to_sbuf(1, merged1, whole, vals0_at + 6 * KIB - 2 * OVERLAP)
+        vt_rows3 = turn_pairs(3, words3, 6, at=vals0_at + 3 * KIB)
 
-        def offsets(cols):
-            return kept_list[:, cols.start // 16 : cols.stop // 16]
-
-        def add_gathered(result, table, cols, merged, name, at=None):
-            gathered = sb([P, cols.stop - cols.start], F32, name, at=at)
-            nc.scalar.activation(gathered[:], table.indirect(offsets(cols)), ACT.Copy)
-            nc.vector.tensor_tensor(result, gathered[:], merged[:, cols], ALU.add)
-
-        result01 = sb([P, 2, I], F32, "result01", at=result_at)
-        nc.vector.tensor_tensor(result01[:, 0, :], vals01[:].rearrange("p b t -> p (b t)").indirect(kept_list[:]), merged0_sb[:], ALU.add)
-        merged3 = merge(3, quantize_vt(3, vt_rows3, at=last_max_at), 3)
-        add_gathered(result01[:, 1, :], vals01[:, 1, :], slice(0, I), merged1, "vals_g1", at=woven_at + 2 * KIB)
-        nc.sync.dma_start(out_rows[:, 0:2, :], result01[:])
+        result = sb([P, 3, I], F32, "result", at=evals23_at + KIB)
+        nc.vector.tensor_tensor(result[:, 0, :], vals_g0[:], merged0[:], ALU.add)
+        merged2 = merge(2, quantize_vt(2, vt_rows2, at=pairs_at), 2)
+        nc.vector.tensor_tensor(result[:, 1, :], window(1, whole), merged_sb1[:], ALU.add)
+        merged3 = merge(3, quantize_vt(3, vt_rows3, at=vals0_at + 6 * KIB), 3)
+        merged_sb2 = to_sbuf(2, merged2, halves[0], vals0_at + 2 * KIB)
+        vals_g2 = gather_vals(2, halves[1], pairs_at)
+        nc.vector.tensor_tensor(result[:, 2, halves[0]], window(2, halves[0]), merged_sb2[:], ALU.add)
+        nc.sync.dma_start(out_rows[:, 0:3, halves[0]], result[:, :, halves[0]])
+        nc.vector.tensor_tensor(result[:, 2, halves[1]], vals_g2[:], merged2[:, halves[1]], ALU.add)
+        nc.sync.dma_start(out_rows[:, 0:3, halves[1]], result[:, :, halves[1]])
 
         pieces = [slice(lo, hi) for lo, hi in zip(TAIL_CUTS, TAIL_CUTS[1:])]
-        merged2_sb = sb([P, I // 2], F32, "merged2_sb", at=vals01_at + KIB)
-        nc.scalar.copy(merged2_sb[:], merged2[:, halves[0]])
-        result2 = sb([P, I], F32, "result2")
-        nc.vector.tensor_tensor(result2[:, halves[0]], vals2[:].indirect(offsets(halves[0])), merged2_sb[:], ALU.add)
-        add_gathered(result2[:, halves[1]], vals2[:], halves[1], merged2, "vals_g2", at=fac_at)
-        nc.sync.dma_start(out_rows[:, 2, :], result2[:])
-
-        merged3_sb = sb([P, TAIL_CUTS[1]], F32, "merged3_sb", at=vals2_at + KIB)
-        nc.scalar.copy(merged3_sb[:], merged3[:, pieces[0]])
-        last = [sb([P, cols.stop - cols.start], F32, "last%d" % n, at=fac_at + n * KIB) for n, cols in enumerate(pieces)]
-        nc.vector.tensor_tensor(last[0][:], vals3[:].indirect(offsets(pieces[0])), merged3_sb[:], ALU.add)
+        merged_sb3 = to_sbuf(3, merged3, pieces[0], vals2_at)
+        last = [sb([P, cols.stop - cols.start], F32, "last%d" % n, at=pairs_at + n * KIB) for n, cols in enumerate(pieces)]
+        nc.vector.tensor_tensor(last[0][:], window(3, pieces[0]), merged_sb3[:], ALU.add)
         nc.sync.dma_start(out_rows[:, 3, pieces[0]], last[0][:])
         for n in (1, 2):
-            add_gathered(last[n][:], vals3[:], pieces[n], merged3, "vals_g3_%d" % n)
+            gathered = gather_vals(3, pieces[n], vals0_at + 6 * KIB + (n - 1) * 2 * OVERLAP - (2 - n) * 2 * OVERLAP)
+            nc.vector.tensor_tensor(last[n][:], gathered[:], merged3[:, pieces[n]], ALU.add)
             nc.sync.dma_start(out_rows[:, 3, pieces[n]], last[n][:])

@@ -26,15 +26,16 @@ ROW0 = P - SCALE_ROWS
 OVERLAP = 128
 TABLE_BYTES = T * 4
 BANK_BYTES = 2 * KIB
-TAIL_CUTS = [0, 256, 384, 512]
+TIE = 64
 
 
 def tile_attend_softmerge_kernel(tc, ekey_words, ekey_scales, keys_words, keys_scales, fac, evals, vals, offs, offs2, out):
     nc = tc.nc
 
-    evals_rows = evals.rearrange("(b p) n -> p b n", p=P)
-    vals_rows = vals.rearrange("(b p) n -> p b n", p=P)
-    out_rows = out.rearrange("(b p) n -> p b n", p=P)
+    def by_tile(rows):
+        return [rows[: E // 2].rearrange("(p u) n -> p u n", u=2), rows[E // 2 :].rearrange("(u p) n -> p u n", u=2)]
+
+    evals_rows, vals_rows, out_rows = by_tile(evals), by_tile(vals), by_tile(out)
 
     with ExitStack() as ctx:
         keep = ctx.enter_context(tc.tile_pool(name="keep", bufs=1))
@@ -82,7 +83,7 @@ def tile_attend_softmerge_kernel(tc, ekey_words, ekey_scales, keys_words, keys_s
         nc.sync.dma_start(keys_table[:].bitcast(I32), keys_words[0].bitcast(I32))
         nc.scalar.dma_start(ekey_table[:].bitcast(I32), ekey_words[0].rearrange("p n t -> p (n t)").bitcast(I32))
         nc.sync.dma_start(fac_row[P - 1 :, :], fac.rearrange("j o -> o j"))
-        nc.sync.dma_start(evals0[:], evals_rows[:, 0, :])
+        nc.sync.dma_start(evals0[:], evals_rows[0][:, 0, :])
 
         ident = sb([P, P], F32, "ident")
         make_identity(nc, ident[:])
@@ -107,10 +108,10 @@ def tile_attend_softmerge_kernel(tc, ekey_words, ekey_scales, keys_words, keys_s
         ekey_g = sb([P, J], U32, "ekey_g", at=ekey_scale_g_at + 2 * OVERLAP)
         nc.vector.tensor_copy(keys_g[:], keys_table[:].indirect(kept_list[:]))
         nc.vector.tensor_copy(ekey_g[:].rearrange("p (r s) -> p s r", r=PACK), ekey_table[:].indirect(evicted_list[:]))
-        nc.sync.dma_start(evals1[:], evals_rows[:, 1, :])
-        nc.sync.dma_start(evals23[:], evals_rows[:, 2:4, :])
+        nc.sync.dma_start(evals1[:], evals_rows[0][:, 1, :])
+        nc.sync.dma_start(evals23[:], evals_rows[1])
         for b in range(PACK):
-            nc.sync.dma_start(vals_table[b][:], vals_rows[:, b, :])
+            nc.sync.dma_start(vals_table[b][:], vals_rows[b // 2][:, b % 2, :])
 
         def gather_whole(table, name, at):
             gathered = sb([P, J], BF16, name, at=at)
@@ -210,29 +211,35 @@ def tile_attend_softmerge_kernel(tc, ekey_words, ekey_scales, keys_words, keys_s
         merged1 = merge(1, quantize_vt(1, turn_pairs(1, words1, 4, at=woven_at - KIB)), 1)
         words2 = gather_dealt(2, woven_at + 2 * KIB)
         words3 = gather_dealt(3, woven_at + 3 * KIB)
-        vals_g0 = gather_vals(0, whole, pairs_at)
+        early, late = slice(0, I - TIE), slice(I - TIE, I)
+        tie, fused, rest = slice(0, TIE), slice(TIE, I // 2), halves[1]
+        parked = slice(TIE, 2 * TIE)
+        result2 = sb([P, I], F32, "result2", at=pairs_at + 2 * KIB)
+        vals_g0 = gather_vals(0, early, pairs_at)
+        nc.scalar.activation(result2[:, parked], window(0, late), ACT.Copy)
         vt_rows2 = turn_pairs(2, words2, 5, at=vals0_at)
         merged_sb1 = to_sbuf(1, merged1, whole, vals0_at + 6 * KIB - 2 * OVERLAP)
         vt_rows3 = turn_pairs(3, words3, 6, at=vals0_at + 3 * KIB)
 
-        result = sb([P, 3, I], F32, "result", at=evals23_at + KIB)
-        nc.vector.tensor_tensor(result[:, 0, :], vals_g0[:], merged0[:], ALU.add)
+        result01 = sb([P, 2, I], F32, "result01", at=evals23_at + KIB)
+        nc.vector.tensor_tensor(result01[:, 0, early], vals_g0[:], merged0[:, early], ALU.add)
         merged2 = merge(2, quantize_vt(2, vt_rows2, at=pairs_at), 2)
-        nc.vector.tensor_tensor(result[:, 1, :], window(1, whole), merged_sb1[:], ALU.add)
+        nc.vector.tensor_tensor(result01[:, 1, :], window(1, whole), merged_sb1[:], ALU.add)
         merged3 = merge(3, quantize_vt(3, vt_rows3, at=vals0_at + 6 * KIB), 3)
-        merged_sb2 = to_sbuf(2, merged2, halves[0], vals0_at + 2 * KIB)
-        vals_g2 = gather_vals(2, halves[1], pairs_at)
-        nc.vector.tensor_tensor(result[:, 2, halves[0]], window(2, halves[0]), merged_sb2[:], ALU.add)
-        nc.sync.dma_start(out_rows[:, 0:3, halves[0]], result[:, :, halves[0]])
-        nc.vector.tensor_tensor(result[:, 2, halves[1]], vals_g2[:], merged2[:, halves[1]], ALU.add)
-        nc.sync.dma_start(out_rows[:, 0:3, halves[1]], result[:, :, halves[1]])
+        nc.scalar.copy(result01[:, 0, late], merged2[:, tie])
+        merged_sb2 = to_sbuf(2, merged2, fused, vals0_at + 2 * KIB)
+        vals_g2 = gather_vals(2, rest, pairs_at)
+        nc.vector.tensor_tensor(result2[:, tie], window(2, tie), result01[:, 0, late], ALU.add)
+        nc.vector.tensor_tensor(result01[:, 0, late], result2[:, parked], merged0[:, late], ALU.add)
+        nc.sync.dma_start(out_rows[0], result01[:])
+        nc.vector.tensor_tensor(result2[:, fused], window(2, fused), merged_sb2[:], ALU.add)
+        nc.vector.tensor_tensor(result2[:, rest], vals_g2[:], merged2[:, rest], ALU.add)
+        nc.sync.dma_start(out_rows[1][:, 0, :], result2[:])
 
-        pieces = [slice(lo, hi) for lo, hi in zip(TAIL_CUTS, TAIL_CUTS[1:])]
-        merged_sb3 = to_sbuf(3, merged3, pieces[0], vals2_at)
-        last = [sb([P, cols.stop - cols.start], F32, "last%d" % n, at=pairs_at + n * KIB) for n, cols in enumerate(pieces)]
-        nc.vector.tensor_tensor(last[0][:], window(3, pieces[0]), merged_sb3[:], ALU.add)
-        nc.sync.dma_start(out_rows[:, 3, pieces[0]], last[0][:])
-        for n in (1, 2):
-            gathered = gather_vals(3, pieces[n], vals0_at + 6 * KIB + (n - 1) * 2 * OVERLAP - (2 - n) * 2 * OVERLAP)
-            nc.vector.tensor_tensor(last[n][:], gathered[:], merged3[:, pieces[n]], ALU.add)
-            nc.sync.dma_start(out_rows[:, 3, pieces[n]], last[n][:])
+        merged_sb3 = to_sbuf(3, merged3, halves[0], pairs_at)
+        vals_g3 = gather_vals(3, halves[1], vals0_at + 6 * KIB)
+        last = [sb([P, I // 2], F32, "last%d" % h) for h in range(2)]
+        nc.vector.tensor_tensor(last[0][:], window(3, halves[0]), merged_sb3[:], ALU.add)
+        nc.sync.dma_start(out_rows[1][:, 1, halves[0]], last[0][:])
+        nc.vector.tensor_tensor(last[1][:], vals_g3[:], merged3[:, halves[1]], ALU.add)
+        nc.sync.dma_start(out_rows[1][:, 1, halves[1]], last[1][:])

@@ -26,7 +26,7 @@ ROW0 = P - SCALE_ROWS
 OVERLAP = 128
 TABLE_BYTES = T * 4
 BANK_BYTES = 2 * KIB
-TIE = 64
+FIRST, FUSED = 192, 320
 
 
 def tile_attend_softmerge_kernel(tc, ekey_words, ekey_scales, keys_words, keys_scales, fac, evals, vals, offs, offs2, out):
@@ -36,6 +36,7 @@ def tile_attend_softmerge_kernel(tc, ekey_words, ekey_scales, keys_words, keys_s
         return [rows[: E // 2].rearrange("(p u) n -> p u n", u=2), rows[E // 2 :].rearrange("(u p) n -> p u n", u=2)]
 
     evals_rows, vals_rows, out_rows = by_tile(evals), by_tile(vals), by_tile(out)
+    place = (1, 0, 0, 1)
 
     with ExitStack() as ctx:
         keep = ctx.enter_context(tc.tile_pool(name="keep", bufs=1))
@@ -83,7 +84,7 @@ def tile_attend_softmerge_kernel(tc, ekey_words, ekey_scales, keys_words, keys_s
         nc.sync.dma_start(keys_table[:].bitcast(I32), keys_words[0].bitcast(I32))
         nc.scalar.dma_start(ekey_table[:].bitcast(I32), ekey_words[0].rearrange("p n t -> p (n t)").bitcast(I32))
         nc.sync.dma_start(fac_row[P - 1 :, :], fac.rearrange("j o -> o j"))
-        nc.sync.dma_start(evals0[:], evals_rows[0][:, 0, :])
+        nc.sync.dma_start(evals0[:], evals_rows[0][:, place[0], :])
 
         ident = sb([P, P], F32, "ident")
         make_identity(nc, ident[:])
@@ -108,10 +109,10 @@ def tile_attend_softmerge_kernel(tc, ekey_words, ekey_scales, keys_words, keys_s
         ekey_g = sb([P, J], U32, "ekey_g", at=ekey_scale_g_at + 2 * OVERLAP)
         nc.vector.tensor_copy(keys_g[:], keys_table[:].indirect(kept_list[:]))
         nc.vector.tensor_copy(ekey_g[:].rearrange("p (r s) -> p s r", r=PACK), ekey_table[:].indirect(evicted_list[:]))
-        nc.sync.dma_start(evals1[:], evals_rows[0][:, 1, :])
+        nc.sync.dma_start(evals1[:], evals_rows[0][:, place[1], :])
         nc.sync.dma_start(evals23[:], evals_rows[1])
         for b in range(PACK):
-            nc.sync.dma_start(vals_table[b][:], vals_rows[b // 2][:, b % 2, :])
+            nc.sync.dma_start(vals_table[b][:], vals_rows[b // 2][:, place[b], :])
 
         def gather_whole(table, name, at):
             gathered = sb([P, J], BF16, name, at=at)
@@ -211,35 +212,35 @@ def tile_attend_softmerge_kernel(tc, ekey_words, ekey_scales, keys_words, keys_s
         merged1 = merge(1, quantize_vt(1, turn_pairs(1, words1, 4, at=woven_at - KIB)), 1)
         words2 = gather_dealt(2, woven_at + 2 * KIB)
         words3 = gather_dealt(3, woven_at + 3 * KIB)
-        early, late = slice(0, I - TIE), slice(I - TIE, I)
-        tie, fused, rest = slice(0, TIE), slice(TIE, I // 2), halves[1]
-        parked = slice(TIE, 2 * TIE)
-        result2 = sb([P, I], F32, "result2", at=pairs_at + 2 * KIB)
-        vals_g0 = gather_vals(0, early, pairs_at)
-        nc.scalar.activation(result2[:, parked], window(0, late), ACT.Copy)
-        vt_rows2 = turn_pairs(2, words2, 5, at=vals0_at)
-        merged_sb1 = to_sbuf(1, merged1, whole, vals0_at + 6 * KIB - 2 * OVERLAP)
-        vt_rows3 = turn_pairs(3, words3, 6, at=vals0_at + 3 * KIB)
-
-        result01 = sb([P, 2, I], F32, "result01", at=evals23_at + KIB)
-        nc.vector.tensor_tensor(result01[:, 0, early], vals_g0[:], merged0[:, early], ALU.add)
+        fused, rest = slice(0, FUSED), slice(FUSED, I)
+        short, long = slice(0, I - FUSED), slice(I - FUSED, I)
+        merged_sb0 = to_sbuf(0, merged0, short, pairs_at)
+        result10 = sb([P, 2 * I + short.stop], F32, "result10")
+        result1, result0, parked = result10[:, :I], result10[:, I : 2 * I], result10[:, I + short.stop :]
+        nc.scalar.copy(parked, merged1[:])
+        vt_rows2 = turn_pairs(2, words2, 5)
+        vt_rows3 = turn_pairs(3, words3, 6)
+        vals_g0 = gather_vals(0, long, woven_at + 3 * KIB - 2 * OVERLAP)
+        nc.vector.tensor_tensor(result0[:, short], window(0, short), merged_sb0[:], ALU.add)
         merged2 = merge(2, quantize_vt(2, vt_rows2, at=pairs_at), 2)
-        nc.vector.tensor_tensor(result01[:, 1, :], window(1, whole), merged_sb1[:], ALU.add)
-        merged3 = merge(3, quantize_vt(3, vt_rows3, at=vals0_at + 6 * KIB), 3)
-        nc.scalar.copy(result01[:, 0, late], merged2[:, tie])
-        merged_sb2 = to_sbuf(2, merged2, fused, vals0_at + 2 * KIB)
+        nc.vector.tensor_tensor(result1, window(1, whole), parked, ALU.add)
+        merged3 = merge(3, quantize_vt(3, vt_rows3, at=vals1_at + KIB), 3)
+        nc.vector.tensor_tensor(result0[:, long], vals_g0[:], merged0[:, long], ALU.add)
+        nc.sync.dma_start(out_rows[0], result10[:, : 2 * I].rearrange("p (u i) -> p u i", u=2))
+
+        merged_sb2 = to_sbuf(2, merged2, fused, vals0_at)
         vals_g2 = gather_vals(2, rest, pairs_at)
-        nc.vector.tensor_tensor(result2[:, tie], window(2, tie), result01[:, 0, late], ALU.add)
-        nc.vector.tensor_tensor(result01[:, 0, late], result2[:, parked], merged0[:, late], ALU.add)
-        nc.sync.dma_start(out_rows[0], result01[:])
+        result2 = sb([P, I], F32, "result2")
         nc.vector.tensor_tensor(result2[:, fused], window(2, fused), merged_sb2[:], ALU.add)
         nc.vector.tensor_tensor(result2[:, rest], vals_g2[:], merged2[:, rest], ALU.add)
         nc.sync.dma_start(out_rows[1][:, 0, :], result2[:])
 
-        merged_sb3 = to_sbuf(3, merged3, halves[0], pairs_at)
-        vals_g3 = gather_vals(3, halves[1], vals0_at + 6 * KIB)
-        last = [sb([P, I // 2], F32, "last%d" % h) for h in range(2)]
-        nc.vector.tensor_tensor(last[0][:], window(3, halves[0]), merged_sb3[:], ALU.add)
-        nc.sync.dma_start(out_rows[1][:, 1, halves[0]], last[0][:])
-        nc.vector.tensor_tensor(last[1][:], vals_g3[:], merged3[:, halves[1]], ALU.add)
-        nc.sync.dma_start(out_rows[1][:, 1, halves[1]], last[1][:])
+        merged_sb3 = to_sbuf(3, merged3, fused, vals2_at)
+        vals_g3 = gather_vals(3, rest, vals1_at + KIB)
+        for n, cols in enumerate((slice(0, FIRST), slice(FIRST, FUSED))):
+            piece = sb([P, cols.stop - cols.start], F32, "piece%d" % n, at=pairs_at + (n - 1) * (4 * FIRST - OVERLAP) + n * OVERLAP)
+            nc.vector.tensor_tensor(piece[:], window(3, cols), merged_sb3[:, cols], ALU.add)
+            nc.sync.dma_start(out_rows[1][:, 1, cols], piece[:])
+        last = sb([P, I - FUSED], F32, "last")
+        nc.vector.tensor_tensor(last[:], vals_g3[:], merged3[:, rest], ALU.add)
+        nc.sync.dma_start(out_rows[1][:, 1, rest], last[:])

@@ -53,22 +53,24 @@ def tile_attend_softmerge_kernel(tc, ekey_words, ekey_scales, keys_words, keys_s
 
         evals1_at = 0
         keys_scale_g_at = evals1_at + TABLE_BYTES - OVERLAP
-        evals23_at = keys_scale_g_at + I - OVERLAP
-        vals0_at = 26 * KIB
-        keys_at = vals0_at + TABLE_BYTES - OVERLAP
-        vals1_at = keys_at + 2 * T - OVERLAP
-        vals2_at = 48 * KIB
-        ekey_at = vals2_at + TABLE_BYTES - OVERLAP
-        vals3_at = ekey_at + TABLE_BYTES - OVERLAP
+        evals23_at = 10 * KIB
+        keys_at = evals23_at + 2 * TABLE_BYTES - OVERLAP
+        vals0_at = 32 * KIB
+        ekey_at = vals0_at + TABLE_BYTES - OVERLAP
+        vals1_at = ekey_at + TABLE_BYTES - OVERLAP
+        vals2_at = 100 * KIB
+        evals0_at = vals2_at + TABLE_BYTES - OVERLAP
+        vals3_at = evals0_at + TABLE_BYTES - OVERLAP
+        keys_scale_at = 60 * KIB
         ekey_scale_g_at, sums_at, woven_at, pairs_at, fac_at = (k * KIB for k in (76, 80, 84, 88, 92))
 
         kept_list = sb([P, I // 16], U16, "kept_list")
         evicted_list = sb([P, J // 16], U16, "evicted_list")
         keys_table = sb([P, T], U16, "keys_table", at=keys_at)
         ekey_table = sb([P, T], U32, "ekey_table", at=ekey_at)
-        keys_scale_table = sb([P, T], U8, "keys_scale_table")
+        keys_scale_table = sb([P, T], U8, "keys_scale_table", at=keys_scale_at)
         ekey_scale_table = sb([P, T], U8, "ekey_scale_table")
-        evals0 = sb([P, T], F32, "evals0")
+        evals0 = sb([P, T], F32, "evals0", at=evals0_at)
         evals1 = sb([P, T], F32, "evals1", at=evals1_at)
         evals23 = sb([P, 2, T], F32, "evals23", at=evals23_at)
         vals_table = [sb([P, T], F32, "vals%d" % b, at=at) for b, at in enumerate((vals0_at, vals1_at, vals2_at, vals3_at))]
@@ -91,14 +93,14 @@ def tile_attend_softmerge_kernel(tc, ekey_words, ekey_scales, keys_words, keys_s
         fac_turned = bank([P, PACK, P], "fac_turned", 4)
         for r in range(PACK):
             nc.tensor.transpose(fac_turned[:, r, :], fac_row[:, r:J:PACK], ident[:])
-        fac_sb = sb([P, PACK], F32, "fac_sb")
-        nc.scalar.copy(fac_sb[:], fac_turned[:, :, P - 1])
 
         ekey_scale_g = sb([P, J], U8, "ekey_scale_g", at=ekey_scale_g_at)
         keys_scale_g = sb([P, I], U8, "keys_scale_g", at=keys_scale_g_at)
         planes = sb([P, J + I], U8, "planes")
         nc.vector.tensor_copy(ekey_scale_g[:], ekey_scale_table[:].indirect(evicted_list[:]))
         nc.vector.tensor_copy(keys_scale_g[:], keys_scale_table[:].indirect(kept_list[:]))
+        fac_sb = sb([P, PACK], F32, "fac_sb", at=keys_scale_at)
+        nc.scalar.copy(fac_sb[:], fac_turned[:, :, P - 1])
         nc.vector.tensor_copy(
             planes[:, :J].rearrange("p (r s) -> p r s", r=PACK), ekey_scale_g[:].rearrange("p (s r) -> p r s", r=PACK)
         )
@@ -111,8 +113,8 @@ def tile_attend_softmerge_kernel(tc, ekey_words, ekey_scales, keys_words, keys_s
         nc.vector.tensor_copy(ekey_g[:].rearrange("p (r s) -> p s r", r=PACK), ekey_table[:].indirect(evicted_list[:]))
         nc.sync.dma_start(evals1[:], evals_rows[0][:, place[1], :])
         nc.sync.dma_start(evals23[:], evals_rows[1])
-        for b in range(PACK):
-            nc.sync.dma_start(vals_table[b][:], vals_rows[b // 2][:, place[b], :])
+        for b in (0, 1):
+            nc.sync.dma_start(vals_table[b][:], vals_rows[0][:, place[b], :])
 
         def gather_whole(table, name, at):
             gathered = sb([P, J], BF16, name, at=at)
@@ -127,6 +129,8 @@ def tile_attend_softmerge_kernel(tc, ekey_words, ekey_scales, keys_words, keys_s
             return [words[:, u * P : (u + 1) * P] for u in range(2)]
 
         words0 = gather_whole(evals0[:], "evals_g0", fac_at)
+        for b in (2, 3):
+            nc.sync.dma_start(vals_table[b][:], vals_rows[1][:, place[b], :])
 
         scores = [bank([P, I], "score%d" % r, r) for r in range(PACK)]
         for r in range(PACK):

@@ -23,7 +23,7 @@ PACK = 4
 KIB = 1024
 SCALE_ROWS = 16
 ROW0 = P - SCALE_ROWS
-OVERLAP = 128
+OVERLAP = 256
 TABLE_BYTES = T * 4
 BANK_BYTES = 2 * KIB
 FIRST, FUSED = 192, 320
@@ -48,8 +48,8 @@ def tile_attend_softmerge_kernel(tc, ekey_words, ekey_scales, keys_words, keys_s
 
         def sb(shape, dtype, name, at=None):
             if at is not None:
-                return placed.tile(shape, dtype, name=name, align_bytes=64, offset=at)
-            return keep.tile(shape, dtype, name=name, align_bytes=64)
+                return placed.tile(shape, dtype, name=name, align_bytes=OVERLAP, offset=at)
+            return keep.tile(shape, dtype, name=name, align_bytes=OVERLAP)
 
         evals1_at = 0
         keys_scale_g_at = evals1_at + TABLE_BYTES - OVERLAP
@@ -108,7 +108,7 @@ def tile_attend_softmerge_kernel(tc, ekey_words, ekey_scales, keys_words, keys_s
         for r in range(4):
             nc.sync.dma_start(planes[r:P:32, :].bitcast(I32), planes[ROW0 + r : P : 4, :].bitcast(I32))
         keys_g = sb([P, I], U16, "keys_g", at=ekey_scale_g_at + OVERLAP - 2 * I)
-        ekey_g = sb([P, J], U32, "ekey_g", at=ekey_scale_g_at + 2 * OVERLAP)
+        ekey_g = sb([P, J], U32, "ekey_g", at=ekey_scale_g_at + OVERLAP)
         nc.vector.tensor_copy(keys_g[:], keys_table[:].indirect(kept_list[:]))
         nc.vector.tensor_copy(ekey_g[:].rearrange("p (r s) -> p s r", r=PACK), ekey_table[:].indirect(evicted_list[:]))
         nc.sync.dma_start(evals1[:], evals_rows[0][:, place[1], :])

from contextlib import ExitStack

import concourse.mybir as mybir
from concourse.masks import make_identity

D, T, J, I, E = 512, 2048, 512, 512, 512
FLOPS = 2 * D * J * I + 2 * J * E * I

F32 = mybir.dt.float32
BF16 = mybir.dt.bfloat16
I32 = mybir.dt.int32
U32 = mybir.dt.uint32
U16 = mybir.dt.uint16
U8 = mybir.dt.uint8
FP8X4 = mybir.dt.float8_e4m3fn_x4
FP4X4 = mybir.dt.float4_e2m1fn_x4
ALU = mybir.AluOpType
ACT = mybir.ActivationFunctionType
AXIS = mybir.AxisListType

P = 128
PACK = 4
KIB = 1024
SCALE_ROWS = 16
ROW0 = P - SCALE_ROWS
OVERLAP = 256
TABLE_BYTES = T * 4
BANK_BYTES = 2 * KIB
FIRST, FUSED = 192, 320


def tile_attend_softmerge_kernel(tc, ekey_words, ekey_scales, keys_words, keys_scales, fac, evals, vals, offs, offs2, out):
    nc = tc.nc

    def by_tile(rows):
        return [rows[: E // 2].rearrange("(p u) n -> p u n", u=2), rows[E // 2 :].rearrange("(u p) n -> p u n", u=2)]

    evals_rows, vals_rows, out_rows = by_tile(evals), by_tile(vals), by_tile(out)
    place = (1, 0, 0, 1)

    with ExitStack() as ctx:
        keep = ctx.enter_context(tc.tile_pool(name="keep", bufs=1))
        placed = ctx.enter_context(tc.tile_pool(name="placed", bufs=1))
        psum = ctx.enter_context(tc.psum_pool(name="psum", bufs=1))

        def bank(shape, name, number):
            return psum.tile(shape, F32, name=name, offset=number * BANK_BYTES)

        def sb(shape, dtype, name, at=None):
            if at is not None:
                return placed.tile(shape, dtype, name=name, align_bytes=OVERLAP, offset=at)
            return keep.tile(shape, dtype, name=name, align_bytes=OVERLAP)

        evals1_at = 0
        keys_scale_g_at = evals1_at + TABLE_BYTES - OVERLAP
        evals23_at = 10 * KIB
        keys_at = evals23_at + 2 * TABLE_BYTES - OVERLAP
        vals0_at = 32 * KIB
        ekey_at = vals0_at + TABLE_BYTES - OVERLAP
        vals1_at = ekey_at + TABLE_BYTES - OVERLAP
        vals2_at = 100 * KIB
        evals0_at = vals2_at + TABLE_BYTES - OVERLAP
        vals3_at = evals0_at + TABLE_BYTES - OVERLAP
        keys_scale_at = 60 * KIB
        ekey_scale_g_at, sums_at, woven_at, pairs_at, fac_at = (k * KIB for k in (76, 80, 84, 88, 92))

        kept_list = sb([P, I // 16], U16, "kept_list")
        evicted_list = sb([P, J // 16], U16, "evicted_list")
        keys_table = sb([P, T], U16, "keys_table", at=keys_at)
        ekey_table = sb([P, T], U32, "ekey_table", at=ekey_at)
        keys_scale_table = sb([P, T], U8, "keys_scale_table", at=keys_scale_at)
        ekey_scale_table = sb([P, T], U8, "ekey_scale_table")
        evals0 = sb([P, T], F32, "evals0", at=evals0_at)
        evals1 = sb([P, T], F32, "evals1", at=evals1_at)
        evals23 = sb([P, 2, T], F32, "evals23", at=evals23_at)
        vals_table = [sb([P, T], F32, "vals%d" % b, at=at) for b, at in enumerate((vals0_at, vals1_at, vals2_at, vals3_at))]
        fac_row = sb([P, J], F32, "fac_row", at=fac_at)

        nc.gpsimd.memset(ekey_scale_table[:ROW0, :].bitcast(I32), 0)
        nc.vector.memset(keys_scale_table[:ROW0, :].bitcast(I32), 0)
        nc.vector.memset(fac_row[: P - 1, :], 0.0)
        nc.sync.dma_start(kept_list[:], offs)
        nc.scalar.dma_start(ekey_scale_table[ROW0:, :].bitcast(I32), ekey_scales[0].bitcast(I32))
        nc.sync.dma_start(evicted_list[:], offs2)
        nc.scalar.dma_start(keys_scale_table[ROW0:, :].bitcast(I32), keys_scales[0].bitcast(I32))
        nc.sync.dma_start(keys_table[:].bitcast(I32), keys_words[0].bitcast(I32))
        nc.scalar.dma_start(ekey_table[:].bitcast(I32), ekey_words[0].rearrange("p n t -> p (n t)").bitcast(I32))
        nc.sync.dma_start(fac_row[P - 1 :, :], fac.rearrange("j o -> o j"))
        nc.sync.dma_start(evals0[:], evals_rows[0][:, place[0], :])

        ident = sb([P, P], F32, "ident")
        make_identity(nc, ident[:])
        fac_turned = bank([P, PACK, P], "fac_turned", 4)
        for r in range(PACK):
            nc.tensor.transpose(fac_turned[:, r, :], fac_row[:, r:J:PACK], ident[:])

        ekey_scale_g = sb([P, J], U8, "ekey_scale_g", at=ekey_scale_g_at)
        keys_scale_g = sb([P, I], U8, "keys_scale_g", at=keys_scale_g_at)
        planes = sb([P, J + I], U8, "planes")
        nc.vector.tensor_copy(ekey_scale_g[:], ekey_scale_table[:].indirect(evicted_list[:]))
        nc.vector.tensor_copy(keys_scale_g[:], keys_scale_table[:].indirect(kept_list[:]))
        fac_sb = sb([P, PACK], F32, "fac_sb", at=keys_scale_at)
        nc.scalar.copy(fac_sb[:], fac_turned[:, :, P - 1])
        nc.vector.tensor_copy(
            planes[:, :J].rearrange("p (r s) -> p r s", r=PACK), ekey_scale_g[:].rearrange("p (s r) -> p r s", r=PACK)
        )
        nc.vector.tensor_copy(planes[:, J:].bitcast(I32), keys_scale_g[:].bitcast(I32))
        for r in range(4):
            nc.sync.dma_start(planes[r:P:32, :].bitcast(I32), planes[ROW0 + r : P : 4, :].bitcast(I32))
        keys_g = sb([P, I], U16, "keys_g", at=ekey_scale_g_at + OVERLAP - 2 * I)
        ekey_g = sb([P, J], U32, "ekey_g", at=ekey_scale_g_at + OVERLAP)
        nc.vector.tensor_copy(keys_g[:], keys_table[:].indirect(kept_list[:]))
        nc.vector.tensor_copy(ekey_g[:].rearrange("p (r s) -> p s r", r=PACK), ekey_table[:].indirect(evicted_list[:]))
        nc.sync.dma_start(evals1[:], evals_rows[0][:, place[1], :])
        nc.sync.dma_start(evals23[:], evals_rows[1])
        for b in (0, 1):
            nc.sync.dma_start(vals_table[b][:], vals_rows[0][:, place[b], :])

        def gather_whole(table, name, at):
            gathered = sb([P, J], BF16, name, at=at)
            nc.scalar.activation(gathered[:], table.indirect(evicted_list[:]), ACT.Copy)
            words = gathered[:].bitcast(F32)
            return [words[:, u : J // 2 : 2] for u in range(2)]

        def gather_dealt(b, at):
            gathered = sb([P, J], BF16, "evals_g%d" % b, at=at)
            nc.vector.tensor_copy(gathered[:].rearrange("p (u s c) -> p s u c", u=2, c=2), evals23[:, b - 2, :].indirect(evicted_list[:]))
            words = gathered[:].bitcast(F32)
            return [words[:, u * P : (u + 1) * P] for u in range(2)]

        words0 = gather_whole(evals0[:], "evals_g0", fac_at)
        for b in (2, 3):
            nc.sync.dma_start(vals_table[b][:], vals_rows[1][:, place[b], :])

        scores = [bank([P, I], "score%d" % r, r) for r in range(PACK)]
        for r in range(PACK):
            cols = slice(r * P, (r + 1) * P)
            nc.tensor.matmul_mx(
                out=scores[r][:], lhsT=ekey_g[:, cols].bitcast(FP8X4), lhsT_scale=planes[:, cols],
                rhs=keys_g[:].bitcast(FP4X4), rhs_scale=planes[:, J:], start=True, stop=True,
            )

        neg_max = [sb([P, 1], F32, "neg_max%d" % r, at=sums_at if r == PACK - 1 else None) for r in range(PACK)]
        row_sum = [sb([P, 2], F32, "row_sum%d" % u) for u in range(2)]
        inv_sum = [sb([P, 2], F32, "inv_sum%d" % u) for u in range(2)]
        p_rows = [sb([P, I], F32, "p_rows%d" % r) for r in range(PACK)]
        w_pairs = sb([P, 2, I, 2], BF16, "w_pairs", at=pairs_at)
        w_woven = [sb([P, I // 2, PACK], BF16, "w_woven%d" % h, at=woven_at + h * 2 * KIB) for h in range(2)]
        w_codes = sb([P, I], U32, "w_codes")
        w_scales = sb([P, I], U8, "w_scales")
        halves = [slice(0, I // 2), slice(I // 2, I)]
        whole = slice(0, I)

        for r in range(PACK):
            nc.vector.tensor_reduce(neg_max[r][:], scores[r][:], AXIS.X, ALU.max, negate=True)
            nc.scalar.activation(
                p_rows[r][:], scores[r][:], ACT.Exp, bias=neg_max[r][:], accum_out=row_sum[r // 2][:, r % 2 : r % 2 + 1]
            )
        words1 = gather_whole(evals1[:], "evals_g1", sums_at)

        def product(r, cols):
            u, c = divmod(r, 2)
            nc.vector.tensor_scalar(
                w_pairs[:, u, cols, c], p_rows[r][:, cols], inv_sum[u][:, c : c + 1], fac_sb[:, r : r + 1], ALU.mult, ALU.mult
            )

        nc.vector.reciprocal(inv_sum[0][:], row_sum[0][:])
        product(0, whole)
        product(1, whole)
        nc.vector.reciprocal(inv_sum[1][:], row_sum[1][:])
        product(2, whole)
        product(3, whole)
        for h in range(2):
            nc.vector.tensor_copy(w_woven[h][:].bitcast(F32), w_pairs[:, :, halves[h], :].bitcast(F32).rearrange("p u i o -> p i (u o)"))
        for h in range(2):
            nc.vector.quantize_mx(
                out=w_codes[:, halves[h]].bitcast(FP8X4), scales=w_scales[:, halves[h]], in_=w_woven[h][:].rearrange("p i t -> p (i t)")
            )

        def turn_pairs(b, words, number, at=None):
            turned = bank([P, 2, P], "turned%d" % b, number)
            for u in range(2):
                nc.tensor.transpose(turned[:, u, :], words[u], ident[:])
            rows = sb([P, P * PACK], BF16, "vt_rows%d" % b, at=at)
            nc.scalar.copy(rows[:].bitcast(F32).rearrange("p (e u) -> p e u", u=2), turned[:].rearrange("p u e -> p e u"))
            return rows

        def quantize_vt(b, rows, at=None):
            codes = sb([P, P], U32, "vt_codes%d" % b, at=at)
            scales = sb([P, P], U8, "vt_scales%d" % b)
            nc.vector.quantize_mx(out=codes[:].bitcast(FP8X4), scales=scales[:], in_=rows[:])
            return codes, scales

        def merge(b, vt, number):
            merged = bank([P, I], "merged%d" % b, number)
            nc.tensor.matmul_mx(
                out=merged[:], lhsT=vt[0][:].bitcast(FP8X4), lhsT_scale=vt[1][:],
                rhs=w_codes[:].bitcast(FP8X4), rhs_scale=w_scales[:], start=True, stop=True,
            )
            return merged

        def window(b, cols):
            return vals_table[b][:].indirect(kept_list[:, cols.start // 16 : cols.stop // 16])

        def gather_vals(b, cols, at):
            gathered = sb([P, cols.stop - cols.start], F32, "vals_g%d_%d" % (b, cols.start), at=at)
            nc.scalar.activation(gathered[:], window(b, cols), ACT.Copy)
            return gathered

        def to_sbuf(b, merged, cols, at):
            merged_sb = sb([P, cols.stop - cols.start], F32, "merged_sb%d" % b, at=at)
            nc.scalar.copy(merged_sb[:], merged[:, cols])
            return merged_sb

        merged0 = merge(0, quantize_vt(0, turn_pairs(0, words0, 3)), 0)
        merged1 = merge(1, quantize_vt(1, turn_pairs(1, words1, 4, at=woven_at - KIB)), 1)
        words2 = gather_dealt(2, woven_at + 2 * KIB)
        words3 = gather_dealt(3, woven_at + 3 * KIB)
        fused, rest = slice(0, FUSED), slice(FUSED, I)
        short, long = slice(0, I - FUSED), slice(I - FUSED, I)
        merged_sb0 = to_sbuf(0, merged0, short, pairs_at)
        result10 = sb([P, 2 * I + short.stop], F32, "result10")
        result1, result0, parked = result10[:, :I], result10[:, I : 2 * I], result10[:, I + short.stop :]
        nc.scalar.copy(parked, merged1[:])
        vt_rows2 = turn_pairs(2, words2, 5)
        vt_rows3 = turn_pairs(3, words3, 6)
        vals_g0 = gather_vals(0, long, woven_at + 3 * KIB - 2 * OVERLAP)
        nc.vector.tensor_tensor(result0[:, short], window(0, short), merged_sb0[:], ALU.add)
        merged2 = merge(2, quantize_vt(2, vt_rows2, at=pairs_at), 2)
        nc.vector.tensor_tensor(result1, window(1, whole), parked, ALU.add)
        merged3 = merge(3, quantize_vt(3, vt_rows3, at=vals1_at + KIB), 3)
        nc.vector.tensor_tensor(result0[:, long], vals_g0[:], merged0[:, long], ALU.add)
        nc.sync.dma_start(out_rows[0], result10[:, : 2 * I].rearrange("p (u i) -> p u i", u=2))

        merged_sb2 = to_sbuf(2, merged2, fused, vals0_at)
        vals_g2 = gather_vals(2, rest, pairs_at)
        result2 = sb([P, I], F32, "result2")
        nc.vector.tensor_tensor(result2[:, fused], window(2, fused), merged_sb2[:], ALU.add)
        nc.vector.tensor_tensor(result2[:, rest], vals_g2[:], merged2[:, rest], ALU.add)
        nc.sync.dma_start(out_rows[1][:, 0, :], result2[:])

        merged_sb3 = to_sbuf(3, merged3, fused, vals2_at)
        vals_g3 = gather_vals(3, rest, vals1_at + KIB)
        for n, cols in enumerate((slice(0, FIRST), slice(FIRST, FUSED))):
            piece = sb([P, cols.stop - cols.start], F32, "piece%d" % n, at=pairs_at + (n - 1) * (4 * FIRST - OVERLAP) + n * OVERLAP)
            nc.vector.tensor_tensor(piece[:], window(3, cols), merged_sb3[:, cols], ALU.add)
            nc.sync.dma_start(out_rows[1][:, 1, cols], piece[:])
        last = sb([P, I - FUSED], F32, "last")
        nc.vector.tensor_tensor(last[:], vals_g3[:], merged3[:, rest], ALU.add)
        nc.sync.dma_start(out_rows[1][:, 1, rest], last[:])
